import numpy as np, ml_dtypes
CORES = [8,136,40,168]
N = 4
BF = ml_dtypes.bfloat16
V, SQ, M, S, J = 2304, 4, 64, 4, 256
PAR = [0, 0, 0, 0, 0, 0, 0, 0, 0, 0, 0, 0, 0, 0, 0, 0, 0, 1, 1, 1, 1, 1, 1, 1, 1, 2, 2, 2, 2, 3, 3, 3, 3, 4, 4, 4, 4, 6, 6, 6, 9, 9, 13, 13, 16, 16, 17, 17, 17, 17, 18, 18, 19, 19, 20, 25, 25, 29, 29, 33, 33, 37, 40, 44]
ROW = [0, 0, 1, 2, 3, 4, 5, 6, 7, 8, 9, 10, 11, 12, 13, 14, 15, 0, 1, 2, 3, 4, 5, 6, 7, 0, 1, 8, 9, 0, 2, 10, 11, 0, 3, 12, 13, 0, 14, 15, 0, 5, 0, 6, 0, 15, 0, 1, 2, 3, 0, 4, 0, 5, 0, 0, 1, 0, 7, 0, 14, 0, 0, 0]
C = 64
def parts(rng):
    gi = np.arange(8)[:, None, None]
    od = np.argsort(rng.random((8, V)), axis=1); blk = ((np.argsort(od, axis=1) // C) * C)[:, None, :]
    base = od[gi, blk + rng.integers(0, C, (8, 16, V))]
    turn = (rng.integers(0, 8, (N, 8, 1, V)) * 2 + 1) * np.arange(16)[:, None] + rng.integers(0, 16, (N, 8, 1, V))
    q = np.take_along_axis(base[None], turn & 15, 2)
    own = rng.random(q.shape, dtype=np.float32)
    q = np.where(own < 0.2, od[gi, blk + rng.integers(0, C, q.shape)], q); q = np.where(own > 0.9, rng.integers(0, V, q.shape), q)
    size = np.exp2(rng.integers(-1, 2, (8, 16, 1))).astype(np.float32)
    k = (0.8 * rng.standard_normal((8, 16, V), dtype=np.float32) + 0.6 * rng.standard_normal((N, 8, 16, V), dtype=np.float32)) * size
    x = rng.standard_normal((N, 8, 16, SQ), dtype=np.float32) * size
    kp = (1.5 * rng.random((N, 8, 16, 1)) - 0.25) * size
    cm = np.take_along_axis(rng.integers(0, V // C, (N, 8, 4)), rng.integers(0, 4, (N, 8, SQ)), 2)
    tk = od[np.arange(8)[:, None], C * cm + rng.integers(0, C, (N, 8, SQ))]
    return q, k, x, kp, tk
def tidy(v):
    return np.where(np.abs(v) < 2.0 ** -60, 0, v)
def pack(q, k, x, kp, tk):
    return {"qt": np.ascontiguousarray(q.reshape(N, 128, V)).astype(np.int32), "kt": np.ascontiguousarray(tidy(k).reshape(N, 128, V)).astype(np.float32).astype(BF),
            "x0": np.ascontiguousarray(tidy(x).reshape(N, 128, SQ)).astype(np.float32), "kap": np.ascontiguousarray(tidy(kp).reshape(N, 128, 1)).astype(np.float32),
            "tok": np.ascontiguousarray(tk).astype(np.int32)}
def branch(rng, q, tk, g, e):
    w = rng.permutation(V)[:SQ * (e + 3)].reshape(e + 3, SQ); dep = [0]
    for n in range(1, M): dep.append(dep[PAR[n]] + 1)
    rows = sorted({ROW[n] for n in range(1, M) if dep[n] == e + 1}, reverse=True)
    tk[:, g] = w[0]
    for s in range(SQ):
        for i in range(e + 1): q[:, g, :, int(w[i, s])] = w[i + 1, s]
        for n in range(0, N, 2):
            q[n, g, :, int(w[e, s])] = w[e + 2, s]; q[n, g, rows[(s + SQ * (n // 2)) % len(rows)], int(w[e, s])] = w[e + 1, s]
def setup_inputs(rng):
    return pack(*parts(rng))
def setup_inputs_spread(rng):
    q, k, x, kp, tk = parts(rng)
    k = k * np.exp2(rng.integers(-3, 4, (8, 1, V))) * (rng.random((8, 1, V)) > 0.0625)
    x = x * np.exp2(rng.integers(-3, 4, (N, 8, 1, SQ))); kp = kp * np.exp2(rng.integers(-3, 3, (N, 8, 16, 1)))
    g = rng.permutation(8); z = np.ones((8, 1, 1)); z[g[:3]] = np.array([2.0 ** 12, 2.0 ** -50, 2.0 ** -57])[:, None, None]
    k = np.clip(k * z, -65536, 65536); x = np.clip(x * z, -65536, 65536); kp = np.clip(kp * z, -65536, 65536)
    branch(rng, q, tk, int(g[3]), 2); branch(rng, q, tk, int(g[4]), 1)
    return pack(q, k, x, kp, tk)
def setup_inputs_ends(rng):
    q, k, x, kp, tk = parts(rng)
    q = np.where(rng.random(q.shape, dtype=np.float32) < 0.72, rng.integers(0, 2, q.shape) * (V - 1), q)
    q[:, :, 15, V - 1] = V - 1; q[:, :, 14, V - 1] = 0; q[:, :, 0, 0] = 0; q[:, :, 1, 0] = V - 1
    tk = rng.integers(0, 2, tk.shape) * (V - 1); tk[:, :, 0] = 0; tk[:, :, SQ - 1] = V - 1
    k = np.clip(np.rint(2 * k) * 0.5, -4, 4); x = np.clip(np.rint(2 * x) * 0.5, -4, 4); kp = np.rint(2 * kp) * 0.5
    k[:, ::2, :, V - 1] = k[:, ::2, :, 0]
    k[:, 5, :, V - 1] = 40; k[:, 5, :, 0] = -40; k[:, 1, :, V - 1] = -40; k[:, 1, :, 0] = 40
    kp[N - 1, 7] = 64; kp[0, 7] = -64; kp[0, 4] = 64; kp[1, 4] = -64
    return pack(q, k, x, kp, tk)
def setup_inputs_corners(rng):
    q, k, x, kp, tk = parts(rng); ar = np.arange(V); g = rng.permutation(8)
    q[:, g[0]] = ar
    q[:, g[1]] = (ar + 1) % V; tk[:, g[1]] = V - 1 - rng.integers(0, 4, (N, SQ))
    q[:, g[2], 0::2] = (ar - 1) % V; q[:, g[2], 1::2] = ar; tk[:, g[2]] = rng.integers(0, 4, (N, SQ))
    for n in range(N): q[n, g[3]] = (q[n, g[3]] // N) * N + n
    tk[:, g[4]] = tk[:, g[4], :1]
    q[:, g[5]] = rng.permutation(V)
    q[:, g[6]] = np.where(rng.random((N, 16, V)) < 0.3, ar, rng.integers(0, 2, (N, 16, V)) * (V - 1))
    tk[:, g[7]] = rng.integers(0, 2, (N, SQ)) * (V - 1)
    return pack(q, k, x, kp, tk)
def setup_inputs_crowd(rng):
    q, k, x, kp, tk = parts(rng); g = rng.permutation(8)
    size = np.ones(M, np.int64); full = 256 // M; left = 256 - full * M; rows = []
    for n in range(M - 1, 0, -1): size[PAR[n]] += size[n]
    for n in range(1, M):
        if PAR[n] == 0 and size[n] <= left: left -= int(size[n]); rows.append(ROW[n])
    for i in range(4):
        h = int(g[i]); v = (V - 1, int(rng.integers(1, V - 1)), 0, int(rng.integers(1, V - 1)))[i]
        w = rng.permutation(V); w = w[w != v][:19]; u, p, z = int(w[0]), int(w[1]), int(w[2])
        q[:, h, :, v] = v; q[:, h, :, u] = v; q[:, h, :, z] = z; q[:, h, :, p] = z
        for c in rows: q[:, h, c, p] = v
        for c in w[3:]: q[:, h, :, int(c)] = v
        q[1::2, h, :, v] = w[3:][np.argsort(rng.random((N // 2, 16)), axis=1)]
        tk[:, h] = v
        for n in range(N):
            o = rng.permutation(SQ)
            if i % 2 == 1 and full < SQ: tk[n, h, o[full:]] = z; tk[n, h, o[full]] = p
            if i > 1: tk[n, h, o[0]] = u
    for i in (4, 5):
        w = rng.permutation(V)[:3]
        if i == 4: w = np.array([0, V - 1, 1 + int(rng.integers(0, V - 2))])
        for c in w: q[:, g[i], :, int(c)] = w[rng.integers(0, 3, (N, 16))]
        tk[:, g[i]] = w[rng.integers(0, 3, (N, SQ))]
    tk[:, g[6]] = tk[:, g[6], :1]; tk[:, g[7]] = tk[0, g[7], 0]
    return pack(q, k, x, kp, tk)
def setup_inputs_ties(rng):
    q, k, x, kp, tk = parts(rng)
    e = rng.integers(1, 4, (8, 16, 1)) * 2.0 ** -12 * np.where(rng.random((8, 16, 1)) < 0.6, -1, 1)
    k = np.clip(np.rint(4 * k) * 0.25, -2, 2); x = np.clip(np.rint(4 * x) * 0.25, -2, 2) + e
    kp = np.zeros((N, 1, 1, 1)) + e
    g = rng.permutation(8)[:4]; m = 2.0 ** -14 * np.array([1, 2, 3, 8, 16, 24, -1, -3])
    k[:, g] = np.where(rng.random((N, 4, 16, V), dtype=np.float32) < 0.3, 4096.0, 0.0)
    x[:, g] = rng.choice(m, (N, 4, 16, SQ))
    kp[:, g] = -4096.0
    x[:, g[3]] = 4096.0; kp[:, g[3]] = -rng.choice(m, (N, 16, 1))
    return pack(q, k, x, kp, tk)
def check_inputs(d):
    bad = []
    for k in ("qt", "tok"):
        if np.min(d[k]) < 0 or np.max(d[k]) > V - 1: bad.append("range of " + k)
    for k in ("kt", "x0", "kap"):
        v = np.asarray(d[k]).astype(np.float32)
        if not np.all(np.isfinite(v)) or not np.all(np.abs(v) <= 65536) or not np.all((v == 0) | (np.abs(v) >= 2.0 ** -60)): bad.append("size of " + k)
    return bad
def reference(qt, kt, x0, kap, tok):
    Q = qt.astype(np.int64).reshape(N, 8, 16, V); K = kt.astype(np.float32).reshape(N, 8, 16, V)
    x = np.array(x0, np.float32).reshape(N, 8, 16, SQ); kp = kap.astype(np.float32).reshape(N, 8, 16, 1, 1)
    A = np.array(Q); s = np.array(tok, np.int64); half = np.float32(0.5); gi = np.arange(8); trace = []; yn = np.zeros((N, 8, 16, M, SQ), np.float32)
    for t in range(S):
        for r in range(N):
            q = (r + 1 + t % (N - 1)) % N
            node = [s[r]]
            for n in range(1, M): node.append(np.take_along_axis(A[r][:, ROW[n]], node[PAR[n]], 1))
            tk = np.stack(node, axis=1)
            flat = tk.reshape(8, 1, J)
            kn = np.take_along_axis(K[q], flat, 2).reshape(8, 16, M, SQ)
            xs = [x[r]]
            for n in range(1, M): xs.append(xs[PAR[n]] * half + kn[:, :, n])
            xn = np.stack(xs, axis=2)
            th = (xn - kp[q]).reshape(8, 16, 1, J)
            cand = np.take_along_axis(Q[q], flat, 2)
            kc = np.take_along_axis(K[q], cand.reshape(8, 1, 16 * J), 2).reshape(8, 16, 16, J)
            score = np.add.reduce((kc >= th).astype(np.int64), axis=1)
            cols = np.take_along_axis(cand, np.argsort(-score, axis=1, kind="stable"), 1)
            top = cols[:, 0].reshape(8, M, SQ)
            ok = np.zeros((8, M, SQ), bool); ok[:, 0] = True; best = np.zeros((8, SQ), np.int64)
            for n in range(1, M):
                ok[:, n] = ok[:, PAR[n]] & (tk[:, n] == top[:, PAR[n]]); best = np.where(ok[:, n], n, best)
            s[r] = np.take_along_axis(top, best[:, None, :], 1)[:, 0]
            x[r] = np.take_along_axis(xn, best[:, None, None, :], 2)[:, :, 0]
            if t < S - 1:
                for j in range(J): A[r][gi, :, flat[:, 0, j]] = cols[:, :, j]
            else: yn[r] = xn
        trace.append(np.array(s))
    return {"yt": np.stack(trace, axis=2).reshape(N, 8, S * SQ).astype(np.float32), "yx": x.reshape(N, 128, SQ), "yn": yn.reshape(N, 128, J)}

@@ -1,0 +1,784 @@
+from concourse.mybir import AluOpType as OP, ActivationFunctionType as AF
+
+V = 2304
+H = V // 2
+NSTEP = 4
+PAR = [0] * 17 + [1] * 8 + [2] * 4 + [3] * 4 + [4] * 4 + [6] * 3 + [9, 9, 13, 13, 16, 16, 17, 17, 17, 17, 18, 18, 19, 19, 20,
+                                                                  25, 25, 29, 29, 33, 33, 37, 40, 44]
+ROW = [0] + list(range(16)) + list(range(8)) + [0, 1, 8, 9, 0, 2, 10, 11, 0, 3, 12, 13, 0, 14, 15, 0, 5, 0, 6, 0, 15,
+                                                0, 1, 2, 3, 0, 4, 0, 5, 0, 0, 1, 0, 7, 0, 14, 0, 0, 0]
+DEPTH = [0] * 64
+for _n in range(1, 64):
+    DEPTH[_n] = DEPTH[PAR[_n]] + 1
+LENS = (1, 2, 3, 4, 8, 16)
+PARTS = ((0, 2), (2, 4))
+SOON = "rd"
+SHARE = ((0, 3), (1, 3), (2, 3))
+
+
+def _sb(cols, dtype):
+    return ("sbuf", [128, cols], dtype)
+
+
+F, B, HF, I, U = "float32", "bfloat16", "float16", "int32", "uint16"
+SCRATCH = {
+    "q": _sb(V, I), "a": _sb(V + 64, I), "k": _sb(V + 16, B), "kp": _sb(4, F), "tk": _sb(4, I),
+    "pi": _sb(8, I), "col": _sb(32, F), "xp": _sb(176, F), "stp": _sb(176, B), "idw": _sb(160, B), "ide": _sb(160, B),
+    "ido": _sb(160, B), "runs": _sb(160 * len(LENS), B), "negi": _sb(128, B), "bigi": _sb(128, B), "one0": _sb(128, B),
+    "one1": _sb(128, B), "onew": _sb(128, B), "fmi": _sb(128, I), "fm": _sb(128, B), "shf": _sb(128 * 15, B),
+    "dm": _sb(128 * 15, B), "rowx": _sb(80, F), "uc": _sb(320, F), "cu": _sb(324, B), "cid": _sb(192, B), "cidf": _sb(192, F),
+    "zero": _sb(256, B), "ctile": _sb(40, B), "crow": _sb(256, B), "prio": _sb(256, B), "priof": _sb(256, F),
+    "i64": _sb(64, F), "diag": _sb(64, F), "rst": _sb(64, F), "tie": _sb(64, B), "cst": _sb(96, F), "lst": _sb(72, U),
+    "ids": _sb(40, F), "sc": _sb(256, F), "isc": _sb(256, F),
+    "w": _sb(320, F), "u": _sb(324, HF), "rt": _sb(4, U), "pl": _sb(16, U), "ls": _sb(24 * NSTEP, U), "ts": _sb(44, F),
+    "m": _sb(64, B), "pp": _sb(24, B), "vm": _sb(32, F), "ix": _sb(2, U), "nx": _sb(16 * (NSTEP + 1), F), "ytb": _sb(16, F),
+    "nb": _sb(16, F), "ab": _sb(1024, F), "dump": _sb(1024, B), "cnt": _sb(16, F), "o1": _sb(32, F), "off": _sb(16, U),
+    "yw": _sb(264, F), "yo": _sb(256, F),
+    "cd": _sb(256, HF), "tr": _sb(256, F), "ct": _sb(256, U), "kn": _sb(256, F), "x": _sb(256, F), "xh": _sb(200, F),
+    "th": _sb(1024, F), "ge": _sb(2048, B), "key": _sb(256, B), "sg": _sb(1024, B), "es": _sb(768, F), "ks": _sb(256, B),
+    "kc": _sb(1024, B), "runh": _sb(160, B), "negf": _sb(128, F),
+    "ctl": _sb(16, U), "g1": _sb(256, HF), "c16": _sb(16, U), "dg": _sb(256, HF), "xr": _sb(256, F), "xrh": _sb(256, F),
+    "thr": _sb(256, F), "gec": _sb(256, B), "zs": _sb(256, F), "za": _sb(16, I), "zb": _sb(16, I), "cs": _sb(32 * NSTEP, F),
+    "l_xt": _sb(8 * NSTEP, F), "l_ch": _sb(32 * NSTEP, F), "l_lt": _sb(24 * NSTEP, U), "l_e": _sb(768, F), "l_kn": _sb(256, B),
+}
+for _b in range(8):
+    SCRATCH["p%d" % _b] = ("psum", [128, 512], F)
+SEMAPHORES = (["ev", "es_", "et", "eg", "sent", "d_q", "d_k", "d_a", "d_x", "d_kp", "d_tk", "d_yt", "d_yx", "d_yn1", "d_yn3"]
+              + ["a_xt%d" % t for t in range(NSTEP)] + ["a_ch%d" % t for t in range(NSTEP)] + ["a_kn%d" % a for a, _ in PARTS]
+              + ["a_lt%d_%d" % (t, a) for t in range(NSTEP) for a, _ in PARTS]
+              + ["a_e%d_%d" % (t, c) for t in range(NSTEP - 1) for c in range(4)])
+BANKS = ["p%d" % _b for _b in range(8)]
+ENGINE_SEM = {"v": "ev", "s": "es_", "t": "et", "g": "eg"}
+
+
+def ucol(n):
+    if DEPTH[n] == 1:
+        return n % 16
+    return (64 if DEPTH[n] == 2 else 128) + 64 * (n // 16 - 1) + n % 16
+
+
+def runs_of(level, up):
+    out = []
+    for n in range(1, 64):
+        if DEPTH[n] != level:
+            continue
+        p = n
+        for _ in range(up):
+            p = PAR[p]
+        if out and out[-1][0] == p and out[-1][1] == n // 16:
+            out[-1][3] += 1
+        else:
+            out.append([p, n // 16, n % 16, 1])
+    cut = []
+    for p, b, lo, ln in out:
+        while ln:
+            part = max(x for x in LENS if x <= ln)
+            cut.append((p, b, lo, part))
+            lo, ln = lo + part, ln - part
+    return cut
+
+
+CYC, GATHER, SCATTER, PE_COL, PE_LAT, WAKE, ISSUE, HOP, ROW_NS, LINK, DMA0, HBM = 1.0, 1.5, 3.5, 0.5, 100, 60, 600, 2100, 60, 12.0, 2000, 200.0
+
+
+PASSES = 60
+SHAKE = 600
+PLANS = {}
+
+
+def arrange(ops, sends):
+    n = len(ops)
+    pre = []
+    for op in ops:
+        pre.append([sends[d[0]] if isinstance(d, tuple) else d for d in op["deps"]])
+    kept = [j for j in range(n) if ops[j]["e"] == "y"]
+    kept = set((d, j) for d, j in zip(kept, kept[1:]) if d not in pre[j])
+    for d, j in kept:
+        pre[j].append(d)
+    succ = [[] for _ in range(n)]
+    left = [len(p) for p in pre]
+    for j, p in enumerate(pre):
+        for d in p:
+            succ[d].append(j)
+
+    def lag(d, j):
+        if (ops[d]["e"] == "t" and ops[j]["e"] == "t") or (d, j) in kept:
+            return 0
+        return ops[d]["lat"] + WAKE
+
+    order, todo, stack = [], list(left), [j for j in range(n) if not left[j]]
+    while stack:
+        j = stack.pop()
+        order.append(j)
+        for k in succ[j]:
+            todo[k] -= 1
+            if not todo[k]:
+                stack.append(k)
+    tail = [0.0] * n
+    for _ in range(NSTEP):
+        for j in reversed(order):
+            tail[j] = ops[j]["ns"] + max([lag(j, k) + tail[k] for k in succ[j]] + [tail[k] for k in ops[j].get("soon", ())] + [0])
+    before = [[(d, lag(d, j)) for d in pre[j]] for j in range(n)]
+    after = [[(k, lag(j, k)) for k in succ[j]] for j in range(n)]
+
+    def fill(turn, needs):
+        gaps = {e: [[0.0, 1e18]] for e in "vstgy"}
+        end = [0.0] * n
+        for j in turn:
+            at, ns, room = max([end[d] + w for d, w in needs[j]] + [0.0]), ops[j]["ns"], gaps[ops[j]["e"]]
+            i = len(room) - 1
+            while i and room[i - 1][1] >= at + ns:
+                i -= 1
+            while max(room[i][0], at) + ns > room[i][1]:
+                i += 1
+            lo, hi = room[i]
+            at = max(lo, at)
+            end[j] = at + ns
+            room[i:i + 1] = [x for x in ([lo, at], [at + ns, hi]) if x[1] - x[0] >= 30]
+        return end
+
+    if n not in PLANS:
+        turn, best = sorted(range(n), key=lambda j: (-tail[j], j)), None
+        seed = 1
+        for p in range(PASSES):
+            end = fill(turn, before)
+            if best is None or max(end) < best[0]:
+                best = (max(end), sorted(range(n), key=lambda j: (end[j] - ops[j]["ns"], j)), back if p else tail)
+            back = fill(sorted(range(n), key=lambda j: -end[j]), after)
+            if p % 3 == 2:
+                back = list(best[2])
+                for j in reversed(order):
+                    seed = (seed * 1103515245 + 12345) % 2147483648
+                    back[j] = max([back[j] + (seed / 2147483648 - 0.5) * SHAKE] + [back[k] + 1 for k in succ[j]])
+            turn = sorted(range(n), key=lambda j: -back[j])
+        PLANS[n] = best
+    out = PLANS[n][1]
+    new = {j: i for i, j in enumerate(out)}
+    return [dict(ops[j], deps=[d if isinstance(d, tuple) else new[d] for d in ops[j]["deps"]]) for j in out]
+
+
+def emit(g, T, ops):
+    queue = {"v": g.vector, "s": g.scalar, "t": g.tensor, "g": g, "y": g.sync}
+    clock = {e: {} for e in queue}
+    number, needed, waits, snaps = {e: 0 for e in queue}, set(), [], []
+    place = []
+    for op in ops:
+        e = op["e"]
+        mine, ck = [], clock[e]
+        deps = sorted(op["deps"], key=lambda d: -d if isinstance(d, int) else 1)
+        for d in deps:
+            if isinstance(d, tuple):
+                if d[0] not in ck:
+                    ck[d[0]] = 1
+                    mine.append(d)
+                continue
+            src = ops[d]
+            if src["sem"] is not None:
+                if src["sem"] in ck:
+                    continue
+                mine.append((src["sem"], 16))
+                ck[src["sem"]] = 1
+            else:
+                if src["e"] == "t" and e == "t":
+                    continue
+                if ck.get(src["e"], -1) >= place[d]:
+                    continue
+                mine.append(d)
+                needed.add(d)
+                ck[src["e"]] = place[d]
+            for key, val in snaps[d].items():
+                if ck.get(key, -1) < val:
+                    ck[key] = val
+        waits.append(mine)
+        snaps.append(dict(ck))
+        place.append(number[e])
+        number[e] += 1
+    count, seen = {}, {e: 0 for e in queue}
+    for n, op in enumerate(ops):
+        if n in needed:
+            seen[op["e"]] += 1
+            count[n] = seen[op["e"]]
+    for n, op in enumerate(ops):
+        q = queue[op["e"]]
+        for d in waits[n]:
+            if isinstance(d, tuple):
+                q.wait_ge(T.sem[d[0]], d[1])
+            else:
+                q.wait_ge(T.sem[ENGINE_SEM[ops[d]["e"]]], count[d])
+        if op["fn"] is None:
+            continue
+        ins = op["fn"]()
+        if op["sem"] is not None:
+            ins.then_inc(T.sem[op["sem"]], 16)
+        elif n in needed:
+            ins.then_inc(T.sem[ENGINE_SEM[op["e"]]], 1)
+
+
+def rank_program(g, core, T, topo):
+    rank = T.rank_of(core)
+    if rank is None:
+        return
+    N = len(T.cores)
+    vec, act, pe = g.vector, g.scalar, g.tensor
+    ops, last, readers, sent, sends, mark = [], {}, {}, [0], {}, []
+
+    def ind(win, off):
+        mark.append(1)
+        return win.indirect(off)
+
+    def took(out, fixed, each=1.0):
+        if mark:
+            each = GATHER * mark.pop()
+        return fixed + max(16, out.shape[1] * each) * CYC
+
+    def add(e, fn, r=(), w=(), sem=None, remote=False, ns=100.0, lat=0.0):
+        banks = [key for key in w if key in BANKS and e != "t"]
+        w = [key for key in w if key not in banks]
+        r = list(r) + banks
+        deps = set()
+        for key in r:
+            if key in last:
+                deps.add(last[key])
+        for key in banks:
+            deps.update(j for j in readers.get(key, ()) if ops[j]["e"] != e)
+        for key in w:
+            if key in last:
+                deps.add(last[key])
+            deps.update(readers.get(key, ()))
+        n = len(ops)
+        ops.append({"e": e, "fn": fn, "deps": deps, "sem": sem, "ns": ns, "lat": lat})
+        for key in r:
+            if not remote:
+                readers.setdefault(key, []).append(n)
+        for key in w:
+            last[key] = n
+            readers[key] = []
+
+    def ts(out, in0, s1, s2, op0, op1, r, w):
+        if op1 is None:
+            add("v", lambda: vec.tensor_scalar(out, in0, s1, None, op0), r, w, ns=took(out, 50))
+        else:
+            add("v", lambda: vec.tensor_scalar(out, in0, s1, s2, op0, op1), r, w, ns=took(out, 50))
+
+    def tt(out, a, b, op, r, w):
+        add("v", lambda: vec.tensor_tensor(out, a, b, op), r, w, ns=took(out, 50, 2.0))
+
+    def cp(out, a, r, w):
+        add("v", lambda: vec.tensor_copy(out, a), r, w, ns=took(out, 50))
+
+    def scan(out, a, b, init, op0, op1, r, w):
+        add("v", lambda: vec.tensor_tensor_scan(out, a, b, init, op0, op1), r, w, ns=took(out, 50))
+
+    def ms(out, val, w, r=()):
+        add("v", lambda: vec.memset(out, val), r, w, ns=took(out, 50))
+
+    def ac(out, a, func, bias, scale, r, w, acc=None):
+        if acc is None:
+            add("s", lambda: act.activation(out, a, func, bias=bias, scale=scale), r, w, ns=took(out, 65))
+        else:
+            add("s", lambda: act.activation(out, a, func, bias=bias, scale=scale, accum_out=acc), r, w, ns=took(out, 85))
+
+    def lin(out, a, scale, bias, r, w):
+        ac(out, a, AF.Identity, bias, scale, r, w)
+
+    def mm(bank, out, lhsT, rhs, start, stop, r):
+        add("t", lambda: pe.matmul(out, lhsT, rhs, start, stop), r, [bank], ns=max(64, out.shape[1]) * PE_COL, lat=PE_LAT)
+
+    def iota(out, pattern, base, mult, w, r=(), whole=False):
+        if whole:
+            add("g", lambda: g.iota(out, pattern, base, mult), r, w, ns=took(out, 130, 2.0))
+        else:
+            add("g", lambda: g.iota(out, pattern, base, mult, allow_small_or_imprecise_dtypes=True), r, w, ns=took(out, 130, 2.0))
+
+    def dma(e, out, a, sem, r, w, nbytes=0):
+        add(e, lambda: (g.sync if e == "y" else act).dma_start(out, a), r, w, sem, ns=50, lat=DMA0 + nbytes / HBM)
+
+    def send(to, out, a, sem, r, width):
+        dst = T.cores[to]
+        rid, pid = topo.addr(dst, core)
+        ways = len(topo.engines(core, dst))
+        sent[0] += ways
+        sends[sem] = len(ops)
+        add("g", lambda: g.remote_dma(out, a, T.sem[sem], T.sem.sent, pid, rid, topo.mask(core, dst)), r, remote=True,
+            ns=ISSUE, lat=HOP + 128 / ways * (ROW_NS + width / LINK))
+
+    def lands(key, sem, frm):
+        last[key] = (sem, len(topo.engines(T.cores[frm], core)))
+
+    def verifier(t):
+        return (rank + 1 + t % (N - 1)) % N
+
+    def drafter(t):
+        return (rank - 1 - t % (N - 1)) % N
+
+    for t in range(NSTEP):
+        lands("l_xt%d" % t, "a_xt%d" % t, drafter(t))
+        for a, b in PARTS:
+            for c in range(a, b):
+                lands("l_lt%d_%d" % (t, c), "a_lt%d_%d" % (t, a), drafter(t))
+        lands("l_ch%d" % t, "a_ch%d" % t, verifier(t))
+        for c in range(4):
+            if t < NSTEP - 1:
+                lands("l_e%d_%d" % (t, c), "a_e%d_%d" % (t, c), verifier(t))
+    for a, b in PARTS:
+        for c in range(a, b):
+            lands("l_kn%d" % c, "a_kn%d" % a, verifier(NSTEP - 1))
+
+    col, cst, lst = T.col, T.cst, T.lst
+    ident = T.idw[:, 16:144]
+    C_I, C_0, C_N0, C_EV, C_OD, C_UC, C_KB, C_EB, C_S, C_Q, C_PM, C_IX, C_H8, C_MX, C_M4, C_NK, C_T = range(17)
+    C_T2, C_NB, C_K2 = 17, 20, 24
+
+    def cc(j):
+        return col[:, j:j + 1]
+
+    def run(lo, ln):
+        at = 160 * LENS.index(ln) + 15 - lo
+        return T.runs[:, at:at + 128]
+
+    ones = run(0, 16)
+    K_JUNK, K_DMK, K_S4, K_A, K_B = 0, 16, 32, 40, 64
+    L_UC, L_PM, L_PAR, L_REP, L_DA, L_DB, L_DC = 0, 20, 36, 52, 56, 58, 60
+
+    ms(T.tk[:], 0, ["tk"])
+    dma("s", T.nx[:, 0:4], T.x0[:], "d_x", [], ["nx0x"])
+    dma("s", T.kp[:, 0:1], T.kap[:], "d_kp", [], ["kp"])
+    dma("y", T.tk[0:128:16, :], T.tok[:], "d_tk", [], ["tk"])
+    dma("y", T.q[:], T.qt[:], "d_q", [], ["q"], 128 * V * 4)
+    dma("y", T.k[:, 0:V], T.kt[:], "d_k", [], ["k"], 128 * V * 6)
+    dma("y", T.a[:, 0:V], T.qt[:], "d_a", ["q"], ["a"], 128 * V * 6)
+
+    iota(T.pi[:, 0:1], [[0, 1]], 0, 1, ["pi0"], whole=True)
+    iota(T.xp[:], [[1, 176]], -16, -1, ["xp"])
+    vals = [15] + list(range(15)) + [500] + ROW[17:46] + [500] * 16 + ROW[46:64]
+    ms(T.rowx[:], -7.0, ["rowx"])
+    ts(T.pi[:, 1:2], T.pi[:, 0:1], 15, None, OP.bitwise_and, None, ["pi0"], ["pi1"])
+    cp(cc(C_I), T.pi[:, 1:2], ["pi1"], ["c_i"])
+    ts(T.stp[:], T.xp[:], cc(C_I), 15.0, OP.add, OP.is_ge, ["xp", "c_i"], ["stp"])
+    ts(T.idw[:], T.xp[:, 0:160], 0.0, None, OP.is_equal, None, ["xp"], ["idw"])
+    ts(cc(C_0), cc(C_I), 0.0, None, OP.is_equal, None, ["c_i"], ["c_0"])
+    for j, ln in enumerate(LENS):
+        tt(T.runs[:, 160 * j:160 * j + 160], T.stp[:, 16:176], T.stp[:, 16 - ln:176 - ln], OP.subtract, ["stp"], ["run%d" % ln])
+    RUNS = ["run%d" % ln for ln in LENS]
+    ts(T.u[:, 320:324], T.tk[:], -float(H), cc(C_0), OP.add, OP.mult, ["tk", "c_0"], ["rd"])
+    mm("p0", T.p0[:, 0:4], ones, T.u[:, 320:324], True, True, ["rd", "run16"])
+    ts(T.nx[:, 4:8], T.p0[:, 0:4], float(H), None, OP.add, None, [], ["p0", "nx0t"])
+    ts(T.rt[:], T.p0[:, 0:4], float(H), None, OP.add, None, [], ["p0", "rt"])
+    j, pieces = 0, []
+    while j < 80:
+        n = 1
+        if j + 1 < 80 and vals[j + 1] - vals[j] in (0, 1) and vals[j] != 0:
+            while j + n < 80 and vals[j + n] - vals[j + n - 1] == vals[j + 1] - vals[j]:
+                n += 1
+        if vals[j] != 0:
+            key = "rowx%d" % j
+            pieces.append(key)
+            if n > 1 and vals[j + 1] != vals[j]:
+                iota(T.rowx[:, j:j + n], [[1, n]], vals[j] - 7, 0, [key], ["rowx"])
+            else:
+                ms(T.rowx[:, j:j + n], float(vals[j] - 7), [key], ["rowx"])
+        j += n
+    iota(cst[:, K_A:K_A + 20], [[16, 5], [0, 4]], 0, 0, ["k_a"])
+    iota(T.cidf[:], [[1, 192]], 8, 0, ["cidf"])
+    send(verifier(0), T.l_xt[:, 0:8], T.nx[:, 0:8], "a_xt0", ["nx0x", "nx0t"], 32)
+    ts(lst[:, L_UC:L_UC + 20], cst[:, K_A:K_A + 20], cc(C_I), None, OP.add, None, ["k_a", "c_i"], ["l_uc"])
+    lin(cc(C_UC), cc(C_I), -float(V), float(H + 7 * V), ["c_i"], ["c_uc"])
+    iota(T.zero[:, 0:40], [[0, 40]], 0, 0, ["zero"])
+    iota(T.zero[:, 40:256], [[0, 216]], 0, 0, ["zero2"])
+    ts(T.cu[:, 0:320], ind(T.rowx[:], lst[:, L_UC:L_UC + 20]), 144.0, float(H), OP.mult, OP.min, pieces + ["l_uc"], ["cu"])
+    ts(T.cu[:, 320:324], T.zero[:, 0:4], float(H), cc(C_0), OP.add, OP.mult, ["zero", "c_0"], ["curd"])
+    lin(T.uc[:], ind(T.rowx[:], lst[:, L_UC:L_UC + 20]), float(V), cc(C_UC), pieces + ["l_uc", "c_uc"], ["uc"])
+    lin(T.cidf[:, 0:64:16], T.cidf[:, 0:64:16], 1.0, 64.0, [], ["cidf"])
+    lin(T.cid[:], T.cidf[:], cc(C_0), 0.0, ["cidf", "c_0"], ["cid"])
+
+    def node_cols(src, n):
+        return src[:, ucol(n):ucol(n) + 49:16]
+
+    def pe_parents(src, init, keys, level, up, at, bank="p1"):
+        first = 1 if level == 2 else 2
+        rr = runs_of(level, up)
+        mm(bank, T[bank][:, at:at + 8], ident, init[:, 16 + at:24 + at], True, False, keys[1:] + ["idw"])
+        for n, (p, b, lo, ln) in enumerate(rr):
+            o = at + 4 * (b - first)
+            mm(bank, T[bank][:, o:o + 4], run(lo, ln), node_cols(src, p), False, n == len(rr) - 1, keys + RUNS)
+
+    def pe_tile(src, init, keys, level):
+        if level == 1:
+            mm("p0", T.p0[:, 0:8], ident, init[:, 0:8], True, False, keys[1:] + ["idw"])
+            mm("p4", T.p4[:, 8:16], ident, init[:, 8:16], True, False, keys[1:] + ["idw"])
+            mm("p0", T.p0[:, 0:4], run(0, 1), src[:, 320:324], False, False, keys[1:] + RUNS)
+        for bank, pair, closes in (("p0", (0, 1), 2), ("p4", (2, 3), 3)):
+            for i in range(16):
+                blocks = [b for b in pair if 16 * b + i > 0 and DEPTH[16 * b + i] == level]
+                if blocks:
+                    base = ucol(16 * blocks[0] + i)
+                    mm(bank, T[bank][:, 4 * blocks[0]:4 * blocks[-1] + 4], run(i, 1), src[:, base:base + 64 * len(blocks) - 15:16],
+                       False, level == closes and i == 15, keys + RUNS)
+
+    def pe_row(src, inits, keys):
+        for n, init in enumerate(inits):
+            mm("p2", T.p2[:, 0:256], ident, init, n == 0, False, keys + ["idw"])
+        mm("p2", T.p2[:, 0:64:16], ones, src[:, 320:324], False, False, keys + RUNS)
+        for s in range(4):
+            mm("p2", T.p2[:, 16 * s + 1:16 * s + 16], ones, src[:, 16 * s + 1:16 * s + 16], False, False, keys)
+        mm("p2", T.p2[:, 64:128:16], ones, src[:, 0:64:16], False, False, keys)
+        mm("p2", T.p2[:, 64:192], ones, src[:, 64:192], False, False, keys)
+        mm("p2", T.p2[:, 128:256], ones, src[:, 192:320], False, True, keys)
+
+    pe_parents(T.cid, T.zero, ["cid", "zero"], 2, 1, 0, "p7")
+    pe_parents(T.cid, T.zero, ["cid", "zero"], 3, 1, 8, "p7")
+    keys = ["cu", "curd", "zero"]
+    pe_parents(T.cu, T.zero, keys, 2, 1, 0)
+    pe_parents(T.cu, T.zero, keys, 3, 1, 8)
+    pe_parents(T.cu, T.zero, keys, 3, 2, 16)
+    for level in (1, 2, 3):
+        pe_tile(T.cu, T.zero, keys, level)
+    pe_row(T.cu, [T.zero[:]], keys + ["zero2"])
+    ac(T.ids[:, 0:16], T.p7[:, 0:16], AF.Identity, 0.0, 1.0, [], ["p7", "ids"])
+    ac(T.ctile[:, 0:8], T.p0[:, 0:8], AF.Identity, 0.0, 1.0, [], ["p0", "ctile"])
+    ac(T.ctile[:, 8:16], T.p4[:, 8:16], AF.Identity, 0.0, 1.0, [], ["p4", "ctile2"])
+    ac(T.crow[:], T.p2[:, 0:256], AF.Identity, 0.0, 1.0, [], ["p2", "crow"])
+    ts(T.ids[:, 16:32], T.ids[:, 0:16], 0.0, None, OP.is_equal, None, ["ids"], ["idz"])
+    tt(T.ctile[:, 16:32], T.p1[:, 0:16], T.ids[:, 16:32], OP.subtract, ["idz"], ["p1", "cpl"])
+    tt(T.ctile[:, 32:40], T.p1[:, 16:24], T.ids[:, 24:32], OP.subtract, ["idz"], ["p1", "cgp"])
+    lin(cc(C_MX), cc(C_0), float(V), 0.0, ["c_0"], ["c_mx"])
+
+    def later_constants():
+        iota(T.i64[:], [[0, 4], [1, 16]], 0, 0, ["i64"])
+        iota(cst[:, K_S4:K_S4 + 4], [[1, 4]], 0, 0, ["k_s4"])
+        iota(cst[:, K_JUNK:K_JUNK + 16], [[0, 4], [16, 4]], V, 0, ["k_junk"])
+        iota(cst[:, K_B:K_B + 16], [[64, 4], [4, 4]], 0, 0, ["k_b"])
+        iota(cst[:, K_DMK:K_DMK + 12], [[0, 3], [1, 4]], 0, 0, ["k_dmk"])
+        iota(T.fmi[:], [[-1, 128]], 128, 1, ["fmi"], whole=True)
+        iota(T.priof[:], [[0, 4], [1, 4], [4, 16]], 0, 0, ["priof"])
+        iota(T.k[:, V:V + 16], [[0, 16]], 0, 0, ["kz"])
+        ts(T.diag[:], T.i64[:], cc(C_I), None, OP.is_equal, None, ["i64", "c_i"], ["diag"])
+        ts(T.rst[:], T.i64[:], 0.0, None, OP.not_equal, None, ["i64"], ["rst"])
+        lin(T.tie[:], T.i64[:], -4096.0, 15 * 4096.0, ["i64"], ["tie"])
+        lin(T.onew[:], ones, 65536.0, 0.0, RUNS, ["onew"])
+        cp(lst[:, L_REP:L_REP + 4], cst[:, K_S4:K_S4 + 4], ["k_s4"], ["l_rep"])
+        lin(cc(C_NK), T.kp[:, 0:1], -1.0, 0.0, ["kp"], ["c_nk"])
+        yield
+        ts(T.fmi[:], T.fmi[:], 15, None, OP.bitwise_and, None, [], ["fmi"])
+        ts(T.pi[:, 2:3], T.pi[:, 0:1], 4, 1, OP.logical_shift_right, OP.bitwise_and, ["pi0"], ["pi2"])
+        ts(T.pi[:, 3:4], T.pi[:, 0:1], 3, None, OP.bitwise_and, None, ["pi0"], ["pi3"])
+        ts(T.pi[:, 4:5], T.pi[:, 1:2], 2, None, OP.logical_shift_right, None, ["pi1"], ["pi4"])
+        lin(T.negi[:], ident, -1.0, 0.0, ["idw"], ["negi"])
+        tt(T.fm[:], T.fmi[:], ones, OP.mult, ["fmi"] + RUNS, ["fm"])
+        cp(cc(C_OD), T.pi[:, 2:3], ["pi2"], ["c_od"])
+        cp(cc(C_S), T.pi[:, 3:4], ["pi3"], ["c_s"])
+        cp(cc(C_Q), T.pi[:, 4:5], ["pi4"], ["c_q"])
+        for d in range(1, 16):
+            ts(T.shf[:, 128 * (d - 1):128 * d], T.fm[:], float(d), None, OP.is_equal, None, ["fm"], ["shf%d" % d])
+            bank = "p%d" % (3 + (d - 1) // 4)
+            o = 128 * ((d - 1) % 4)
+            mm(bank, T[bank][:, o:o + 128], ident, T.shf[:, 128 * (d - 1):128 * d], True, False, ["shf%d" % d, "idw"])
+            mm(bank, T[bank][:, o:o + 128], ident, T.negi[:], False, True, ["negi"])
+            if d % 4 == 0 or d == 15:
+                lo = 128 * 4 * ((d - 1) // 4)
+                ac(T.dm[:, lo:128 * d], T[bank][:, 0:128 * d - lo], AF.Identity, 0.0, 1.0 if d <= 8 else -float(H), [], [bank, "dm%d" % d])
+        yield
+        ac(T.bigi[:], ident, AF.Identity, 0.0, float(H), ["idw"], ["bigi"])
+        ac(T.prio[:], T.priof[:], AF.Identity, 0.0, 1.0 / 128, ["priof"], ["prio"])
+        lin(cc(C_EV), cc(C_OD), -1.0, 1.0, ["c_od"], ["c_ev"])
+        lin(T.ido[:], T.idw[:], cc(C_OD), 0.0, ["idw", "c_od"], ["ido"])
+        lin(cc(C_PM), cc(C_S), 16.0, cc(C_Q), ["c_s", "c_q"], ["c_pm"])
+        lin(T.ide[:], T.idw[:], cc(C_EV), 0.0, ["idw", "c_ev"], ["ide"])
+        lin(cc(C_M4), cc(C_0), -4.0, 4.0, ["c_0"], ["c_m4"])
+        ts(lst[:, L_PM:L_PM + 16], cst[:, K_B:K_B + 16], cc(C_PM), None, OP.add, None, ["k_b", "c_pm"], ["l_pm"])
+        ts(T.ids[:, 32:36], cst[:, K_S4:K_S4 + 4], 4.0, cc(C_0), OP.add, OP.mult, ["k_s4", "c_0"], ["ida"])
+        ts(lst[:, L_PAR:L_PAR + 4], cst[:, K_S4:K_S4 + 4], cc(C_M4), None, OP.add, None, ["k_s4", "c_m4"], ["l_par0"])
+        tt(T.ids[:, 8:12], T.ids[:, 8:12], T.ids[:, 4:8], OP.add, [], ["ids"])
+        tt(T.ids[:, 4:8], T.ids[:, 0:4], T.ids[:, 32:36], OP.add, ["ida"], ["ids"])
+        lin(cc(C_KB), cc(C_I), -1.0, -128.0, ["c_i"], ["c_kb"])
+        cp(lst[:, L_PAR + 4:L_PAR + 16], T.ids[:, 4:16], ["ids"], ["l_par1"])
+        lin(cc(C_EB), cc(C_I), -float(V), 7.5 * V + H, ["c_i"], ["c_eb"])
+        yield
+        lin(cc(C_T), cc(C_I), -4.0, -32.0, ["c_i"], ["c_t"])
+        lin(cst[:, K_JUNK:K_JUNK + 16], cst[:, K_JUNK:K_JUNK + 16], 1.0, cc(C_I), ["c_i"], ["k_junk"])
+        lin(col[:, C_NB:C_NB + 4], cst[:, K_S4:K_S4 + 4], -1.0, cc(C_T), ["k_s4", "c_t"], ["c_nb"])
+        iota(T.ts[:, 0:4], [[0, 4]], 0, 0, ["tspad"])
+        iota(T.a[:, V:V + 64], [[0, 64]], 0, 0, ["az"], whole=True)
+        ts(cst[:, K_DMK:K_DMK + 12], cst[:, K_DMK:K_DMK + 12], cc(C_S), 4.0, OP.is_equal, OP.mult, ["c_s"], ["k_dmk"])
+        lin(cc(C_N0), cc(C_0), -1.0, 1.0, ["c_0"], ["c_n0"])
+        ts(cc(C_H8), cc(C_I), 8.0, -4.0, OP.is_lt, OP.mult, ["c_i"], ["c_h8"])
+        ts(cc(C_IX), cc(C_Q), 1.0, 16.0, OP.is_equal, OP.mult, ["c_q"], ["c_ix"])
+        lin(T.one0[:], ones, cc(C_0), 0.0, RUNS + ["c_0"], ["one0"])
+        lin(T.one1[:], ones, cc(C_N0), 0.0, RUNS + ["c_n0"], ["one1"])
+        cp(lst[:, L_DA:L_DA + 1], cc(C_S), ["c_s"], ["l_da"])
+        ts(lst[:, L_DB:L_DB + 1], cc(C_S), 4.0, None, OP.add, None, ["c_s"], ["l_db"])
+        ts(lst[:, L_DC:L_DC + 1], cc(C_H8), -2.0, cc(C_S), OP.mult, OP.add, ["c_s", "c_h8"], ["l_dc0"])
+        ts(lst[:, L_DC + 1:L_DC + 2], cc(C_H8), -1.0, cc(C_S), OP.mult, OP.add, ["c_s", "c_h8"], ["l_dc1"])
+        tt(cc(C_IX), cc(C_IX), cc(C_S), OP.add, ["c_s"], ["c_ix"])
+        yield
+
+    def last_constants():
+        ms(T.sc[:, 64:192], 4.0, ["sc"])
+        ms(T.sc[:, 192:256], 8.0, ["sc2"])
+        ms(T.sc[:, 0:64], 2.0, ["sc3"])
+        ms(T.isc[:, 0:4], 1.0, ["is0"])
+        ms(T.isc[:, 4:68], 0.5, ["is1"])
+        ms(T.isc[:, 68:184], 0.25, ["is2"])
+        ms(T.isc[:, 184:256], 0.125, ["is3"])
+        ms(T.sc[:, 64:128:16], 2.0, ["sca"], ["sc"])
+        ms(T.sc[:, 128 + 14:192:16], 8.0, ["scb"], ["sc"])
+        ms(T.sc[:, 128 + 15:192:16], 8.0, ["scc"], ["sc"])
+        if SHARE:
+            lin(T.runh[:], T.runs[:, 0:160], 0.5, 0.0, RUNS, ["runh"])
+            lin(T.negf[:], ident, -1.0, 0.0, ["idw"], ["negf"])
+            for c in range(4):
+                cp(cc(C_K2 + c), cc(C_KB), ["c_kb"], ["c_k2%d" % c])
+                for kq in range(4):
+                    if (c, kq) in SHARE:
+                        ts(cc(C_T2), cc(C_Q), float(kq), 128.0, OP.is_equal, OP.mult, ["c_q"], ["c_t2"])
+                        tt(cc(C_K2 + c), cc(C_K2 + c), cc(C_T2), OP.add, ["c_t2"], ["c_k2%d" % c])
+
+    def draft(t):
+        win, wk = (T.q[:], ["q"]) if t == 0 else (T.a[:, 0:V], ["a"])
+        for level, (lo, hi) in enumerate(((0, 64), (64, 192), (192, 320))):
+            tile = T.rt[:] if level == 0 else T.pl[:, 8 * level - 8:8 * level]
+            tk = "rt" if level == 0 else "pl%d" % level
+            tt(T.w[:, lo:hi], ind(win, tile), T.uc[:, lo:hi], OP.subtract, wk + [tk, "uc"], ["w%d" % level])
+            ts(T.u[:, lo:hi], T.w[:, lo:hi], -float(H), float(H), OP.max, OP.min, ["w%d" % level], ["u%d" % level])
+            if level < 2:
+                pe_parents(T.u, T.ctile, ["u%d" % level, "cpl"], level + 2, 1, 8 * level)
+            pe_tile(T.u, T.ctile, ["u%d" % level, "ctile", "ctile2", "rd"], level + 1)
+            if level < 2:
+                cp(T.pl[:, 8 * level:8 * level + 8], T.p1[:, 8 * level:8 * level + 8], [], ["p1", "pl%d" % (level + 1)])
+            for a, b in PARTS:
+                if max(DEPTH[16 * b - 16:16 * b]) == level + 1:
+                    lo, hi = 24 * t + 4 + 4 * a, 24 * t + 4 + 4 * b
+                    bank = "p4" if a else "p0"
+                    cp(T.ls[:, lo:hi], T[bank][:, 4 * a:4 * b], [], [bank, "lsa%d" % a])
+                    if a == 0:
+                        lo -= 4
+                        ts(T.ls[:, lo:lo + 4], T.p0[:, 0:4], cc(C_MX), None, OP.max, None, ["c_mx"], ["p0", "lsb"])
+                    send(verifier(t), T.l_lt[:, lo:hi], T.ls[:, lo:hi], "a_lt%d_%d" % (t, a), ["lsa%d" % a, "lsb"], 2 * (hi - lo))
+
+    def after_draft(t):
+        pe_parents(T.u, T.ctile, ["u0", "cgp"], 3, 2, 16)
+        ac(T.ts[:, 4:12], T.p0[:, 0:8], AF.Identity, 0.0, 1.0, [], ["p0", "tsl", "tsk"])
+        ac(T.ts[:, 12:20], T.p4[:, 8:16], AF.Identity, 0.0, 1.0, ["tsk"], ["p4", "tsl"])
+        if t < NSTEP - 1:
+            pe_row(T.u, [T.crow[:], T.prio[:]], ["u0", "u1", "u2", "rd", "crow", "prio"])
+        ac(T.ts[:, 20:44], T.p1[:, 0:24], AF.Identity, 0.0, 1.0, [], ["p1", "tsp"])
+        if t < NSTEP - 1:
+            for s in range(4):
+                ac(T.nb[:, s:16:4], T.ts[:, 4 + s:20:4], AF.Identity, cc(C_NB + s), -128.0, ["tsl", "c_nb"], ["nb%d" % s])
+
+    def twins():
+        for c in range(16):
+            b = c // 4
+            ac(T.ab[:, 64 * c:64 * c + 64], T.p2[:, 64 * b:64 * b + 64], AF.Abs, T.nb[:, c:c + 1], 128.0, ["nb%d" % (c % 4)], ["p2", "ab%d" % c])
+        for c in range(16):
+            ac(T.dump[:, 64 * c:64 * c + 64], T.ab[:, 64 * c:64 * c + 64], AF.Relu, 131072.0, -4096.0, ["ab%d" % c], ["cnt%d" % c],
+               acc=T.cnt[:, c:c + 1])
+
+    def places():
+        tt(T.o1[:, 0:16], T.cnt[:], cst[:, K_JUNK:K_JUNK + 16], OP.min, ["cnt%d" % c for c in range(16)] + ["k_junk"], ["o1"])
+        tt(T.o1[:, 16:32], T.o1[:, 0:16], T.ts[:, 4:20], OP.max, ["o1", "tsl"], ["o2"])
+        cp(T.off[:], T.o1[:, 16:32], ["o2"], ["off"])
+
+    def overwrite(t, c):
+        o = 256 * t + 64 * c
+        add("v", lambda: vec.tensor_copy(T.a[:].indirect(T.off[:, 4 * c:4 * c + 4]), T.l_e[:, o:o + 64]),
+            ["off", "l_e%d_%d" % (t, c), "az"], ["a"], ns=50 + 64 * SCATTER * CYC)
+
+    def commit(t):
+        tw, ch = T.l_ch[:, 32 * t + 16:32 * t + 32], "l_ch%d" % t
+        tt(T.m[:, 48:64], ind(tw, lst[:, L_DA:L_DA + 1]), T.ts[:, 4:20], OP.is_equal, [ch, "tsl", "l_da"], ["ma"])
+        tt(T.m[:, 0:16], ind(tw, lst[:, L_DB:L_DB + 1]), T.ts[:, 0:16], OP.is_equal, [ch, "tsl", "tspad", "l_db"], ["mb"])
+        tt(T.m[:, 16:48], ind(tw, lst[:, L_DC:L_DC + 2]), T.ts[:, 12:44], OP.is_equal, [ch, "tsl", "tsp", "l_dc0", "l_dc1"], ["mc"])
+        tt(T.pp[:, 0:16], T.m[:, 8:24], T.m[:, 24:40], OP.mult, ["mb", "mc"], ["ppa"])
+        tt(T.pp[:, 16:24], T.pp[:, 8:16], T.m[:, 40:48], OP.mult, ["ppa", "mc"], ["ppb"])
+        mm("p1", T.p1[:, 24:28], T.one1[:], T.m[:, 48:52], True, False, ["ma", "one1"])
+        mm("p1", T.p1[:, 24:28], T.one0[:], T.m[:, 52:56], False, True, ["ma", "one0"])
+        mm("p1", T.p1[:, 28:32], ones, T.pp[:, 0:4], True, False, ["ppa"])
+        mm("p1", T.p1[:, 28:32], ones, T.pp[:, 4:8], False, True, ["ppa"])
+        mm("p1", T.p1[:, 32:36], ones, T.pp[:, 16:20], True, False, ["ppb"])
+        mm("p1", T.p1[:, 32:36], ones, T.pp[:, 20:24], False, True, ["ppb"])
+        tt(T.vm[:, 12:24], T.p1[:, 24:36], cst[:, K_DMK:K_DMK + 12], OP.mult, ["k_dmk"], ["p1", "vmb"])
+        ts(T.vm[:, 0:12], T.vm[:, 12:24], 4.0, None, OP.min, None, ["vmb"], ["vma"])
+        scan(T.vm[:, 12:24], T.vm[:, 0:12], T.zero[:, 0:12], cc(C_IX), OP.add, OP.add, ["vma", "zero", "c_ix"], ["vmb"])
+        cp(T.ix[:, 0:1], T.vm[:, 23:24], ["vmb"], ["ix"])
+        o, nk = 16 * (t + 1), "nx%d" % (t + 1)
+        cp(T.nx[:, o:o + 16], ind(T.l_ch[:, 32 * t:32 * t + 32], T.ix[:, 0:1]), [ch, "ix"], [nk])
+        if t < NSTEP - 1:
+            send(verifier(t + 1), T.l_xt[:, 8 * t + 8:8 * t + 16], T.nx[:, o:o + 8], "a_xt%d" % (t + 1), [nk], 32)
+        ac(T.ytb[:, 4 * t:4 * t + 4], T.nx[:, o + 4:o + 8], AF.Identity, 0.0, 1.0, [nk], ["yt%d" % t])
+        if t < NSTEP - 1:
+            cp(T.rt[:], T.nx[:, o + 4:o + 8], [nk], ["rt"])
+            ts(T.u[:, 320:324], T.nx[:, o + 4:o + 8], -float(H), cc(C_0), OP.add, OP.mult, [nk, "c_0"], ["rd"])
+
+    def chain(t):
+        xt, xk = T.l_xt[:, 8 * t:8 * t + 8], "l_xt%d" % t
+        o = 32 * t
+        rep = lst[:, L_REP:L_REP + 4]
+        cp(T.ctl[:, 0:4], T.l_xt[:, 8 * t + 4:8 * t + 8], [xk], ["ctl0"])
+        ac(T.thr[:, 0:64], ind(xt, rep), AF.Identity, cc(C_NK), 1.0, [xk, "l_rep", "c_nk"], ["thr0"])
+        ac(T.xrh[:, 0:64], ind(xt, rep), AF.Identity, 0.0, 0.5, [xk, "l_rep"], ["xrh0"])
+        ac(T.cs[:, o:o + 4], T.l_xt[:, 8 * t:8 * t + 4], AF.Identity, 0.0, 1.0, [xk], ["csx0"])
+        for d in range(4):
+            lo, hi, tl, n = 64 * d, 64 * d + 64, T.ctl[:, 4 * d:4 * d + 4], str(d)
+            ts(T.g1[:, lo:hi], ind(T.q[:], tl), -float(H), None, OP.add, None, ["q", "ctl" + n], ["g1" + n])
+            if d:
+                tt(T.xr[:, lo:hi], ind(T.k[:, 0:V], tl), T.xrh[:, lo - 64:lo], OP.add, ["k", "ctl" + n, "xrh%d" % (d - 1)], ["xr" + n])
+                ac(T.thr[:, lo:hi], T.xr[:, lo:hi], AF.Identity, cc(C_NK), 1.0, ["xr" + n, "c_nk"], ["thr" + n])
+                if d < 3:
+                    ac(T.xrh[:, lo:hi], T.xr[:, lo:hi], AF.Identity, 0.0, 0.5, ["xr" + n], ["xrh" + n])
+                ac(T.cs[:, o + 4 * d:o + 4 * d + 4], T.xr[:, lo:hi:16], AF.Identity, 0.0, 1.0, ["xr" + n], ["csx" + n])
+            ts(T.c16[:, 4 * d:4 * d + 4], T.g1[:, lo:hi:16], float(H), None, OP.add, None, ["g1" + n], ["c16" + n])
+            tt(T.dg[:, lo:hi], T.g1[:, lo:hi], T.diag[:], OP.mult, ["g1" + n, "diag"], ["dg" + n])
+            mm("p3", T.p3[:, 0:64], ident, T.tie[:], True, False, ["tie"])
+            mm("p3", T.p3[:, 0:64], ones, T.dg[:, lo:hi], False, False, ["dg" + n])
+            tt(T.gec[:, lo:hi], ind(T.k[:, 0:V], T.c16[:, 4 * d:4 * d + 4]), T.thr[:, lo:hi], OP.is_ge,
+               ["k", "c16" + n, "thr" + n], ["gec" + n])
+            mm("p3", T.p3[:, 0:64], T.onew[:], T.gec[:, lo:hi], False, True, ["gec" + n, "onew"])
+            scan(T.zs[:, lo:hi], T.rst[:], T.p3[:, 0:64], 0.0, OP.mult, OP.max, ["rst"], ["p3", "zs" + n])
+            ts(T.za[:, 4 * d:4 * d + 4], T.zs[:, lo + 15:hi:16], float(H), None, OP.add, None, ["zs" + n], ["za" + n])
+            ts(T.zb[:, 4 * d:4 * d + 4], T.za[:, 4 * d:4 * d + 4], 4095, None, OP.bitwise_and, None, ["za" + n], ["zb" + n])
+            if d < 3:
+                cp(T.ctl[:, 4 * d + 4:4 * d + 8], T.zb[:, 4 * d:4 * d + 4], ["zb" + n], ["ctl%d" % (d + 1)])
+        cp(T.cs[:, o + 16:o + 32], T.zb[:], ["zb0", "zb1", "zb2", "zb3"], ["cst"])
+        send(drafter(t), T.l_ch[:, o:o + 32], T.cs[:, o:o + 32], "a_ch%d" % t, ["cst", "csx0", "csx1", "csx2", "csx3"], 128)
+
+    def roots(t):
+        xk = "l_xt%d" % t
+        ac(T.xh[:, 0:4], T.l_xt[:, 8 * t:8 * t + 4], AF.Identity, 0.0, 1.0, [xk], ["xha"])
+        ac(T.xh[:, 4:8], T.l_xt[:, 8 * t:8 * t + 4], AF.Identity, 0.0, 0.5, [xk], ["xhb"])
+
+    def numbers_list(t, c0, c1):
+        o = 24 * t + (4 if c0 else 0)
+        return T.l_lt[:, o + 4 * c0:o + 4 * c1]
+
+    PREP = sorted(set([(0, 1)] + [(max(a, 1), b) for a, b in PARTS if b > 1]))
+
+    def verify(t):
+        def prepare(bank, c0, c1):
+            lk, o = "l_lt%d_%d" % (t, c0), 24 * t + 4
+            cs = range(c0, c1)
+            ts(T.cd[:, 64 * c0:64 * c1], ind(T.q[:], T.l_lt[:, o + 4 * c0:o + 4 * c1]), -float(H), None, OP.add, None, ["q", lk],
+               ["cd%d" % c for c in cs])
+            ac(T.kn[:, 64 * c0:64 * c1], ind(T.k[:], numbers_list(t, c0, c1)), AF.Identity, 0.0, 1.0, ["k", "kz", lk], ["kn%d" % c for c in cs])
+            mix(bank, c0, c1)
+            add("v", lambda: vec.transpose(T.tr[:, 64 * c0:64 * c1], T[bank][:, 64 * c0:64 * c1]), [], [bank] + ["tr%d" % c for c in cs],
+                ns=50 + 64 * (c1 - c0) * CYC)
+            ts(T.ct[:, 64 * c0:64 * c1], ind(T.tr[:, 0:64 * c1], lst[:, L_PM + 4 * c0:L_PM + 4 * c1]), float(H), None, OP.add, None,
+               ["tr%d" % c for c in range(c1)] + ["l_pm"], ["ct%d" % c for c in cs])
+
+        def mix(bank, c0, c1):
+            for b in range(2 * c0, 2 * c1):
+                for h in range(2):
+                    at = 32 * b + 16 * h
+                    src = T.ide if h == 0 else T.ido
+                    for to in range(2):
+                        lo = 16 + 16 * (h - to)
+                        mm(bank, T[bank][:, at:at + 16], src[:, lo:lo + 128], T.cd[:, 32 * b + 16 * to:32 * b + 16 * to + 16],
+                           to == 0, to == 1, ["cd%d" % c0, "ide", "ido"])
+
+        def state(c):
+            at = 64 * c
+            tt(T.x[:, at:at + 64], ind(T.xh[:, 0:8 + at], lst[:, L_PAR + 4 * c:L_PAR + 4 * c + 4]), T.kn[:, at:at + 64],
+               OP.add, ["xha", "xhb", "l_par0", "l_par1", "kn%d" % c] + ["xh%d" % j for j in range(c)], ["x%d" % c])
+
+        def half(c):
+            ac(T.xh[:, 8 + 64 * c:72 + 64 * c], T.x[:, 64 * c:64 * c + 64], AF.Identity, 0.0, 0.5, ["x%d" % c], ["xh%d" % c])
+
+        def limits(c):
+            for j in range(4):
+                at = 256 * c + 64 * j
+                ac(T.th[:, at:at + 64], T.x[:, 64 * c:64 * c + 64], AF.Identity, cc(C_NK), 1.0, ["x%d" % c, "c_nk"], ["th%d_%d" % (c, j)])
+
+        def votes(c, kq):
+            at, gk = 1024 * (c % 2) + 256 * kq, "ge%d_%d" % (c % 2, kq)
+            bank = "p4" if c % 2 == 0 else "p0"
+            numbers, th = ind(T.k[:, 0:V], T.ct[:, 64 * c + 16 * kq:64 * c + 16 * kq + 16]), T.th[:, 256 * c:256 * c + 256]
+            tk = ["th%d_%d" % (c, j) for j in range(4)]
+            if (c, kq) in SHARE:
+                kc = T.kc[:, 256 * c:256 * c + 256]
+                ac(kc, numbers, AF.Identity, 0.0, 1.0, ["k", "ct%d" % c], ["kc%d" % c])
+                add("t", lambda: pe.matmul(T.p1[:, 256:512], T.negf[:], th, True, False), tk + ["negf"], ["p1"], ns=1024 * PE_COL, lat=PE_LAT)
+                mm("p1", T.p1[:, 256:512], ident, kc, False, True, ["kc%d" % c])
+                ac(T.ge[:, at:at + 256], T.p1[:, 256:512], AF.Sign, 2.0 ** -100, 1.0, [], ["p1", gk])
+            else:
+                tt(T.ge[:, at:at + 256], numbers, th, OP.is_ge, ["k", "ct%d" % c] + tk, [gk])
+            for kk in range(4):
+                k = 4 * kq + kk
+                lhs = T.runh[:, 15 - k:143 - k] if (c, kq) in SHARE else run(k, 1)
+                mm(bank, T[bank][:, 0:64], lhs, T.ge[:, at + 64 * kk:at + 64 * kk + 64], k == 0, k == 15, [gk, "runh"])
+
+        def ranks(c):
+            bank = "p4" if c % 2 == 0 else "p0"
+            key, kk = T.key[:, 64 * c:64 * c + 64], "key%d" % c
+            ac(key, T[bank][:, 0:64], AF.Identity, cc(C_K2 + c if SHARE else C_KB), 16.0, ["c_kb", "c_k2%d" % c], [bank, kk])
+            so = 512 * (c % 2)
+            for d in range(1, 9):
+                db = ("p5" if c % 2 == 0 else "p6") if c < 3 else ("p6" if d <= 4 else "p5")
+                mm(db, T[db][:, 64 * d - 64:64 * d], T.dm[:, 128 * d - 128:128 * d], key, True, True, [kk, "dm4", "dm8"])
+            mm("p7", T.p7[:, 0:64], ident, T.cd[:, 64 * c:64 * c + 64], True, False, ["cd%d" % c])
+            if c < 3:
+                db = "p5" if c % 2 == 0 else "p6"
+                ac(T.sg[:, so:so + 512], T[db][:, 0:512], AF.Sign, 0.0, 1.0, [], [db, "sga%d" % (c % 2), "sgb%d" % (c % 2)])
+            else:
+                ts(T.sg[:, so:so + 256], T.p6[:, 0:256], -1.0, 1.0, OP.max, OP.min, [], ["p6", "sga1"])
+                ac(T.sg[:, so + 256:so + 512], T.p5[:, 256:512], AF.Sign, 0.0, 1.0, [], ["p5", "sgb1"])
+            for d in range(1, 9):
+                lhs = T.bigi[:] if d == 8 else T.dm[:, 128 * (15 - d):128 * (16 - d)]
+                mm("p7", T.p7[:, 0:64], lhs, T.sg[:, so + 64 * d - 64:so + 64 * d], False, d == 8,
+                   ["sg%s%d" % ("a" if d <= 4 else "b", c % 2), "dm12", "dm15", "bigi"])
+            at = 256 * t + 64 * c
+            ac(T.es[:, at:at + 64], T.p7[:, 0:64], AF.Identity, cc(C_EB), 1.0, ["c_eb"], ["p7", "es%d" % c])
+            send(drafter(t), T.l_e[:, at:at + 64], T.es[:, at:at + 64], "a_e%d_%d" % (t, c), ["es%d" % c], 256)
+
+        for bank, (c0, c1) in zip(("p7", "p6", "p5"), PREP):
+            prepare(bank, c0, c1)
+        for c in range(4):
+            state(c)
+            limits(c)
+            if c < 3:
+                half(c)
+        for c in range(4):
+            for kq in range(4):
+                votes(c, kq)
+            ranks(c)
+
+    for _ in later_constants():
+        pass
+    last_constants()
+    for t in range(NSTEP):
+        chain(t)
+        draft(t)
+        if t:
+            ops[last["cst"]]["soon"] = [last[SOON]]
+        after_draft(t)
+        if t < NSTEP - 1:
+            twins()
+        commit(t)
+        if t < NSTEP - 1:
+            roots(t)
+            verify(t)
+            places()
+            for c in range(4):
+                overwrite(t, c)
+    t = NSTEP - 1
+    ac(T.yw[:, 0:4], T.nx[:, 16 * t:16 * t + 4], AF.Identity, 0.0, 1.0, ["nx%d" % t], ["ywa"])
+    ac(T.yw[:, 4:8], T.nx[:, 16 * t:16 * t + 4], AF.Identity, 0.0, 1.0, ["nx%d" % t], ["ywb"])
+    for c0, c1 in PREP:
+        tt(T.ks[:, 64 * c0:64 * c1], ind(T.k[:], numbers_list(t, c0, c1)), T.sc[:, 64 * c0:64 * c1], OP.mult,
+           ["k", "kz", "l_lt%d_%d" % (t, c0), "sc", "sc2", "sc3", "sca", "scb", "scc"], ["ks%d" % c for c in range(c0, c1)])
+    for a, b in PARTS:
+        send(drafter(t), T.l_kn[:, 64 * a:64 * b], T.ks[:, 64 * a:64 * b], "a_kn%d" % a, ["ks%d" % c for c in range(a, b)], 128 * (b - a))
+    dma("s", T.yx[:], T.nx[:, 16 * NSTEP:16 * NSTEP + 4], "d_yx", ["nx%d" % NSTEP], ["yx"])
+    dma("s", T.yt[:], T.ytb[0:128:16, :], "d_yt", ["yt%d" % j for j in range(NSTEP)], ["yt"])
+    for c in range(4):
+        at = 64 * c
+        tt(T.yw[:, 8 + at:72 + at], ind(T.yw[:, 0:8 + at], lst[:, L_PAR + 4 * c:L_PAR + 4 * c + 4]), T.l_kn[:, at:at + 64],
+           OP.add, ["ywa", "ywb", "l_kn%d" % c, "l_par0", "l_par1"] + ["yw%d" % j for j in range(c)], ["yw%d" % c])
+        if c % 2:
+            lo, hi, e = at - 64, at + 64, "s" if c == 1 else "y"
+            tt(T.yo[:, lo:hi], ind(T.yw[:, 8:8 + hi], lst[:, L_PM + 4 * c - 4:L_PM + 4 * c + 4]), T.isc[:, lo:hi], OP.mult,
+               ["yw%d" % j for j in range(c + 1)] + ["l_pm", "is0", "is1", "is2", "is3"], ["yo%d" % c])
+            dma(e, T.yn[:, lo:hi], T.yo[:, lo:hi], "d_yn%d" % c, ["yo%d" % c], ["yn%d" % c], 128 * 512)
+    add("g", None, ["yx", "yt", "yn1", "yn3", "a"])
+    emit(g, T, arrange(ops, sends))
+    g.wait_ge(T.sem.sent, sent[0])

@@ -12,8 +12,8 @@ for _n in range(1, 64):
     DEPTH[_n] = DEPTH[PAR[_n]] + 1
 LENS = (1, 2, 3, 4, 8, 16)
 PARTS = ((0, 2), (2, 4))
-SOON = "rd"
-SHARE = ((0, 3), (1, 3), (2, 3))
+SOON = "u2"
+SHARE = ()
 
 
 def _sb(cols, dtype):
@@ -28,7 +28,7 @@ SCRATCH = {
     "one1": _sb(128, B), "onew": _sb(128, B), "fmi": _sb(128, I), "fm": _sb(128, B), "shf": _sb(128 * 15, B),
     "dm": _sb(128 * 15, B), "rowx": _sb(80, F), "uc": _sb(320, F), "cu": _sb(324, B), "cid": _sb(192, B), "cidf": _sb(192, F),
     "zero": _sb(256, B), "ctile": _sb(40, B), "crow": _sb(256, B), "prio": _sb(256, B), "priof": _sb(256, F),
-    "i64": _sb(64, F), "diag": _sb(64, F), "rst": _sb(64, F), "tie": _sb(64, B), "cst": _sb(96, F), "lst": _sb(72, U),
+    "i64": _sb(64, F), "diag": _sb(64, F), "rst": _sb(64, F), "tie": _sb(64, B), "cst": _sb(96, F), "lst": _sb(80, U), "nbc": _sb(16, F),
     "ids": _sb(40, F), "sc": _sb(256, F), "isc": _sb(256, F),
     "w": _sb(320, F), "u": _sb(324, HF), "rt": _sb(4, U), "pl": _sb(16, U), "ls": _sb(24 * NSTEP, U), "ts": _sb(44, F),
     "m": _sb(64, B), "pp": _sb(24, B), "vm": _sb(32, F), "ix": _sb(2, U), "nx": _sb(16 * (NSTEP + 1), F), "ytb": _sb(16, F),
@@ -38,7 +38,7 @@ SCRATCH = {
     "th": _sb(1024, F), "ge": _sb(2048, B), "key": _sb(256, B), "sg": _sb(1024, B), "es": _sb(768, F), "ks": _sb(256, B),
     "kc": _sb(1024, B), "runh": _sb(160, B), "negf": _sb(128, F),
     "ctl": _sb(16, U), "g1": _sb(256, HF), "c16": _sb(16, U), "dg": _sb(256, HF), "xr": _sb(256, F), "xrh": _sb(256, F),
-    "thr": _sb(256, F), "gec": _sb(256, B), "zs": _sb(256, F), "za": _sb(16, I), "zb": _sb(16, I), "cs": _sb(32 * NSTEP, F),
+    "thr": _sb(256, F), "gec": _sb(256, B), "zs": _sb(256, F), "za": _sb(16, F), "cs": _sb(32 * NSTEP, F),
     "l_xt": _sb(8 * NSTEP, F), "l_ch": _sb(32 * NSTEP, F), "l_lt": _sb(24 * NSTEP, U), "l_e": _sb(768, F), "l_kn": _sb(256, B),
 }
 for _b in range(8):
@@ -78,11 +78,14 @@ def runs_of(level, up):
     return cut
 
 
-CYC, GATHER, SCATTER, PE_COL, PE_LAT, WAKE, ISSUE, HOP, ROW_NS, LINK, DMA0, HBM = 1.0, 1.5, 3.5, 0.5, 100, 60, 600, 2100, 60, 12.0, 2000, 200.0
+CYC, GATHER, SCATTER, PE_COL, PE_LAT, WAKE, ISSUE, HOP, ROW_NS, LINK, DMA0, HBM = 0.85, 1.5, 3.5, 0.42, 100, 200, 600, 1500, 60, 12.0, 2000, 200.0
 
 
-PASSES = 60
+PASSES = 24
 SHAKE = 600
+SLACK = 0
+PACE = (2, 2)
+EARLY = (1, 0)
 PLANS = {}
 
 
@@ -120,6 +123,10 @@ def arrange(ops, sends):
             tail[j] = ops[j]["ns"] + max([lag(j, k) + tail[k] for k in succ[j]] + [tail[k] for k in ops[j].get("soon", ())] + [0])
     before = [[(d, lag(d, j)) for d in pre[j]] for j in range(n)]
     after = [[(k, lag(j, k)) for k in succ[j]] for j in range(n)]
+    for j in range(n):
+        for k in ops[j].get("soon", ()):
+            before[k].append((j, -SLACK))
+            after[j].append((k, -SLACK))
 
     def fill(turn, needs):
         gaps = {e: [[0.0, 1e18]] for e in "vstgy"}
@@ -338,7 +345,7 @@ def rank_program(g, core, T, topo):
 
     ones = run(0, 16)
     K_JUNK, K_DMK, K_S4, K_A, K_B = 0, 16, 32, 40, 64
-    L_UC, L_PM, L_PAR, L_REP, L_DA, L_DB, L_DC = 0, 20, 36, 52, 56, 58, 60
+    L_UC, L_PM, L_PAR, L_REP, L_DA, L_DB, L_DC, L_TH = 0, 20, 36, 52, 56, 58, 60, 64
 
     ms(T.tk[:], 0, ["tk"])
     dma("s", T.nx[:, 0:4], T.x0[:], "d_x", [], ["nx0x"])
@@ -494,9 +501,11 @@ def rank_program(g, core, T, topo):
         cp(lst[:, L_PAR + 4:L_PAR + 16], T.ids[:, 4:16], ["ids"], ["l_par1"])
         lin(cc(C_EB), cc(C_I), -float(V), 7.5 * V + H, ["c_i"], ["c_eb"])
         yield
-        lin(cc(C_T), cc(C_I), -4.0, -32.0, ["c_i"], ["c_t"])
+        lin(cc(C_T), cc(C_I), -4.0 / 128, 32.0 / 128, ["c_i"], ["c_t"])
         lin(cst[:, K_JUNK:K_JUNK + 16], cst[:, K_JUNK:K_JUNK + 16], 1.0, cc(C_I), ["c_i"], ["k_junk"])
-        lin(col[:, C_NB:C_NB + 4], cst[:, K_S4:K_S4 + 4], -1.0, cc(C_T), ["k_s4", "c_t"], ["c_nb"])
+        ts(lst[:, L_TH:L_TH + 16], cst[:, K_JUNK:K_JUNK + 16], -float(V), None, OP.add, None, ["k_junk"], ["l_th"])
+        iota(T.nbc[:], [[0, 4], [1, 4]], 0, 0, ["c_nb"])
+        lin(T.nbc[:], T.nbc[:], -1.0 / 128, cc(C_T), ["c_t"], ["c_nb"])
         iota(T.ts[:, 0:4], [[0, 4]], 0, 0, ["tspad"])
         iota(T.a[:, V:V + 64], [[0, 64]], 0, 0, ["az"], whole=True)
         ts(cst[:, K_DMK:K_DMK + 12], cst[:, K_DMK:K_DMK + 12], cc(C_S), 4.0, OP.is_equal, OP.mult, ["c_s"], ["k_dmk"])
@@ -563,19 +572,22 @@ def rank_program(g, core, T, topo):
             pe_row(T.u, [T.crow[:], T.prio[:]], ["u0", "u1", "u2", "rd", "crow", "prio"])
         ac(T.ts[:, 20:44], T.p1[:, 0:24], AF.Identity, 0.0, 1.0, [], ["p1", "tsp"])
         if t < NSTEP - 1:
-            for s in range(4):
-                ac(T.nb[:, s:16:4], T.ts[:, 4 + s:20:4], AF.Identity, cc(C_NB + s), -128.0, ["tsl", "c_nb"], ["nb%d" % s])
+            tt(T.nb[:], T.nbc[:], T.ts[:, 4:20], OP.subtract, ["tsl", "c_nb"], ["nb"])
 
     def twins():
         for c in range(16):
             b = c // 4
-            ac(T.ab[:, 64 * c:64 * c + 64], T.p2[:, 64 * b:64 * b + 64], AF.Abs, T.nb[:, c:c + 1], 128.0, ["nb%d" % (c % 4)], ["p2", "ab%d" % c])
-        for c in range(16):
-            ac(T.dump[:, 64 * c:64 * c + 64], T.ab[:, 64 * c:64 * c + 64], AF.Relu, 131072.0, -4096.0, ["ab%d" % c], ["cnt%d" % c],
-               acc=T.cnt[:, c:c + 1])
+            at = 256 * (c % 4) + 64 * b
+            ac(T.ab[:, at:at + 64], T.p2[:, 64 * b:64 * b + 64], AF.Abs, T.nb[:, c:c + 1], 1.0, ["nb"], ["p2", "ab%d" % c])
+        for h in range(2):
+            ac(T.dump[:, 512 * h:512 * h + 512], T.ab[:, 512 * h:512 * h + 512], AF.Relu, 131072.0, -4096.0 * 128,
+               ["ab%d" % c for c in range(16) if c % 4 // 2 == h], ["near%d" % h])
+        for s in range(4):
+            for i in range(16):
+                mm("p2", T.p2[:, 256:272], run(i, 1), T.dump[:, 256 * s + i:256 * s + 256:16], s + i == 0, s + i == 18, ["near%d" % (s // 2)])
 
     def places():
-        tt(T.o1[:, 0:16], T.cnt[:], cst[:, K_JUNK:K_JUNK + 16], OP.min, ["cnt%d" % c for c in range(16)] + ["k_junk"], ["o1"])
+        tt(T.o1[:, 0:16], T.p2[:, 256:272], cst[:, K_JUNK:K_JUNK + 16], OP.min, ["k_junk"], ["p2", "o1"])
         tt(T.o1[:, 16:32], T.o1[:, 0:16], T.ts[:, 4:20], OP.max, ["o1", "tsl"], ["o2"])
         cp(T.off[:], T.o1[:, 16:32], ["o2"], ["off"])
 
@@ -598,9 +610,8 @@ def rank_program(g, core, T, topo):
         mm("p1", T.p1[:, 32:36], ones, T.pp[:, 16:20], True, False, ["ppb"])
         mm("p1", T.p1[:, 32:36], ones, T.pp[:, 20:24], False, True, ["ppb"])
         tt(T.vm[:, 12:24], T.p1[:, 24:36], cst[:, K_DMK:K_DMK + 12], OP.mult, ["k_dmk"], ["p1", "vmb"])
-        ts(T.vm[:, 0:12], T.vm[:, 12:24], 4.0, None, OP.min, None, ["vmb"], ["vma"])
-        scan(T.vm[:, 12:24], T.vm[:, 0:12], T.zero[:, 0:12], cc(C_IX), OP.add, OP.add, ["vma", "zero", "c_ix"], ["vmb"])
-        cp(T.ix[:, 0:1], T.vm[:, 23:24], ["vmb"], ["ix"])
+        ac(T.vm[:, 0:12], T.vm[:, 12:24], AF.Sign, 0.0, 1.0, ["vmb"], ["vma"], acc=T.vm[:, 24:25])
+        ts(T.ix[:, 0:1], T.vm[:, 24:25], 4.0, cc(C_IX), OP.mult, OP.add, ["vma", "c_ix"], ["ix"])
         o, nk = 16 * (t + 1), "nx%d" % (t + 1)
         cp(T.nx[:, o:o + 16], ind(T.l_ch[:, 32 * t:32 * t + 32], T.ix[:, 0:1]), [ch, "ix"], [nk])
         if t < NSTEP - 1:
@@ -614,19 +625,21 @@ def rank_program(g, core, T, topo):
         xt, xk = T.l_xt[:, 8 * t:8 * t + 8], "l_xt%d" % t
         o = 32 * t
         rep = lst[:, L_REP:L_REP + 4]
-        cp(T.ctl[:, 0:4], T.l_xt[:, 8 * t + 4:8 * t + 8], [xk], ["ctl0"])
+        cp(T.ctl[:, 0:4], T.l_xt[:, 8 * t + 4:8 * t + 8], [xk], ["ctl0_%d" % s for s in range(4)])
         ac(T.thr[:, 0:64], ind(xt, rep), AF.Identity, cc(C_NK), 1.0, [xk, "l_rep", "c_nk"], ["thr0"])
         ac(T.xrh[:, 0:64], ind(xt, rep), AF.Identity, 0.0, 0.5, [xk, "l_rep"], ["xrh0"])
         ac(T.cs[:, o:o + 4], T.l_xt[:, 8 * t:8 * t + 4], AF.Identity, 0.0, 1.0, [xk], ["csx0"])
         for d in range(4):
             lo, hi, tl, n = 64 * d, 64 * d + 64, T.ctl[:, 4 * d:4 * d + 4], str(d)
-            ts(T.g1[:, lo:hi], ind(T.q[:], tl), -float(H), None, OP.add, None, ["q", "ctl" + n], ["g1" + n])
+            tk = ["ctl%d_%d" % (d, s) for s in range(4)]
+            ts(T.g1[:, lo:hi], ind(T.q[:], tl), -float(H), None, OP.add, None, ["q"] + tk, ["g1" + n])
             if d:
-                tt(T.xr[:, lo:hi], ind(T.k[:, 0:V], tl), T.xrh[:, lo - 64:lo], OP.add, ["k", "ctl" + n, "xrh%d" % (d - 1)], ["xr" + n])
+                tt(T.xr[:, lo:hi], ind(T.k[:, 0:V], tl), T.xrh[:, lo - 64:lo], OP.add, ["k", "xrh%d" % (d - 1)] + tk, ["xr" + n])
                 ac(T.thr[:, lo:hi], T.xr[:, lo:hi], AF.Identity, cc(C_NK), 1.0, ["xr" + n, "c_nk"], ["thr" + n])
                 if d < 3:
                     ac(T.xrh[:, lo:hi], T.xr[:, lo:hi], AF.Identity, 0.0, 0.5, ["xr" + n], ["xrh" + n])
-                ac(T.cs[:, o + 4 * d:o + 4 * d + 4], T.xr[:, lo:hi:16], AF.Identity, 0.0, 1.0, ["xr" + n], ["csx" + n])
+                if d == 3:
+                    ac(T.cs[:, o + 4:o + 16], T.xr[:, 64:256:16], AF.Identity, 0.0, 1.0, ["xr1", "xr2", "xr3"], ["csx1"])
             ts(T.c16[:, 4 * d:4 * d + 4], T.g1[:, lo:hi:16], float(H), None, OP.add, None, ["g1" + n], ["c16" + n])
             tt(T.dg[:, lo:hi], T.g1[:, lo:hi], T.diag[:], OP.mult, ["g1" + n, "diag"], ["dg" + n])
             mm("p3", T.p3[:, 0:64], ident, T.tie[:], True, False, ["tie"])
@@ -635,12 +648,14 @@ def rank_program(g, core, T, topo):
                ["k", "c16" + n, "thr" + n], ["gec" + n])
             mm("p3", T.p3[:, 0:64], T.onew[:], T.gec[:, lo:hi], False, True, ["gec" + n, "onew"])
             scan(T.zs[:, lo:hi], T.rst[:], T.p3[:, 0:64], 0.0, OP.mult, OP.max, ["rst"], ["p3", "zs" + n])
-            ts(T.za[:, 4 * d:4 * d + 4], T.zs[:, lo + 15:hi:16], float(H), None, OP.add, None, ["zs" + n], ["za" + n])
-            ts(T.zb[:, 4 * d:4 * d + 4], T.za[:, 4 * d:4 * d + 4], 4095, None, OP.bitwise_and, None, ["za" + n], ["zb" + n])
-            if d < 3:
-                cp(T.ctl[:, 4 * d + 4:4 * d + 8], T.zb[:, 4 * d:4 * d + 4], ["zb" + n], ["ctl%d" % (d + 1)])
-        cp(T.cs[:, o + 16:o + 32], T.zb[:], ["zb0", "zb1", "zb2", "zb3"], ["cst"])
-        send(drafter(t), T.l_ch[:, o:o + 32], T.cs[:, o:o + 32], "a_ch%d" % t, ["cst", "csx0", "csx1", "csx2", "csx3"], 128)
+            ts(T.za[:, 4 * d:4 * d + 4], T.zs[:, lo + 15:hi:16], 1.5 * 2.0 ** 35, 1.5 * 2.0 ** 35, OP.add, OP.subtract, ["zs" + n], ["za" + n])
+            for s in range(4):
+                out = T.ctl[:, 4 * d + 4 + s:4 * d + 5 + s] if d < 3 else T.cs[:, o + 28 + s:o + 29 + s]
+                ts(out, T.zs[:, lo + 16 * s + 15:lo + 16 * s + 16], T.za[:, 4 * d + s:4 * d + s + 1], float(H), OP.subtract, OP.add,
+                   ["zs" + n, "za" + n], ["ctl%d_%d" % (d + 1, s)])
+        cp(T.cs[:, o + 16:o + 28], T.ctl[:, 4:16], ["ctl%d_%d" % (d, s) for d in (1, 2, 3) for s in range(4)], ["cst"])
+        send(drafter(t), T.l_ch[:, o:o + 32], T.cs[:, o:o + 32], "a_ch%d" % t,
+             ["cst", "csx0", "csx1"] + ["ctl4_%d" % s for s in range(4)], 128)
 
     def roots(t):
         xk = "l_xt%d" % t
@@ -685,15 +700,14 @@ def rank_program(g, core, T, topo):
             ac(T.xh[:, 8 + 64 * c:72 + 64 * c], T.x[:, 64 * c:64 * c + 64], AF.Identity, 0.0, 0.5, ["x%d" % c], ["xh%d" % c])
 
         def limits(c):
-            for j in range(4):
-                at = 256 * c + 64 * j
-                ac(T.th[:, at:at + 64], T.x[:, 64 * c:64 * c + 64], AF.Identity, cc(C_NK), 1.0, ["x%d" % c, "c_nk"], ["th%d_%d" % (c, j)])
+            ac(T.th[:, 256 * c:256 * c + 256], ind(T.x[:, 64 * c:64 * c + 64], lst[:, L_TH:L_TH + 16]), AF.Identity, cc(C_NK), 1.0,
+               ["x%d" % c, "c_nk", "l_th"], ["th%d" % c])
 
         def votes(c, kq):
             at, gk = 1024 * (c % 2) + 256 * kq, "ge%d_%d" % (c % 2, kq)
             bank = "p4" if c % 2 == 0 else "p0"
             numbers, th = ind(T.k[:, 0:V], T.ct[:, 64 * c + 16 * kq:64 * c + 16 * kq + 16]), T.th[:, 256 * c:256 * c + 256]
-            tk = ["th%d_%d" % (c, j) for j in range(4)]
+            tk = ["th%d" % c]
             if (c, kq) in SHARE:
                 kc = T.kc[:, 256 * c:256 * c + 256]
                 ac(kc, numbers, AF.Identity, 0.0, 1.0, ["k", "ct%d" % c], ["kc%d" % c])
@@ -740,6 +754,11 @@ def rank_program(g, core, T, topo):
         for c in range(4):
             for kq in range(4):
                 votes(c, kq)
+                gk = last["ge%d_%d" % (c % 2, kq)]
+                if c >= PACE[0] and kq == PACE[1]:
+                    ops[last["es%d" % (c - PACE[0])]]["soon"] = [gk]
+                if t and (c, kq) == EARLY:
+                    ops[last["nx%d" % (t + 1)]]["soon"] = [gk]
             ranks(c)
 
     for _ in later_constants():
@@ -749,7 +768,7 @@ def rank_program(g, core, T, topo):
         chain(t)
         draft(t)
         if t:
-            ops[last["cst"]]["soon"] = [last[SOON]]
+            ops[last["ctl4_3"]]["soon"] = [last[SOON]]
         after_draft(t)
         if t < NSTEP - 1:
             twins()

@@ -13,7 +13,7 @@ for _n in range(1, 64):
 LENS = (1, 2, 3, 4, 8, 16)
 PARTS = ((0, 2), (2, 4))
 SOON = "u2"
-SHARE = ()
+SHARE = ((1, 3), (2, 3))
 
 
 def _sb(cols, dtype):
@@ -28,7 +28,7 @@ SCRATCH = {
     "one1": _sb(128, B), "onew": _sb(128, B), "fmi": _sb(128, I), "fm": _sb(128, B), "shf": _sb(128 * 15, B),
     "dm": _sb(128 * 15, B), "rowx": _sb(80, F), "uc": _sb(320, F), "cu": _sb(324, B), "cid": _sb(192, B), "cidf": _sb(192, F),
     "zero": _sb(256, B), "ctile": _sb(40, B), "crow": _sb(256, B), "prio": _sb(256, B), "priof": _sb(256, F),
-    "i64": _sb(64, F), "diag": _sb(64, F), "rst": _sb(64, F), "tie": _sb(64, B), "cst": _sb(96, F), "lst": _sb(80, U), "nbc": _sb(16, F),
+    "i64": _sb(128, F), "diag": _sb(64, F), "rst": _sb(128, F), "tie": _sb(128, B), "cst": _sb(96, F), "lst": _sb(80, U), "nbc": _sb(16, F),
     "ids": _sb(40, F), "sc": _sb(256, F), "isc": _sb(256, F),
     "w": _sb(320, F), "u": _sb(324, HF), "rt": _sb(4, U), "pl": _sb(16, U), "ls": _sb(24 * NSTEP, U), "ts": _sb(44, F),
     "m": _sb(64, B), "pp": _sb(24, B), "vm": _sb(32, F), "ix": _sb(2, U), "nx": _sb(16 * (NSTEP + 1), F), "ytb": _sb(16, F),
@@ -38,7 +38,7 @@ SCRATCH = {
     "th": _sb(1024, F), "ge": _sb(2048, B), "key": _sb(256, B), "sg": _sb(1024, B), "es": _sb(768, F), "ks": _sb(256, B),
     "kc": _sb(1024, B), "runh": _sb(160, B), "negf": _sb(128, F),
     "ctl": _sb(16, U), "g1": _sb(256, HF), "c16": _sb(16, U), "dg": _sb(256, HF), "xr": _sb(256, F), "xrh": _sb(256, F),
-    "thr": _sb(256, F), "gec": _sb(256, B), "zs": _sb(256, F), "za": _sb(16, F), "cs": _sb(32 * NSTEP, F),
+    "thr": _sb(256, F), "gec": _sb(256, B), "zs": _sb(512, F), "cs": _sb(32 * NSTEP, F),
     "l_xt": _sb(8 * NSTEP, F), "l_ch": _sb(32 * NSTEP, F), "l_lt": _sb(24 * NSTEP, U), "l_e": _sb(768, F), "l_kn": _sb(256, B),
 }
 for _b in range(8):
@@ -78,12 +78,13 @@ def runs_of(level, up):
     return cut
 
 
-CYC, GATHER, SCATTER, PE_COL, PE_LAT, WAKE, ISSUE, HOP, ROW_NS, LINK, DMA0, HBM = 0.85, 1.5, 3.5, 0.42, 100, 200, 600, 1500, 60, 12.0, 2000, 200.0
+CYC, GATHER, SCATTER, PE_COL, PE_LAT, WAKE, ISSUE, HOP, ROW_NS, LINK, DMA0, HBM = 0.9, 1.5, 3.5, 0.45, 100, 180, 250, 1200, 30, 12.0, 2000, 200.0
 
 
-PASSES = 24
-SHAKE = 600
-SLACK = 0
+PASSES = 45
+SHAKE = 1000
+SLACK = 99999
+LOOSE = False
 PACE = (2, 2)
 EARLY = (1, 0)
 PLANS = {}
@@ -105,7 +106,7 @@ def arrange(ops, sends):
             succ[d].append(j)
 
     def lag(d, j):
-        if (ops[d]["e"] == "t" and ops[j]["e"] == "t") or (d, j) in kept:
+        if (ops[d]["e"] == "t" and ops[j]["e"] == "t") or (d, j) in kept or d in ops[j]["loose"]:
             return 0
         return ops[d]["lat"] + WAKE
 
@@ -161,7 +162,7 @@ def arrange(ops, sends):
         PLANS[n] = best
     out = PLANS[n][1]
     new = {j: i for i, j in enumerate(out)}
-    return [dict(ops[j], deps=[d if isinstance(d, tuple) else new[d] for d in ops[j]["deps"]]) for j in out]
+    return [dict(ops[j], deps=[d if isinstance(d, tuple) else new[d] for d in ops[j]["deps"] if d not in ops[j]["loose"]]) for j in out]
 
 
 def emit(g, T, ops):
@@ -253,7 +254,9 @@ def rank_program(g, core, T, topo):
                 deps.add(last[key])
             deps.update(readers.get(key, ()))
         n = len(ops)
-        ops.append({"e": e, "fn": fn, "deps": deps, "sem": sem, "ns": ns, "lat": lat})
+        loose = [d for d in deps if LOOSE and e in "vs" and sem is None and not isinstance(d, tuple) and ops[d]["e"] == e
+                 and ops[d]["sem"] is None and d not in [last.get(key) for key in r]]
+        ops.append({"e": e, "fn": fn, "deps": deps, "sem": sem, "ns": ns, "lat": lat, "loose": loose})
         for key in r:
             if not remote:
                 readers.setdefault(key, []).append(n)
@@ -451,7 +454,7 @@ def rank_program(g, core, T, topo):
     lin(cc(C_MX), cc(C_0), float(V), 0.0, ["c_0"], ["c_mx"])
 
     def later_constants():
-        iota(T.i64[:], [[0, 4], [1, 16]], 0, 0, ["i64"])
+        iota(T.i64[:], [[0, 8], [1, 16]], 0, 0, ["i64"])
         iota(cst[:, K_S4:K_S4 + 4], [[1, 4]], 0, 0, ["k_s4"])
         iota(cst[:, K_JUNK:K_JUNK + 16], [[0, 4], [16, 4]], V, 0, ["k_junk"])
         iota(cst[:, K_B:K_B + 16], [[64, 4], [4, 4]], 0, 0, ["k_b"])
@@ -459,7 +462,7 @@ def rank_program(g, core, T, topo):
         iota(T.fmi[:], [[-1, 128]], 128, 1, ["fmi"], whole=True)
         iota(T.priof[:], [[0, 4], [1, 4], [4, 16]], 0, 0, ["priof"])
         iota(T.k[:, V:V + 16], [[0, 16]], 0, 0, ["kz"])
-        ts(T.diag[:], T.i64[:], cc(C_I), None, OP.is_equal, None, ["i64", "c_i"], ["diag"])
+        ts(T.diag[:], T.i64[:, 0:64], cc(C_I), None, OP.is_equal, None, ["i64", "c_i"], ["diag"])
         ts(T.rst[:], T.i64[:], 0.0, None, OP.not_equal, None, ["i64"], ["rst"])
         lin(T.tie[:], T.i64[:], -4096.0, 15 * 4096.0, ["i64"], ["tie"])
         lin(T.onew[:], ones, 65536.0, 0.0, RUNS, ["onew"])
@@ -642,17 +645,17 @@ def rank_program(g, core, T, topo):
                     ac(T.cs[:, o + 4:o + 16], T.xr[:, 64:256:16], AF.Identity, 0.0, 1.0, ["xr1", "xr2", "xr3"], ["csx1"])
             ts(T.c16[:, 4 * d:4 * d + 4], T.g1[:, lo:hi:16], float(H), None, OP.add, None, ["g1" + n], ["c16" + n])
             tt(T.dg[:, lo:hi], T.g1[:, lo:hi], T.diag[:], OP.mult, ["g1" + n, "diag"], ["dg" + n])
-            mm("p3", T.p3[:, 0:64], ident, T.tie[:], True, False, ["tie"])
+            mm("p3", T.p3[:, 0:128], ident, T.tie[:], True, False, ["tie"])
             mm("p3", T.p3[:, 0:64], ones, T.dg[:, lo:hi], False, False, ["dg" + n])
             tt(T.gec[:, lo:hi], ind(T.k[:, 0:V], T.c16[:, 4 * d:4 * d + 4]), T.thr[:, lo:hi], OP.is_ge,
                ["k", "c16" + n, "thr" + n], ["gec" + n])
-            mm("p3", T.p3[:, 0:64], T.onew[:], T.gec[:, lo:hi], False, True, ["gec" + n, "onew"])
-            scan(T.zs[:, lo:hi], T.rst[:], T.p3[:, 0:64], 0.0, OP.mult, OP.max, ["rst"], ["p3", "zs" + n])
-            ts(T.za[:, 4 * d:4 * d + 4], T.zs[:, lo + 15:hi:16], 1.5 * 2.0 ** 35, 1.5 * 2.0 ** 35, OP.add, OP.subtract, ["zs" + n], ["za" + n])
+            mm("p3", T.p3[:, 0:64], T.onew[:], T.gec[:, lo:hi], False, False, ["gec" + n, "onew"])
+            mm("p3", T.p3[:, 64:128], T.onew[:], T.gec[:, lo:hi], False, True, ["gec" + n, "onew"])
+            scan(T.zs[:, 2 * lo:2 * hi], T.rst[:], T.p3[:, 0:128], 0.0, OP.mult, OP.max, ["rst"], ["p3", "zs" + n])
             for s in range(4):
                 out = T.ctl[:, 4 * d + 4 + s:4 * d + 5 + s] if d < 3 else T.cs[:, o + 28 + s:o + 29 + s]
-                ts(out, T.zs[:, lo + 16 * s + 15:lo + 16 * s + 16], T.za[:, 4 * d + s:4 * d + s + 1], float(H), OP.subtract, OP.add,
-                   ["zs" + n, "za" + n], ["ctl%d_%d" % (d + 1, s)])
+                at = 2 * lo + 16 * s + 15
+                ts(out, T.zs[:, at:at + 1], T.zs[:, at + 64:at + 65], float(H), OP.subtract, OP.add, ["zs" + n], ["ctl%d_%d" % (d + 1, s)])
         cp(T.cs[:, o + 16:o + 28], T.ctl[:, 4:16], ["ctl%d_%d" % (d, s) for d in (1, 2, 3) for s in range(4)], ["cst"])
         send(drafter(t), T.l_ch[:, o:o + 32], T.cs[:, o:o + 32], "a_ch%d" % t,
              ["cst", "csx0", "csx1"] + ["ctl4_%d" % s for s in range(4)], 128)

@@ -2,6 +2,7 @@ from concourse.mybir import AluOpType as OP, ActivationFunctionType as AF
 
 V = 2304
 H = V // 2
+R = 4096
 NSTEP = 4
 PAR = [0] * 17 + [1] * 8 + [2] * 4 + [3] * 4 + [4] * 4 + [6] * 3 + [9, 9, 13, 13, 16, 16, 17, 17, 17, 17, 18, 18, 19, 19, 20,
                                                                   25, 25, 29, 29, 33, 33, 37, 40, 44]
@@ -10,10 +11,16 @@ ROW = [0] + list(range(16)) + list(range(8)) + [0, 1, 8, 9, 0, 2, 10, 11, 0, 3, 
 DEPTH = [0] * 64
 for _n in range(1, 64):
     DEPTH[_n] = DEPTH[PAR[_n]] + 1
-LENS = (1, 2, 3, 4, 8, 16)
-PARTS = ((0, 2), (2, 4))
-SOON = "u2"
-SHARE = ((1, 3), (2, 3))
+FIRST = [DEPTH.index(_d) for _d in range(4)] + [64]
+UCOL, USTEP, START = (320, 0, 64, 192), (16, 16, 32, 32), (0, 1, 16, 40)
+LENS = (1, 2, 4, 8, 16)
+TILES = ((0, 4), (4, 10), (10, 16))
+TILES_LAST = ((0, 4), (4, 12), (10, 16))
+BLOCKS = ((0, 4), (4, 8), (8, 12), (12, 16))
+STATES_LAST = ((0, 4), (4, 8), (8, 12), (10, 16))
+BACK = ((0, 1), (1, 2), (2, 3), (3, 4))
+SHARE = ((0, 3), (1, 3))
+LT = 18
 
 
 def _sb(cols, dtype):
@@ -22,79 +29,77 @@ def _sb(cols, dtype):
 
 F, B, HF, I, U = "float32", "bfloat16", "float16", "int32", "uint16"
 SCRATCH = {
-    "q": _sb(V, I), "a": _sb(V + 64, I), "k": _sb(V + 16, B), "kp": _sb(4, F), "tk": _sb(4, I),
-    "pi": _sb(8, I), "col": _sb(32, F), "xp": _sb(176, F), "stp": _sb(176, B), "idw": _sb(160, B), "ide": _sb(160, B),
-    "ido": _sb(160, B), "runs": _sb(160 * len(LENS), B), "negi": _sb(128, B), "bigi": _sb(128, B), "one0": _sb(128, B),
-    "one1": _sb(128, B), "onew": _sb(128, B), "fmi": _sb(128, I), "fm": _sb(128, B), "shf": _sb(128 * 15, B),
-    "dm": _sb(128 * 15, B), "rowx": _sb(80, F), "uc": _sb(320, F), "cu": _sb(324, B), "cid": _sb(192, B), "cidf": _sb(192, F),
-    "zero": _sb(256, B), "ctile": _sb(40, B), "crow": _sb(256, B), "prio": _sb(256, B), "priof": _sb(256, F),
-    "i64": _sb(128, F), "diag": _sb(64, F), "rst": _sb(128, F), "tie": _sb(128, B), "cst": _sb(96, F), "lst": _sb(80, U), "nbc": _sb(16, F),
-    "ids": _sb(40, F), "sc": _sb(256, F), "isc": _sb(256, F),
-    "w": _sb(320, F), "u": _sb(324, HF), "rt": _sb(4, U), "pl": _sb(16, U), "ls": _sb(24 * NSTEP, U), "ts": _sb(44, F),
-    "m": _sb(64, B), "pp": _sb(24, B), "vm": _sb(32, F), "ix": _sb(2, U), "nx": _sb(16 * (NSTEP + 1), F), "ytb": _sb(16, F),
-    "nb": _sb(16, F), "ab": _sb(1024, F), "dump": _sb(1024, B), "cnt": _sb(16, F), "o1": _sb(32, F), "off": _sb(16, U),
-    "yw": _sb(264, F), "yo": _sb(256, F),
-    "cd": _sb(256, HF), "tr": _sb(256, F), "ct": _sb(256, U), "kn": _sb(256, F), "x": _sb(256, F), "xh": _sb(200, F),
-    "th": _sb(1024, F), "ge": _sb(2048, B), "key": _sb(256, B), "sg": _sb(1024, B), "es": _sb(768, F), "ks": _sb(256, B),
-    "kc": _sb(1024, B), "runh": _sb(160, B), "negf": _sb(128, F),
+    "q": _sb(V, I), "a": _sb(V + 16, I), "k": _sb(V, B), "kp": _sb(4, F), "tk": _sb(4, I), "xi": _sb(4, F),
+    "pi": _sb(8, I), "col": _sb(48, F), "xq": _sb(160, F), "ab": _sb(160 * 4, B), "idw": _sb(160, B), "ide": _sb(160, B), "ido": _sb(160, B),
+    "runs": _sb(160 * len(LENS), B), "runh": _sb(160, B), "negi": _sb(128, B), "negq": _sb(128, B),
+    "negw": _sb(128, B), "negf": _sb(128, F), "onew": _sb(128, B), "upper": _sb(128, B), "fmi": _sb(128, I), "fm": _sb(256, B),
+    "shf": _sb(128 * 15, B), "dm": _sb(128 * 15, B), "lose": _sb(128 * 8, B), "rowx": _sb(80, F), "uc": _sb(320, F),
+    "cu": _sb(384, B), "zero": _sb(48, B), "hp": _sb(48, F), "neg2": _sb(128, B), "ct0": _sb(48, B), "ct1": _sb(16, B), "rows": _sb(176, B), "cst": _sb(128, F),
+    "cb": _sb(224, B), "lst": _sb(80, U), "i64": _sb(128, F), "diag": _sb(64, F), "rst": _sb(128, F), "tie": _sb(128, B),
+    "w": _sb(320, F), "u": _sb(384, HF), "rt": _sb(4, U), "pl": _sb(16, U), "ls": _sb(LT * NSTEP, U),
+    "cts": _sb(48 * NSTEP, HF), "t16": _sb(16, HF), "eq": _sb(128, B), "off": _sb(32, U), "ytb": _sb(12, F),
+    "cd": _sb(256, HF), "tr": _sb(256, F), "ct": _sb(256, U), "ph": _sb(256, F), "x": _sb(256, F), "th": _sb(1024, F),
+    "ge": _sb(2048, B), "kc": _sb(512, B), "key": _sb(256, B), "sg": _sb(1024, B), "es": _sb(768, F),
+    "uta": _sb(80, HF), "utb": _sb(192, HF), "m": _sb(48, B), "one": _sb(20, B), "ix": _sb(20, U), "xg": _sb(64, F),
+    "xs": _sb(32, F), "u0": _sb(64, HF),
     "ctl": _sb(16, U), "g1": _sb(256, HF), "c16": _sb(16, U), "dg": _sb(256, HF), "xr": _sb(256, F), "xrh": _sb(256, F),
-    "thr": _sb(256, F), "gec": _sb(256, B), "zs": _sb(512, F), "cs": _sb(32 * NSTEP, F),
-    "l_xt": _sb(8 * NSTEP, F), "l_ch": _sb(32 * NSTEP, F), "l_lt": _sb(24 * NSTEP, U), "l_e": _sb(768, F), "l_kn": _sb(256, B),
+    "thr": _sb(256, F), "gec": _sb(256, B), "zs": _sb(512, F), "cs": _sb(48, F), "pp": _sb(24, B), "vm": _sb(32, F),
+    "fin": _sb(16, F),
+    "l_x": _sb(8 * NSTEP, F), "l_lt": _sb(LT * NSTEP, U), "l_j": _sb(16, U), "l_ct": _sb(48 * NSTEP, HF), "l_e": _sb(768, F),
+    "l_y": _sb(256, F), "l_f": _sb(8, F),
 }
 for _b in range(8):
     SCRATCH["p%d" % _b] = ("psum", [128, 512], F)
-SEMAPHORES = (["ev", "es_", "et", "eg", "sent", "d_q", "d_k", "d_a", "d_x", "d_kp", "d_tk", "d_yt", "d_yx", "d_yn1", "d_yn3"]
-              + ["a_xt%d" % t for t in range(NSTEP)] + ["a_ch%d" % t for t in range(NSTEP)] + ["a_kn%d" % a for a, _ in PARTS]
-              + ["a_lt%d_%d" % (t, a) for t in range(NSTEP) for a, _ in PARTS]
-              + ["a_e%d_%d" % (t, c) for t in range(NSTEP - 1) for c in range(4)])
-BANKS = ["p%d" % _b for _b in range(8)]
+SEMAPHORES = (["ev", "es_", "et", "eg", "sent", "d_q", "d_k", "d_a", "d_x", "d_kp", "d_tk", "d_yt", "d_yu", "d_yx", "d_y0", "d_y1",
+               "a_y0", "a_y1", "a_f", "a_r"]
+              + ["a_x%d" % t for t in range(NSTEP)] + ["a_ct%d" % t for t in range(NSTEP)]
+              + ["a_lt%d_%d" % (t, j) for t in range(NSTEP) for j in range(3)]
+              + ["a_e%d_%d" % (t, c) for t in range(NSTEP - 1) for c in range(5)])
+WHOLE = ("q", "a", "k")
 ENGINE_SEM = {"v": "ev", "s": "es_", "t": "et", "g": "eg"}
 
 
-def ucol(n):
-    if DEPTH[n] == 1:
-        return n % 16
-    return (64 if DEPTH[n] == 2 else 128) + 64 * (n // 16 - 1) + n % 16
-
-
-def runs_of(level, up):
+def runs_of(depth, up, first=FIRST):
     out = []
-    for n in range(1, 64):
-        if DEPTH[n] != level:
-            continue
-        p = n
+    for n in range(first[depth], FIRST[depth + 1]):
+        p, slot = n, n - START[depth]
         for _ in range(up):
             p = PAR[p]
-        if out and out[-1][0] == p and out[-1][1] == n // 16:
+        if out and out[-1][0] == p and out[-1][1] == slot // 16:
             out[-1][3] += 1
         else:
-            out.append([p, n // 16, n % 16, 1])
+            out.append([p, slot // 16, slot % 16, 1])
     cut = []
-    for p, b, lo, ln in out:
+    for p, h, lo, ln in out:
         while ln:
             part = max(x for x in LENS if x <= ln)
-            cut.append((p, b, lo, part))
+            cut.append((p, h, lo, part))
             lo, ln = lo + part, ln - part
     return cut
 
 
-CYC, GATHER, SCATTER, PE_COL, PE_LAT, WAKE, ISSUE, HOP, ROW_NS, LINK, DMA0, HBM = 0.9, 1.5, 3.5, 0.45, 100, 180, 250, 1200, 30, 12.0, 2000, 200.0
+def pieces(vals):
+    out, j = [], 0
+    while j < len(vals):
+        n, step = 1, vals[j + 1] - vals[j] if j + 1 < len(vals) else 0
+        while j + n < len(vals) and n < 16 and vals[j + n] == vals[j] + n * step:
+            n += 1
+        out.append((j, vals[j], step if n > 1 else 0, n))
+        j += n
+    return out
 
 
-PASSES = 45
-SHAKE = 1000
-SLACK = 99999
-LOOSE = False
-PACE = (2, 2)
-EARLY = (1, 0)
+CYC, GATHER, SCATTER, PE_COL, PE_LAT, WAKE, ISSUE, HOP, ROW_NS, LINK, DMA0, HBM = 0.85, 1.5, 3.8, 0.43, 100, 190, 250, 750, 25, 20.0, 1500, 250.0
+PASSES = 2500
+STRETCH = 3000
+SHAKE = 1500
+CASES = ((1.0, 190, 0.8), (1.0, 190, 1.5), (1.3, 220, 1.0), (1.0, 130, 1.0))
 PLANS = {}
 
 
 def arrange(ops, sends):
     n = len(ops)
-    pre = []
-    for op in ops:
-        pre.append([sends[d[0]] if isinstance(d, tuple) else d for d in op["deps"]])
+    pre = [sorted(set(sends[d[0]] if isinstance(d, tuple) else d for d in op["deps"])) for op in ops]
     kept = [j for j in range(n) if ops[j]["e"] == "y"]
     kept = set((d, j) for d, j in zip(kept, kept[1:]) if d not in pre[j])
     for d, j in kept:
@@ -106,7 +111,7 @@ def arrange(ops, sends):
             succ[d].append(j)
 
     def lag(d, j):
-        if (ops[d]["e"] == "t" and ops[j]["e"] == "t") or (d, j) in kept or d in ops[j]["loose"]:
+        if (ops[d]["e"] == "t" and ops[j]["e"] == "t") or (d, j) in kept:
             return 0
         return ops[d]["lat"] + WAKE
 
@@ -119,50 +124,66 @@ def arrange(ops, sends):
             if not todo[k]:
                 stack.append(k)
     tail = [0.0] * n
-    for _ in range(NSTEP):
-        for j in reversed(order):
-            tail[j] = ops[j]["ns"] + max([lag(j, k) + tail[k] for k in succ[j]] + [tail[k] for k in ops[j].get("soon", ())] + [0])
+    for j in reversed(order):
+        tail[j] = ops[j]["ns"] + max([lag(j, k) + tail[k] for k in succ[j]] + [0])
     before = [[(d, lag(d, j)) for d in pre[j]] for j in range(n)]
     after = [[(k, lag(j, k)) for k in succ[j]] for j in range(n)]
-    for j in range(n):
-        for k in ops[j].get("soon", ()):
-            before[k].append((j, -SLACK))
-            after[j].append((k, -SLACK))
 
     def fill(turn, needs):
-        gaps = {e: [[0.0, 1e18]] for e in "vstgy"}
+        gaps = {e: [[0.0, 1e18]] for e in "vstgyw"}
         end = [0.0] * n
         for j in turn:
-            at, ns, room = max([end[d] + w for d, w in needs[j]] + [0.0]), ops[j]["ns"], gaps[ops[j]["e"]]
+            start, ns, room = max([end[d] + w for d, w in needs[j]] + [0.0]), ops[j]["ns"], gaps[ops[j]["e"]]
             i = len(room) - 1
-            while i and room[i - 1][1] >= at + ns:
+            while i and room[i - 1][1] >= start + ns:
                 i -= 1
-            while max(room[i][0], at) + ns > room[i][1]:
+            while max(room[i][0], start) + ns > room[i][1]:
                 i += 1
             lo, hi = room[i]
-            at = max(lo, at)
-            end[j] = at + ns
-            room[i:i + 1] = [x for x in ([lo, at], [at + ns, hi]) if x[1] - x[0] >= 30]
+            start = max(lo, start)
+            end[j] = start + ns
+            room[i:i + 1] = [x for x in ([lo, start], [start + ns, hi]) if x[1] - x[0] >= 6]
         return end
 
+    def replay(turn, ns, needs):
+        free, end = dict.fromkeys("vstgyw", 0.0), [0.0] * n
+        for j in turn:
+            start = free[ops[j]["e"]]
+            for d, w in needs[j]:
+                if end[d] + w > start:
+                    start = end[d] + w
+            end[j] = free[ops[j]["e"]] = start + ns[j]
+        return max(end)
+
     if n not in PLANS:
-        turn, best = sorted(range(n), key=lambda j: (-tail[j], j)), None
-        seed = 1
+        cases = []
+        for slow, wake, far in CASES:
+            ns = [op["ns"] * (slow if op["e"] in "vst" else far) for op in ops]
+            cases.append((ns, [[(d, w and (w + wake - WAKE + (far - 1) * HOP * (ops[d]["e"] == "w"))) for d, w in before[j]] for j in range(n)]))
+        back, best, seed = tail, None, 1
         for p in range(PASSES):
-            end = fill(turn, before)
-            if best is None or max(end) < best[0]:
-                best = (max(end), sorted(range(n), key=lambda j: (end[j] - ops[j]["ns"], j)), back if p else tail)
-            back = fill(sorted(range(n), key=lambda j: -end[j]), after)
-            if p % 3 == 2:
-                back = list(best[2])
-                for j in reversed(order):
+            end = fill(sorted(range(n), key=lambda j: -back[j]), before)
+            turn = sorted(range(n), key=lambda j: (end[j] - ops[j]["ns"], j))
+            total = sum(replay(turn, *case) for case in cases) / len(cases)
+            if best is None or total <= best[0]:
+                best = (total, turn, back)
+            if p % 4 == 0:
+                back = fill(sorted(range(n), key=lambda j: -end[j]), after)
+                continue
+            back = list(best[2])
+            seed = (seed * 1103515245 + 12345) % 2147483648
+            lo = seed / 2147483648 * best[0] - STRETCH / 2
+            for j in reversed(order):
+                if lo <= back[j] < lo + STRETCH:
                     seed = (seed * 1103515245 + 12345) % 2147483648
-                    back[j] = max([back[j] + (seed / 2147483648 - 0.5) * SHAKE] + [back[k] + 1 for k in succ[j]])
-            turn = sorted(range(n), key=lambda j: -back[j])
+                    back[j] += (seed / 2147483648 - 0.5) * SHAKE
+                for k in succ[j]:
+                    if back[j] <= back[k]:
+                        back[j] = back[k] + 1
         PLANS[n] = best
-    out = PLANS[n][1]
+    out = [j for j in PLANS[n][1] if ops[j]["e"] != "w"]
     new = {j: i for i, j in enumerate(out)}
-    return [dict(ops[j], deps=[d if isinstance(d, tuple) else new[d] for d in ops[j]["deps"] if d not in ops[j]["loose"]]) for j in out]
+    return [dict(ops[j], deps=[d if isinstance(d, tuple) else new[d] for d in ops[j]["deps"]]) for j in out]
 
 
 def emit(g, T, ops):
@@ -222,585 +243,559 @@ def emit(g, T, ops):
             ins.then_inc(T.sem[ENGINE_SEM[op["e"]]], 1)
 
 
+def at(name, lo=0, hi=None, step=1):
+    return (name, range(lo, SCRATCH[name][1][1] if hi is None else hi, step), None)
+
+
+def ind(win, off):
+    return (win[0], win[1], off)
+
+
 def rank_program(g, core, T, topo):
     rank = T.rank_of(core)
     if rank is None:
         return
     N = len(T.cores)
     vec, act, pe = g.vector, g.scalar, g.tensor
-    ops, last, readers, sent, sends, mark = [], {}, {}, [0], {}, []
+    ops, last, readers, sent, sends = [], {}, {}, [0], {}
 
-    def ind(win, off):
-        mark.append(1)
-        return win.indirect(off)
+    def ap(x):
+        if not isinstance(x, tuple):
+            return x
+        view = T[x[0]][:, x[1].start:x[1][-1] + 1:x[1].step]
+        return view if x[2] is None else view.indirect(ap(x[2]))
 
-    def took(out, fixed, each=1.0):
-        if mark:
-            each = GATHER * mark.pop()
-        return fixed + max(16, out.shape[1] * each) * CYC
+    def cells(x):
+        if isinstance(x, str):
+            return [x]
+        if x[0] in WHOLE or psum(x):
+            return [x[0]]
+        return [(x[0], c) for c in x[1]]
 
-    def add(e, fn, r=(), w=(), sem=None, remote=False, ns=100.0, lat=0.0):
-        banks = [key for key in w if key in BANKS and e != "t"]
-        w = [key for key in w if key not in banks]
-        r = list(r) + banks
-        deps = set()
-        for key in r:
-            if key in last:
-                deps.add(last[key])
-        for key in banks:
-            deps.update(j for j in readers.get(key, ()) if ops[j]["e"] != e)
-        for key in w:
-            if key in last:
-                deps.add(last[key])
-            deps.update(readers.get(key, ()))
+    def psum(x):
+        return SCRATCH[x[0]][0] == "psum"
+
+    def width(x):
+        return len(x[1]) if x[2] is None else 16 * len(x[2][1])
+
+    def add(e, fn, w, r, ns, lat=0.0, sem=None, remote=False):
+        r = [x for x in r if isinstance(x, (tuple, str))]
+        r += [x[2] for x in r + w if isinstance(x, tuple) and x[2] is not None]
+        rd = set(c for x in r for c in cells(x))
+        wr = set(c for x in w for c in cells(x))
+        deps = set(last[c] for c in rd | wr if c in last)
+        for c in wr:
+            deps.update(readers.get(c, ()))
+        for x in r:
+            if isinstance(x, tuple) and psum(x):
+                deps.update(j for j in readers.get(x[0], ()) if ops[j]["e"] != e)
         n = len(ops)
-        loose = [d for d in deps if LOOSE and e in "vs" and sem is None and not isinstance(d, tuple) and ops[d]["e"] == e
-                 and ops[d]["sem"] is None and d not in [last.get(key) for key in r]]
-        ops.append({"e": e, "fn": fn, "deps": deps, "sem": sem, "ns": ns, "lat": lat, "loose": loose})
-        for key in r:
-            if not remote:
-                readers.setdefault(key, []).append(n)
-        for key in w:
-            last[key] = n
-            readers[key] = []
+        ops.append({"e": e, "fn": fn, "deps": deps, "sem": sem, "ns": ns, "lat": lat})
+        if not remote:
+            for c in rd:
+                readers.setdefault(c, []).append(n)
+        for c in wr:
+            last[c] = n
+            readers[c] = []
 
-    def ts(out, in0, s1, s2, op0, op1, r, w):
-        if op1 is None:
-            add("v", lambda: vec.tensor_scalar(out, in0, s1, None, op0), r, w, ns=took(out, 50))
-        else:
-            add("v", lambda: vec.tensor_scalar(out, in0, s1, s2, op0, op1), r, w, ns=took(out, 50))
+    def took(fixed, out, ins, each=1.0):
+        if out[2] is not None:
+            return fixed + width(out) * SCATTER * CYC
+        if any(x[2] is not None for x in ins):
+            return fixed + width(out) * GATHER * CYC
+        if each == 1.0 and fixed == 50 and all(SCRATCH[x[0]][2] in (B, HF, U) for x in [out] + ins):
+            each = 0.5
+        return max(64 * CYC, fixed + width(out) * each * CYC)
 
-    def tt(out, a, b, op, r, w):
-        add("v", lambda: vec.tensor_tensor(out, a, b, op), r, w, ns=took(out, 50, 2.0))
+    def ts(out, a, s1, s2, op0, op1=None):
+        more = () if op1 is None else (op1,)
+        add("v", lambda: vec.tensor_scalar(ap(out), ap(a), ap(s1), ap(s2), op0, *more), [out], [a, s1, s2], took(50, out, [a]))
 
-    def cp(out, a, r, w):
-        add("v", lambda: vec.tensor_copy(out, a), r, w, ns=took(out, 50))
+    def tt(out, a, b, op):
+        add("v", lambda: vec.tensor_tensor(ap(out), ap(a), ap(b), op), [out], [a, b],
+            took(50, out, [a, b], 1.01 if psum(a) or psum(b) else 2.0))
 
-    def scan(out, a, b, init, op0, op1, r, w):
-        add("v", lambda: vec.tensor_tensor_scan(out, a, b, init, op0, op1), r, w, ns=took(out, 50))
+    def cp(out, a, more=()):
+        add("v", lambda: vec.tensor_copy(ap(out), ap(a)), [out], [a] + list(more), took(50, out, [a]))
 
-    def ms(out, val, w, r=()):
-        add("v", lambda: vec.memset(out, val), r, w, ns=took(out, 50))
+    def ms(out, val):
+        add("v", lambda: vec.memset(ap(out), val), [out], [], took(50, out, []))
 
-    def ac(out, a, func, bias, scale, r, w, acc=None):
+    def ac(out, a, func=AF.Identity, bias=0.0, scale=1.0, acc=None):
         if acc is None:
-            add("s", lambda: act.activation(out, a, func, bias=bias, scale=scale), r, w, ns=took(out, 65))
+            add("s", lambda: act.activation(ap(out), ap(a), func, bias=ap(bias), scale=ap(scale)), [out], [a, bias, scale], took(65, out, [a]))
         else:
-            add("s", lambda: act.activation(out, a, func, bias=bias, scale=scale, accum_out=acc), r, w, ns=took(out, 85))
+            add("s", lambda: act.activation(ap(out), ap(a), func, bias=ap(bias), scale=ap(scale), accum_out=ap(acc)),
+                [out, acc], [a, bias, scale], took(85, out, [a]))
 
-    def lin(out, a, scale, bias, r, w):
-        ac(out, a, AF.Identity, bias, scale, r, w)
+    def mm(out, lhsT, rhs, start=False, stop=False):
+        slow = 4 if SCRATCH[rhs[0]][2] == F else 1
+        add("t", lambda: pe.matmul(ap(out), ap(lhsT), ap(rhs), start, stop), [out], [lhsT, rhs], max(64, width(out)) * slow * PE_COL, PE_LAT)
 
-    def mm(bank, out, lhsT, rhs, start, stop, r):
-        add("t", lambda: pe.matmul(out, lhsT, rhs, start, stop), r, [bank], ns=max(64, out.shape[1]) * PE_COL, lat=PE_LAT)
+    def group(terms):
+        for n, (out, lhsT, rhs) in enumerate(terms):
+            mm(out, lhsT, rhs, n == 0, n == len(terms) - 1)
 
-    def iota(out, pattern, base, mult, w, r=(), whole=False):
-        if whole:
-            add("g", lambda: g.iota(out, pattern, base, mult), r, w, ns=took(out, 130, 2.0))
-        else:
-            add("g", lambda: g.iota(out, pattern, base, mult, allow_small_or_imprecise_dtypes=True), r, w, ns=took(out, 130, 2.0))
+    def iota(out, pattern, base, mult=0):
+        more = {} if SCRATCH[out[0]][2] == I else {"allow_small_or_imprecise_dtypes": True}
+        add("g", lambda: g.iota(ap(out), pattern, base, mult, **more), [out], [], 130 + 2 * width(out) * CYC)
 
-    def dma(e, out, a, sem, r, w, nbytes=0):
-        add(e, lambda: (g.sync if e == "y" else act).dma_start(out, a), r, w, sem, ns=50, lat=DMA0 + nbytes / HBM)
+    def keep(out, a, pattern, op, fill):
+        add("g", lambda: g.affine_select(ap(out), ap(a), pattern, op, fill, 0, 1), [out], [a], 170 + 2 * width(out) * CYC)
 
-    def send(to, out, a, sem, r, width):
+    def table(name, lo, vals):
+        for turn, (j, first, step, n) in enumerate(pieces(vals)):
+            out = at(name, lo + j, lo + j + n)
+            if turn % 3 == 2:
+                iota(out, [[step, n]], first)
+            elif step or turn % 3:
+                ac(out, at("i64", 0, n), bias=float(first), scale=float(step))
+            else:
+                ms(out, float(first))
+
+    def dma(e, out, a, sem, w, r, nbytes=0):
+        add(e, lambda: (g.sync if e == "y" else act).dma_start(out, a), w, r, 50, DMA0 + nbytes / HBM, sem)
+
+    def send(to, out, a, sem):
         dst = T.cores[to]
         rid, pid = topo.addr(dst, core)
         ways = len(topo.engines(core, dst))
         sent[0] += ways
+        nbytes = width(a) * (4 if SCRATCH[a[0]][2] == F else 2)
+        add("g", lambda: g.remote_dma(ap(out), ap(a), T.sem[sem], T.sem.sent, pid, rid, topo.mask(core, dst)), [], [a],
+            ISSUE, -WAKE, remote=True)
         sends[sem] = len(ops)
-        add("g", lambda: g.remote_dma(out, a, T.sem[sem], T.sem.sent, pid, rid, topo.mask(core, dst)), r, remote=True,
-            ns=ISSUE, lat=HOP + 128 / ways * (ROW_NS + width / LINK))
+        ops.append({"e": "w", "deps": {len(ops) - 1}, "ns": 128 / ways * (ROW_NS + nbytes / LINK), "lat": HOP})
 
-    def lands(key, sem, frm):
-        last[key] = (sem, len(topo.engines(T.cores[frm], core)))
+    def lands(place, sem, frm):
+        for c in cells(place):
+            last[c] = (sem, len(topo.engines(T.cores[frm], core)))
 
-    def verifier(t):
-        return (rank + 1 + t % (N - 1)) % N
+    def verifier(t, r=rank):
+        return (r + 1 + t % (N - 1)) % N
 
     def drafter(t):
         return (rank - 1 - t % (N - 1)) % N
 
-    for t in range(NSTEP):
-        lands("l_xt%d" % t, "a_xt%d" % t, drafter(t))
-        for a, b in PARTS:
-            for c in range(a, b):
-                lands("l_lt%d_%d" % (t, c), "a_lt%d_%d" % (t, a), drafter(t))
-        lands("l_ch%d" % t, "a_ch%d" % t, verifier(t))
-        for c in range(4):
-            if t < NSTEP - 1:
-                lands("l_e%d_%d" % (t, c), "a_e%d_%d" % (t, c), verifier(t))
-    for a, b in PARTS:
-        for c in range(a, b):
-            lands("l_kn%d" % c, "a_kn%d" % a, verifier(NSTEP - 1))
+    LAST = NSTEP - 1
+    CUT = 16 * STATES_LAST[-1][0]
 
-    col, cst, lst = T.col, T.cst, T.lst
-    ident = T.idw[:, 16:144]
-    C_I, C_0, C_N0, C_EV, C_OD, C_UC, C_KB, C_EB, C_S, C_Q, C_PM, C_IX, C_H8, C_MX, C_M4, C_NK, C_T = range(17)
-    C_T2, C_NB, C_K2 = 17, 20, 24
+    def tiles(t):
+        out, lo = [], LT * t
+        for c0, c1 in TILES if t < LAST else TILES_LAST:
+            out.append((c0, c1, lo))
+            lo += c1 - c0
+        return out
+
+    def tokens(t, c0, c1):
+        lo = [place - a for a, b, place in tiles(t) if a <= c0][-1 if c1 == 16 else 0 if c0 == 0 else 1]
+        return at("l_lt", lo + c0, lo + c1)
+
+    def back_parts(t):
+        return [(256 * t + 64 * a, 256 * t + 64 * b, "a_e%d_%d" % (t, a)) for a, b in BACK]
+
+    for t in range(NSTEP):
+        lands(at("l_x", 8 * t, 8 * t + 4), "a_x%d" % t, verifier(t - 1, drafter(t)) if t else drafter(0))
+        lands(at("l_ct", 48 * t, 48 * t + 48), "a_ct%d" % t, drafter(t))
+        for j, (c0, c1, lo) in enumerate(tiles(t)):
+            lands(at("l_lt", lo, lo + c1 - c0), "a_lt%d_%d" % (t, j), drafter(t))
+        if t < LAST:
+            lands(at("l_j", 4 * t, 4 * t + 4), "a_e%d_4" % t, verifier(t))
+            for lo, hi, sem in back_parts(t):
+                lands(at("l_e", lo, hi), sem, verifier(t))
+    lands(at("l_y", 0, CUT), "a_y0", verifier(LAST))
+    lands(at("l_y", CUT, 256), "a_y1", verifier(LAST))
+    lands(at("l_f"), "a_f", verifier(LAST))
+    lands(at("l_j", 12, 16), "a_r", verifier(LAST - 1, drafter(LAST)))
+
+    (C_I, C_0, C_TK, C_UC, C_UT, C_KB, C_S, C_Q, C_IX, C_NK, C_JK, C_T, C_EV, C_OD, C_PM) = range(15)
+    C_K2, C_MID, C_LOSE, C_PAD = 20, 24, 32, 36
+    K_A, K_S4, K_TH, K_PM, K_NC, K_R, K_DMK = 0, 20, 24, 40, 56, 76, 92
+    B_15, B_3, B_NC, B_S, B_SH, B_H = 0, 36, 56, 76, 80, 144
+    L_UC, L_CMP, L_PAR, L_REP, L_TH, L_PM = 0, 20, 24, 40, 44, 60
 
     def cc(j):
-        return col[:, j:j + 1]
+        return at("col", j, j + 1)
 
-    def run(lo, ln):
-        at = 160 * LENS.index(ln) + 15 - lo
-        return T.runs[:, at:at + 128]
+    def run(lo, ln, name="runs"):
+        first = (160 * LENS.index(ln) if name == "runs" else 0) + 15 - lo
+        return at(name, first, first + 128)
 
-    ones = run(0, 16)
-    K_JUNK, K_DMK, K_S4, K_A, K_B = 0, 16, 32, 40, 64
-    L_UC, L_PM, L_PAR, L_REP, L_DA, L_DB, L_DC, L_TH = 0, 20, 36, 52, 56, 58, 60, 64
+    def mat(name, j=0):
+        return at(name, 128 * j, 128 * j + 128)
 
-    ms(T.tk[:], 0, ["tk"])
-    dma("s", T.nx[:, 0:4], T.x0[:], "d_x", [], ["nx0x"])
-    dma("s", T.kp[:, 0:1], T.kap[:], "d_kp", [], ["kp"])
-    dma("y", T.tk[0:128:16, :], T.tok[:], "d_tk", [], ["tk"])
-    dma("y", T.q[:], T.qt[:], "d_q", [], ["q"], 128 * V * 4)
-    dma("y", T.k[:, 0:V], T.kt[:], "d_k", [], ["k"], 128 * V * 6)
-    dma("y", T.a[:, 0:V], T.qt[:], "d_a", ["q"], ["a"], 128 * V * 6)
+    ident, ones, negi, negq = at("idw", 16, 144), run(0, 16), mat("negi"), mat("negq")
 
-    iota(T.pi[:, 0:1], [[0, 1]], 0, 1, ["pi0"], whole=True)
-    iota(T.xp[:], [[1, 176]], -16, -1, ["xp"])
-    vals = [15] + list(range(15)) + [500] + ROW[17:46] + [500] * 16 + ROW[46:64]
-    ms(T.rowx[:], -7.0, ["rowx"])
-    ts(T.pi[:, 1:2], T.pi[:, 0:1], 15, None, OP.bitwise_and, None, ["pi0"], ["pi1"])
-    cp(cc(C_I), T.pi[:, 1:2], ["pi1"], ["c_i"])
-    ts(T.stp[:], T.xp[:], cc(C_I), 15.0, OP.add, OP.is_ge, ["xp", "c_i"], ["stp"])
-    ts(T.idw[:], T.xp[:, 0:160], 0.0, None, OP.is_equal, None, ["xp"], ["idw"])
-    ts(cc(C_0), cc(C_I), 0.0, None, OP.is_equal, None, ["c_i"], ["c_0"])
-    for j, ln in enumerate(LENS):
-        tt(T.runs[:, 160 * j:160 * j + 160], T.stp[:, 16:176], T.stp[:, 16 - ln:176 - ln], OP.subtract, ["stp"], ["run%d" % ln])
-    RUNS = ["run%d" % ln for ln in LENS]
-    ts(T.u[:, 320:324], T.tk[:], -float(H), cc(C_0), OP.add, OP.mult, ["tk", "c_0"], ["rd"])
-    mm("p0", T.p0[:, 0:4], ones, T.u[:, 320:324], True, True, ["rd", "run16"])
-    ts(T.nx[:, 4:8], T.p0[:, 0:4], float(H), None, OP.add, None, [], ["p0", "nx0t"])
-    ts(T.rt[:], T.p0[:, 0:4], float(H), None, OP.add, None, [], ["p0", "rt"])
-    j, pieces = 0, []
-    while j < 80:
-        n = 1
-        if j + 1 < 80 and vals[j + 1] - vals[j] in (0, 1) and vals[j] != 0:
-            while j + n < 80 and vals[j + n] - vals[j + n - 1] == vals[j + 1] - vals[j]:
-                n += 1
-        if vals[j] != 0:
-            key = "rowx%d" % j
-            pieces.append(key)
-            if n > 1 and vals[j + 1] != vals[j]:
-                iota(T.rowx[:, j:j + n], [[1, n]], vals[j] - 7, 0, [key], ["rowx"])
-            else:
-                ms(T.rowx[:, j:j + n], float(vals[j] - 7), [key], ["rowx"])
-        j += n
-    iota(cst[:, K_A:K_A + 20], [[16, 5], [0, 4]], 0, 0, ["k_a"])
-    iota(T.cidf[:], [[1, 192]], 8, 0, ["cidf"])
-    send(verifier(0), T.l_xt[:, 0:8], T.nx[:, 0:8], "a_xt0", ["nx0x", "nx0t"], 32)
-    ts(lst[:, L_UC:L_UC + 20], cst[:, K_A:K_A + 20], cc(C_I), None, OP.add, None, ["k_a", "c_i"], ["l_uc"])
-    lin(cc(C_UC), cc(C_I), -float(V), float(H + 7 * V), ["c_i"], ["c_uc"])
-    iota(T.zero[:, 0:40], [[0, 40]], 0, 0, ["zero"])
-    iota(T.zero[:, 40:256], [[0, 216]], 0, 0, ["zero2"])
-    ts(T.cu[:, 0:320], ind(T.rowx[:], lst[:, L_UC:L_UC + 20]), 144.0, float(H), OP.mult, OP.min, pieces + ["l_uc"], ["cu"])
-    ts(T.cu[:, 320:324], T.zero[:, 0:4], float(H), cc(C_0), OP.add, OP.mult, ["zero", "c_0"], ["curd"])
-    lin(T.uc[:], ind(T.rowx[:], lst[:, L_UC:L_UC + 20]), float(V), cc(C_UC), pieces + ["l_uc", "c_uc"], ["uc"])
-    lin(T.cidf[:, 0:64:16], T.cidf[:, 0:64:16], 1.0, 64.0, [], ["cidf"])
-    lin(T.cid[:], T.cidf[:], cc(C_0), 0.0, ["cidf", "c_0"], ["cid"])
+    ms(at("tk"), 0)
+    dma("s", T.xi[:], T.x0[:], "d_x", [at("xi")], [])
+    dma("s", T.kp[:, 0:1], T.kap[:], "d_kp", [at("kp", 0, 1)], [])
+    dma("y", T.tk[0:128:16, :], T.tok[:], "d_tk", [at("tk")], [])
+    dma("y", T.q[:], T.qt[:], "d_q", ["q"], [], 128 * V * 4)
+    dma("y", T.k[:], T.kt[:], "d_k", ["k"], [], 128 * V * 6)
+    dma("y", T.a[:, 0:V], T.qt[:], "d_a", ["a"], ["q"], 128 * V * 6)
+    send(verifier(0), at("l_x", 0, 4), at("xi"), "a_x0")
+    ops[-1]["lat"] += 5000
 
-    def node_cols(src, n):
-        return src[:, ucol(n):ucol(n) + 49:16]
+    iota(at("pi", 0, 1), [[0, 1]], 0, 1)
+    iota(at("i64"), [[0, 8], [1, 16]], 0)
+    iota(at("xq"), [[1, 160]], 0, -1)
+    ts(at("pi", 1, 2), at("pi", 0, 1), 15, None, OP.bitwise_and)
+    cp(cc(C_I), at("pi", 1, 2))
+    ts(at("idw"), at("xq"), 16.0, None, OP.is_equal)
+    ts(at("runs", 0, 160), at("xq"), cc(C_I), 15.0, OP.add, OP.is_equal)
+    for j, ln in enumerate(LENS[1:]):
+        ac(cc(C_MID + j), cc(C_I), bias=-15.0 - (ln - 1) / 2)
+        ac(at("ab", 160 * j, 160 * j + 160), at("xq"), AF.Abs, cc(C_MID + j))
+        ts(at("runs", 160 * j + 160, 160 * j + 320), at("ab", 160 * j, 160 * j + 160), ln / 2, None, OP.is_lt)
+    table("rowx", 0, ROW[1:17] + ROW[16:48] + ROW[40:64] + [0] * 8)
+    iota(at("cst", K_A, K_A + 4), [[0, 4]], 0)
+    iota(at("cst", K_A + 4, K_A + 20), [[32, 2], [0, 4], [16, 2]], 16)
+    ts(at("lst", L_UC, L_UC + 20), at("cst", K_A, K_A + 20), cc(C_I), None, OP.add)
+    ac(cc(C_UC), cc(C_I), bias=float(H), scale=-float(R))
+    ac(cc(C_UT), cc(C_I), bias=-float(H), scale=float(R))
+    rows = ind(at("rowx"), at("lst", L_UC, L_UC + 20))
+    ac(at("cu", 0, 320), rows, bias=-7.0 * 144, scale=144.0)
+    ac(at("uc"), rows, bias=cc(C_UC), scale=float(R))
+    ms(at("cu", 320, 384, 16), -7.0 * 144)
+    ms(at("zero"), 0.0)
+    ts(cc(C_0), cc(C_I), 0.0, None, OP.is_equal)
+    ts(cc(C_TK), cc(C_0), -2.0 * H, float(H), OP.mult, OP.add)
+    ts(at("u", 320, 384, 16), at("tk"), cc(C_TK), None, OP.add)
+    ms(at("hp"), float(H))
+    for d in (2, 3):
+        for h, (bound, op) in enumerate(((FIRST[d] - START[d], OP.is_lt), (FIRST[d + 1] - START[d] - 16, OP.is_ge))):
+            ts(cc(C_PAD + 2 * d + h), cc(C_I), float(bound), float(R), op, OP.mult)
+            half = at("hp", 8 * d + 4 + h, 8 * d + 12, 2)
+            ac(half, half, bias=cc(C_PAD + 2 * d + h))
 
-    def pe_parents(src, init, keys, level, up, at, bank="p1"):
-        first = 1 if level == 2 else 2
-        rr = runs_of(level, up)
-        mm(bank, T[bank][:, at:at + 8], ident, init[:, 16 + at:24 + at], True, False, keys[1:] + ["idw"])
-        for n, (p, b, lo, ln) in enumerate(rr):
-            o = at + 4 * (b - first)
-            mm(bank, T[bank][:, o:o + 4], run(lo, ln), node_cols(src, p), False, n == len(rr) - 1, keys + RUNS)
+    def node(src, n):
+        lo, step = UCOL[DEPTH[n]] + n - START[DEPTH[n]], USTEP[DEPTH[n]]
+        return at(src, lo, lo + 3 * step + 1, step)
 
-    def pe_tile(src, init, keys, level):
-        if level == 1:
-            mm("p0", T.p0[:, 0:8], ident, init[:, 0:8], True, False, keys[1:] + ["idw"])
-            mm("p4", T.p4[:, 8:16], ident, init[:, 8:16], True, False, keys[1:] + ["idw"])
-            mm("p0", T.p0[:, 0:4], run(0, 1), src[:, 320:324], False, False, keys[1:] + RUNS)
-        for bank, pair, closes in (("p0", (0, 1), 2), ("p4", (2, 3), 3)):
-            for i in range(16):
-                blocks = [b for b in pair if 16 * b + i > 0 and DEPTH[16 * b + i] == level]
-                if blocks:
-                    base = ucol(16 * blocks[0] + i)
-                    mm(bank, T[bank][:, 4 * blocks[0]:4 * blocks[-1] + 4], run(i, 1), src[:, base:base + 64 * len(blocks) - 15:16],
-                       False, level == closes and i == 15, keys + RUNS)
+    def pe_root(src, init):
+        group([(at("p0", 44, 48), ident, at(init, 44, 48)), (at("p0", 44, 48), ones, node(src, 0))])
 
-    def pe_row(src, inits, keys):
-        for n, init in enumerate(inits):
-            mm("p2", T.p2[:, 0:256], ident, init, n == 0, False, keys + ["idw"])
-        mm("p2", T.p2[:, 0:64:16], ones, src[:, 320:324], False, False, keys + RUNS)
-        for s in range(4):
-            mm("p2", T.p2[:, 16 * s + 1:16 * s + 16], ones, src[:, 16 * s + 1:16 * s + 16], False, False, keys)
-        mm("p2", T.p2[:, 64:128:16], ones, src[:, 0:64:16], False, False, keys)
-        mm("p2", T.p2[:, 64:192], ones, src[:, 64:192], False, False, keys)
-        mm("p2", T.p2[:, 128:256], ones, src[:, 192:320], False, True, keys)
+    def pe_parents(src, init, depth, up, lo):
+        group([(at("p0", lo, lo + 8), ident, at(init, lo, lo + 8))]
+              + [(at("p0", lo + h, lo + 8, 2), run(first, ln), node(src, p))
+                 for p, h, first, ln in runs_of(depth, up, FIRST if up > 1 else START)])
 
-    pe_parents(T.cid, T.zero, ["cid", "zero"], 2, 1, 0, "p7")
-    pe_parents(T.cid, T.zero, ["cid", "zero"], 3, 1, 8, "p7")
-    keys = ["cu", "curd", "zero"]
-    pe_parents(T.cu, T.zero, keys, 2, 1, 0)
-    pe_parents(T.cu, T.zero, keys, 3, 1, 8)
-    pe_parents(T.cu, T.zero, keys, 3, 2, 16)
-    for level in (1, 2, 3):
-        pe_tile(T.cu, T.zero, keys, level)
-    pe_row(T.cu, [T.zero[:]], keys + ["zero2"])
-    ac(T.ids[:, 0:16], T.p7[:, 0:16], AF.Identity, 0.0, 1.0, [], ["p7", "ids"])
-    ac(T.ctile[:, 0:8], T.p0[:, 0:8], AF.Identity, 0.0, 1.0, [], ["p0", "ctile"])
-    ac(T.ctile[:, 8:16], T.p4[:, 8:16], AF.Identity, 0.0, 1.0, [], ["p4", "ctile2"])
-    ac(T.crow[:], T.p2[:, 0:256], AF.Identity, 0.0, 1.0, [], ["p2", "crow"])
-    ts(T.ids[:, 16:32], T.ids[:, 0:16], 0.0, None, OP.is_equal, None, ["ids"], ["idz"])
-    tt(T.ctile[:, 16:32], T.p1[:, 0:16], T.ids[:, 16:32], OP.subtract, ["idz"], ["p1", "cpl"])
-    tt(T.ctile[:, 32:40], T.p1[:, 16:24], T.ids[:, 24:32], OP.subtract, ["idz"], ["p1", "cgp"])
-    lin(cc(C_MX), cc(C_0), float(V), 0.0, ["c_0"], ["c_mx"])
+    def pe_nodes(src, init):
+        group([(at("p0", 0, 20), ident, at(init, 0, 20))] + [(at("p0", 0, 20), run(i, 1), at(src, i, 320, 16)) for i in range(16)])
 
-    def later_constants():
-        iota(T.i64[:], [[0, 8], [1, 16]], 0, 0, ["i64"])
-        iota(cst[:, K_S4:K_S4 + 4], [[1, 4]], 0, 0, ["k_s4"])
-        iota(cst[:, K_JUNK:K_JUNK + 16], [[0, 4], [16, 4]], V, 0, ["k_junk"])
-        iota(cst[:, K_B:K_B + 16], [[64, 4], [4, 4]], 0, 0, ["k_b"])
-        iota(cst[:, K_DMK:K_DMK + 12], [[0, 3], [1, 4]], 0, 0, ["k_dmk"])
-        iota(T.fmi[:], [[-1, 128]], 128, 1, ["fmi"], whole=True)
-        iota(T.priof[:], [[0, 4], [1, 4], [4, 16]], 0, 0, ["priof"])
-        iota(T.k[:, V:V + 16], [[0, 16]], 0, 0, ["kz"])
-        ts(T.diag[:], T.i64[:, 0:64], cc(C_I), None, OP.is_equal, None, ["i64", "c_i"], ["diag"])
-        ts(T.rst[:], T.i64[:], 0.0, None, OP.not_equal, None, ["i64"], ["rst"])
-        lin(T.tie[:], T.i64[:], -4096.0, 15 * 4096.0, ["i64"], ["tie"])
-        lin(T.onew[:], ones, 65536.0, 0.0, RUNS, ["onew"])
-        cp(lst[:, L_REP:L_REP + 4], cst[:, K_S4:K_S4 + 4], ["k_s4"], ["l_rep"])
-        lin(cc(C_NK), T.kp[:, 0:1], -1.0, 0.0, ["kp"], ["c_nk"])
-        yield
-        ts(T.fmi[:], T.fmi[:], 15, None, OP.bitwise_and, None, [], ["fmi"])
-        ts(T.pi[:, 2:3], T.pi[:, 0:1], 4, 1, OP.logical_shift_right, OP.bitwise_and, ["pi0"], ["pi2"])
-        ts(T.pi[:, 3:4], T.pi[:, 0:1], 3, None, OP.bitwise_and, None, ["pi0"], ["pi3"])
-        ts(T.pi[:, 4:5], T.pi[:, 1:2], 2, None, OP.logical_shift_right, None, ["pi1"], ["pi4"])
-        lin(T.negi[:], ident, -1.0, 0.0, ["idw"], ["negi"])
-        tt(T.fm[:], T.fmi[:], ones, OP.mult, ["fmi"] + RUNS, ["fm"])
-        cp(cc(C_OD), T.pi[:, 2:3], ["pi2"], ["c_od"])
-        cp(cc(C_S), T.pi[:, 3:4], ["pi3"], ["c_s"])
-        cp(cc(C_Q), T.pi[:, 4:5], ["pi4"], ["c_q"])
-        for d in range(1, 16):
-            ts(T.shf[:, 128 * (d - 1):128 * d], T.fm[:], float(d), None, OP.is_equal, None, ["fm"], ["shf%d" % d])
-            bank = "p%d" % (3 + (d - 1) // 4)
-            o = 128 * ((d - 1) % 4)
-            mm(bank, T[bank][:, o:o + 128], ident, T.shf[:, 128 * (d - 1):128 * d], True, False, ["shf%d" % d, "idw"])
-            mm(bank, T[bank][:, o:o + 128], ident, T.negi[:], False, True, ["negi"])
-            if d % 4 == 0 or d == 15:
-                lo = 128 * 4 * ((d - 1) // 4)
-                ac(T.dm[:, lo:128 * d], T[bank][:, 0:128 * d - lo], AF.Identity, 0.0, 1.0 if d <= 8 else -float(H), [], [bank, "dm%d" % d])
-        yield
-        ac(T.bigi[:], ident, AF.Identity, 0.0, float(H), ["idw"], ["bigi"])
-        ac(T.prio[:], T.priof[:], AF.Identity, 0.0, 1.0 / 128, ["priof"], ["prio"])
-        lin(cc(C_EV), cc(C_OD), -1.0, 1.0, ["c_od"], ["c_ev"])
-        lin(T.ido[:], T.idw[:], cc(C_OD), 0.0, ["idw", "c_od"], ["ido"])
-        lin(cc(C_PM), cc(C_S), 16.0, cc(C_Q), ["c_s", "c_q"], ["c_pm"])
-        lin(T.ide[:], T.idw[:], cc(C_EV), 0.0, ["idw", "c_ev"], ["ide"])
-        lin(cc(C_M4), cc(C_0), -4.0, 4.0, ["c_0"], ["c_m4"])
-        ts(lst[:, L_PM:L_PM + 16], cst[:, K_B:K_B + 16], cc(C_PM), None, OP.add, None, ["k_b", "c_pm"], ["l_pm"])
-        ts(T.ids[:, 32:36], cst[:, K_S4:K_S4 + 4], 4.0, cc(C_0), OP.add, OP.mult, ["k_s4", "c_0"], ["ida"])
-        ts(lst[:, L_PAR:L_PAR + 4], cst[:, K_S4:K_S4 + 4], cc(C_M4), None, OP.add, None, ["k_s4", "c_m4"], ["l_par0"])
-        tt(T.ids[:, 8:12], T.ids[:, 8:12], T.ids[:, 4:8], OP.add, [], ["ids"])
-        tt(T.ids[:, 4:8], T.ids[:, 0:4], T.ids[:, 32:36], OP.add, ["ida"], ["ids"])
-        lin(cc(C_KB), cc(C_I), -1.0, -128.0, ["c_i"], ["c_kb"])
-        cp(lst[:, L_PAR + 4:L_PAR + 16], T.ids[:, 4:16], ["ids"], ["l_par1"])
-        lin(cc(C_EB), cc(C_I), -float(V), 7.5 * V + H, ["c_i"], ["c_eb"])
-        yield
-        lin(cc(C_T), cc(C_I), -4.0 / 128, 32.0 / 128, ["c_i"], ["c_t"])
-        lin(cst[:, K_JUNK:K_JUNK + 16], cst[:, K_JUNK:K_JUNK + 16], 1.0, cc(C_I), ["c_i"], ["k_junk"])
-        ts(lst[:, L_TH:L_TH + 16], cst[:, K_JUNK:K_JUNK + 16], -float(V), None, OP.add, None, ["k_junk"], ["l_th"])
-        iota(T.nbc[:], [[0, 4], [1, 4]], 0, 0, ["c_nb"])
-        lin(T.nbc[:], T.nbc[:], -1.0 / 128, cc(C_T), ["c_t"], ["c_nb"])
-        iota(T.ts[:, 0:4], [[0, 4]], 0, 0, ["tspad"])
-        iota(T.a[:, V:V + 64], [[0, 64]], 0, 0, ["az"], whole=True)
-        ts(cst[:, K_DMK:K_DMK + 12], cst[:, K_DMK:K_DMK + 12], cc(C_S), 4.0, OP.is_equal, OP.mult, ["c_s"], ["k_dmk"])
-        lin(cc(C_N0), cc(C_0), -1.0, 1.0, ["c_0"], ["c_n0"])
-        ts(cc(C_H8), cc(C_I), 8.0, -4.0, OP.is_lt, OP.mult, ["c_i"], ["c_h8"])
-        ts(cc(C_IX), cc(C_Q), 1.0, 16.0, OP.is_equal, OP.mult, ["c_q"], ["c_ix"])
-        lin(T.one0[:], ones, cc(C_0), 0.0, RUNS + ["c_0"], ["one0"])
-        lin(T.one1[:], ones, cc(C_N0), 0.0, RUNS + ["c_n0"], ["one1"])
-        cp(lst[:, L_DA:L_DA + 1], cc(C_S), ["c_s"], ["l_da"])
-        ts(lst[:, L_DB:L_DB + 1], cc(C_S), 4.0, None, OP.add, None, ["c_s"], ["l_db"])
-        ts(lst[:, L_DC:L_DC + 1], cc(C_H8), -2.0, cc(C_S), OP.mult, OP.add, ["c_s", "c_h8"], ["l_dc0"])
-        ts(lst[:, L_DC + 1:L_DC + 2], cc(C_H8), -1.0, cc(C_S), OP.mult, OP.add, ["c_s", "c_h8"], ["l_dc1"])
-        tt(cc(C_IX), cc(C_IX), cc(C_S), OP.add, ["c_s"], ["c_ix"])
-        yield
+    def pe_tile(c0, c1, level):
+        terms = [(at("p1", c0, c1), ident, at("ct1", c0, c1))]
+        terms += [(at("p1", 0, 1), run(s, 1), at("u", UCOL[0] + 16 * s, UCOL[0] + 16 * s + 1)) for s in range(0 if c0 else 4)]
+        for r in range(4):
+            first = c0 if c0 or r else 1
+            for s in range(4):
+                lo = UCOL[level] + s * USTEP[level] + 4 * first + r - START[level]
+                terms.append((at("p1", first, c1), run(4 * r + s, 1), at("u", lo, lo + 4 * (c1 - first) - 3, 4)))
+        group(terms)
 
-    def last_constants():
-        ms(T.sc[:, 64:192], 4.0, ["sc"])
-        ms(T.sc[:, 192:256], 8.0, ["sc2"])
-        ms(T.sc[:, 0:64], 2.0, ["sc3"])
-        ms(T.isc[:, 0:4], 1.0, ["is0"])
-        ms(T.isc[:, 4:68], 0.5, ["is1"])
-        ms(T.isc[:, 68:184], 0.25, ["is2"])
-        ms(T.isc[:, 184:256], 0.125, ["is3"])
-        ms(T.sc[:, 64:128:16], 2.0, ["sca"], ["sc"])
-        ms(T.sc[:, 128 + 14:192:16], 8.0, ["scb"], ["sc"])
-        ms(T.sc[:, 128 + 15:192:16], 8.0, ["scc"], ["sc"])
-        if SHARE:
-            lin(T.runh[:], T.runs[:, 0:160], 0.5, 0.0, RUNS, ["runh"])
-            lin(T.negf[:], ident, -1.0, 0.0, ["idw"], ["negf"])
-            for c in range(4):
-                cp(cc(C_K2 + c), cc(C_KB), ["c_kb"], ["c_k2%d" % c])
-                for kq in range(4):
-                    if (c, kq) in SHARE:
-                        ts(cc(C_T2), cc(C_Q), float(kq), 128.0, OP.is_equal, OP.mult, ["c_q"], ["c_t2"])
-                        tt(cc(C_K2 + c), cc(C_K2 + c), cc(C_T2), OP.add, ["c_t2"], ["c_k2%d" % c])
+    pe_root("cu", "zero")
+    pe_parents("cu", "zero", 2, 1, 20)
+    pe_parents("cu", "zero", 3, 1, 28)
+    pe_parents("cu", "zero", 3, 2, 36)
+    pe_nodes("cu", "zero")
+    ac(at("ct0"), at("p0", 0, 48))
+    ms(at("rows", 64, 65), -7.0 * 144)
+    for d, (lo, hi) in enumerate(zip(START[1:], START[2:] + (64,))):
+        ac(at("rows", 64 + lo, 64 + hi), at("rowx", (0, 16, 48)[d], (0, 16, 48)[d] + hi - lo), bias=-7.0 * 144, scale=144.0)
+    group([(at("p1", 0, 16), run(4 * r, 4), at("rows", 64 + r, 128, 4)) for r in range(4)])
+    ac(at("ct1"), at("p1", 0, 16))
+
+    ts(at("pi", 3, 4), at("pi", 0, 1), 3, None, OP.bitwise_and)
+    ts(at("pi", 4, 5), at("pi", 1, 2), 2, None, OP.logical_shift_right)
+    cp(cc(C_S), at("pi", 3, 4))
+    cp(cc(C_Q), at("pi", 4, 5))
+    iota(at("cst", K_TH, K_TH + 16), [[0, 4], [16, 4]], 0)
+    ts(at("lst", L_TH, L_TH + 16), at("cst", K_TH, K_TH + 16), cc(C_I), None, OP.add)
+    table("rows", 0, PAR)
+    group([(at("p2", 0, 16), run(4 * r, 4), at("rows", r, 64, 4)) for r in range(4)])
+    ts(at("lst", L_PAR, L_PAR + 16), at("p2", 0, 16), 0.25, cc(C_S), OP.mult, OP.add)
+    iota(at("rows", 128, 132), [[1, 4]], 0)
+    iota(at("rows", 132, 148), [[4, 2], [1, 4], [0, 2]], 4)
+    iota(at("rows", 148, 164), [[4, 2], [1, 4], [0, 2]], 0)
+    iota(at("rows", 164, 176), [[1, 6], [0, 2]], 0)
+    group([(at("p7", 0, 3), run(i, 1), at("rows", 128 + i, 176, 16)) for i in range(16)])
+    ts(at("lst", L_CMP, L_CMP + 3), at("p7", 0, 3), 1.0 / 16, None, OP.mult)
+    ts(at("pi", 2, 3), at("pi", 0, 1), 4, 1, OP.logical_shift_right, OP.bitwise_and)
+    cp(cc(C_OD), at("pi", 2, 3))
+    ac(cc(C_EV), cc(C_OD), bias=1.0, scale=-1.0)
+    ac(at("ide"), at("idw"), scale=cc(C_EV))
+    ac(at("ido"), at("idw"), scale=cc(C_OD))
+    ac(cc(C_PM), cc(C_S), bias=cc(C_Q), scale=16.0)
+    iota(at("cst", K_PM, K_PM + 16), [[64, 4], [4, 4]], 0)
+    ts(at("lst", L_PM, L_PM + 16), at("cst", K_PM, K_PM + 16), cc(C_PM), None, OP.add)
+    ac(cc(C_NK), at("kp", 0, 1), scale=-1.0)
+    iota(at("fmi"), [[-1, 128]], 128, 1)
+    ts(at("fmi"), at("fmi"), 15, None, OP.bitwise_and)
+    ts(at("fm", 128, 256), at("fmi"), 1.0, None, OP.add)
+    tt(mat("fm"), at("fm", 128, 256), ones, OP.mult)
+    ac(negi, ident, scale=-1.0)
+    ac(negq, ident, scale=-2.0 / R)
+    for d in range(1, 16):
+        ts(mat("shf", d - 1), mat("fm"), d + 1.0, None, OP.is_equal)
+        bank, o = "p%d" % (3 + (d - 1) // 4), 128 * ((d - 1) % 4)
+        group([(at(bank, o, o + 128), ident, mat("shf", d - 1)), (at(bank, o, o + 128), ident, negi)])
+        if d % 4 == 0 or d == 15:
+            ac(at("dm", 128 * d - o - 128, 128 * d), at(bank, 0, o + 128))
+    ac(cc(C_KB), cc(C_I), bias=-128.0, scale=-1.0)
+    ac(at("runh"), at("runs", 0, 160), scale=0.5)
+    ac(mat("negf"), ident, scale=-1.0)
+    for c in range(4):
+        mine = [kq for b, kq in SHARE if b == c]
+        for j, kq in enumerate(mine):
+            ts(cc(C_T), cc(C_Q), float(kq), 128.0, OP.is_equal, OP.mult)
+            tt(cc(C_K2 + c), cc(C_K2 + c if j else C_KB), cc(C_T), OP.add)
+    ms(at("cb", B_SH, B_SH + 64), -15.0)
+    iota(at("cst", K_R, K_R + 8), [[-1, 8]], 15)
+    ts(at("cst", K_R + 8, K_R + 16), at("cst", K_R, K_R + 8), cc(C_I), None, OP.is_le)
+    tt(at("cst", K_R + 8, K_R + 16), at("cst", K_R + 8, K_R + 16), at("cst", K_R, K_R + 8), OP.mult)
+    ts(at("col", C_LOSE, C_LOSE + 8), at("cst", K_R + 8, K_R + 16), 1.0, None, OP.add)
+    for d in range(8):
+        ts(mat("lose", d), mat("fm"), cc(C_LOSE + d), float(R), OP.is_equal, OP.mult)
+    ac(cc(C_JK), cc(C_I), bias=float(V))
+    add("g", lambda: g.iota(T.a[:, V:V + 16], [[0, 16]], 0, 0), ["az"], [], 160)
+    ac(mat("onew"), ones, scale=65536.0)
+    ac(mat("negw"), ident, scale=-131072.0)
+    keep(mat("upper"), ones, [[-1, 128]], OP.is_gt, 0.0)
+    ms(at("cb", B_15, B_15 + 20), 15.0 * H)
+    ms(at("cb", B_3, B_3 + 12), 0.0)
+    ms(at("cb", B_3 + 12, B_3 + 20), 15.0 * H)
+    ac(mat("neg2"), ident, scale=-2.0)
+    iota(at("cst", K_NC, K_NC + 4), [[0, 4]], START[1])
+    iota(at("cst", K_NC + 4, K_NC + 20), [[START[3] - START[2], 2], [0, 4], [16, 2]], START[2])
+    ts(at("cst", K_NC, K_NC + 20), at("cst", K_NC, K_NC + 20), cc(C_I), -1.0 / 256, OP.add, OP.mult)
+    ac(at("cb", B_NC, B_NC + 20), at("cst", K_NC, K_NC + 20), bias=1.0)
+    iota(at("cst", K_S4, K_S4 + 4), [[1, 4]], 0)
+    ac(at("cb", B_S, B_S + 4), at("cst", K_S4, K_S4 + 4), scale=0.25)
+    iota(at("cst", K_DMK, K_DMK + 12), [[0, 3], [1, 4]], 0)
+    ts(at("diag"), at("i64", 0, 64), cc(C_I), None, OP.is_equal)
+    ts(at("rst"), at("i64"), 0.0, None, OP.not_equal)
+    ac(at("tie"), at("i64"), bias=15.0 * 4096, scale=-4096.0)
+    cp(at("lst", L_REP, L_REP + 4), at("cst", K_S4, K_S4 + 4))
+    ts(at("cst", K_DMK, K_DMK + 12), at("cst", K_DMK, K_DMK + 12), cc(C_S), None, OP.is_equal)
+    ts(cc(C_IX), cc(C_Q), 1.0, 16.0, OP.is_equal, OP.mult)
+    tt(cc(C_IX), cc(C_IX), cc(C_S), OP.add)
+
+    def top_of(out, entries, places):
+        ts(out, ind(entries, places), cc(C_UT), float(H), OP.add, OP.min)
+
+    def root(t):
+        if t:
+            top_of(at("u", 320, 384), at("l_e", 256 * t - 256, 256 * t), at("l_j", 4 * t - 4, 4 * t))
+        pe_root("u", "ct0")
+        cp(at("rt"), at("p0", 44, 48))
+        if t:
+            ac(at("ytb", 4 * t - 4, 4 * t), at("p0", 44, 48))
 
     def draft(t):
-        win, wk = (T.q[:], ["q"]) if t == 0 else (T.a[:, 0:V], ["a"])
-        for level, (lo, hi) in enumerate(((0, 64), (64, 192), (192, 320))):
-            tile = T.rt[:] if level == 0 else T.pl[:, 8 * level - 8:8 * level]
-            tk = "rt" if level == 0 else "pl%d" % level
-            tt(T.w[:, lo:hi], ind(win, tile), T.uc[:, lo:hi], OP.subtract, wk + [tk, "uc"], ["w%d" % level])
-            ts(T.u[:, lo:hi], T.w[:, lo:hi], -float(H), float(H), OP.max, OP.min, ["w%d" % level], ["u%d" % level])
+        win = at("a", 0, V) if t else at("q")
+        for level, (c0, c1, place) in enumerate(tiles(t)):
+            lo, hi = UCOL[level + 1], UCOL[level + 1] + 4 * USTEP[level + 1]
+            tile = at("pl", 8 * level - 8, 8 * level) if level else at("rt")
+            tt(at("w", lo, hi), ind(win, tile), at("uc", lo, hi), OP.subtract)
+            ts(at("u", lo, hi), at("w", lo, hi), -float(H), float(H), OP.max, OP.min)
             if level < 2:
-                pe_parents(T.u, T.ctile, ["u%d" % level, "cpl"], level + 2, 1, 8 * level)
-            pe_tile(T.u, T.ctile, ["u%d" % level, "ctile", "ctile2", "rd"], level + 1)
-            if level < 2:
-                cp(T.pl[:, 8 * level:8 * level + 8], T.p1[:, 8 * level:8 * level + 8], [], ["p1", "pl%d" % (level + 1)])
-            for a, b in PARTS:
-                if max(DEPTH[16 * b - 16:16 * b]) == level + 1:
-                    lo, hi = 24 * t + 4 + 4 * a, 24 * t + 4 + 4 * b
-                    bank = "p4" if a else "p0"
-                    cp(T.ls[:, lo:hi], T[bank][:, 4 * a:4 * b], [], [bank, "lsa%d" % a])
-                    if a == 0:
-                        lo -= 4
-                        ts(T.ls[:, lo:lo + 4], T.p0[:, 0:4], cc(C_MX), None, OP.max, None, ["c_mx"], ["p0", "lsb"])
-                    send(verifier(t), T.l_lt[:, lo:hi], T.ls[:, lo:hi], "a_lt%d_%d" % (t, a), ["lsa%d" % a, "lsb"], 2 * (hi - lo))
-
-    def after_draft(t):
-        pe_parents(T.u, T.ctile, ["u0", "cgp"], 3, 2, 16)
-        ac(T.ts[:, 4:12], T.p0[:, 0:8], AF.Identity, 0.0, 1.0, [], ["p0", "tsl", "tsk"])
-        ac(T.ts[:, 12:20], T.p4[:, 8:16], AF.Identity, 0.0, 1.0, ["tsk"], ["p4", "tsl"])
-        if t < NSTEP - 1:
-            pe_row(T.u, [T.crow[:], T.prio[:]], ["u0", "u1", "u2", "rd", "crow", "prio"])
-        ac(T.ts[:, 20:44], T.p1[:, 0:24], AF.Identity, 0.0, 1.0, [], ["p1", "tsp"])
-        if t < NSTEP - 1:
-            tt(T.nb[:], T.nbc[:], T.ts[:, 4:20], OP.subtract, ["tsl", "c_nb"], ["nb"])
+                pe_parents("u", "ct0", level + 2, 1, 20 + 8 * level)
+                cp(at("pl", 8 * level, 8 * level + 8), at("p0", 20 + 8 * level, 28 + 8 * level))
+            pe_tile(c0, c1, level + 1)
+            cp(at("ls", place, place + c1 - c0), at("p1", c0, c1))
+            send(verifier(t), at("l_lt", place, place + c1 - c0), at("ls", place, place + c1 - c0), "a_lt%d_%d" % (t, level))
+        pe_parents("u", "ct0", 3, 2, 36)
+        pe_nodes("u", "ct0")
+        tt(at("cts", 48 * t, 48 * t + 48), at("p0", 0, 48), at("hp"), OP.subtract)
+        send(verifier(t), at("l_ct", 48 * t, 48 * t + 48), at("cts", 48 * t, 48 * t + 48), "a_ct%d" % t)
 
     def twins():
+        ts(at("t16"), at("p1", 0, 16), -float(H), None, OP.add)
+        for d in range(8):
+            mm(at("p1", 16 + 16 * d, 32 + 16 * d), mat("dm", d), at("t16"), True, True)
+        ts(at("eq"), at("p1", 16, 144), 0.0, None, OP.is_equal)
+        out = at("p1", 144, 160)
+        group([(out, ident, at("t16"))] + [(out, mat("lose", d), at("eq", 16 * d, 16 * d + 16)) for d in range(8)])
+        ts(at("off", 0, 32, 2), out, float(H), cc(C_JK), OP.add, OP.min)
+
+    def overwrite(t):
         for c in range(16):
-            b = c // 4
-            at = 256 * (c % 4) + 64 * b
-            ac(T.ab[:, at:at + 64], T.p2[:, 64 * b:64 * b + 64], AF.Abs, T.nb[:, c:c + 1], 1.0, ["nb"], ["p2", "ab%d" % c])
-        for h in range(2):
-            ac(T.dump[:, 512 * h:512 * h + 512], T.ab[:, 512 * h:512 * h + 512], AF.Relu, 131072.0, -4096.0 * 128,
-               ["ab%d" % c for c in range(16) if c % 4 // 2 == h], ["near%d" % h])
-        for s in range(4):
-            for i in range(16):
-                mm("p2", T.p2[:, 256:272], run(i, 1), T.dump[:, 256 * s + i:256 * s + 256:16], s + i == 0, s + i == 18, ["near%d" % (s // 2)])
+            cp(ind(at("a"), at("off", 2 * c, 2 * c + 1)), at("l_e", 256 * t + 16 * c, 256 * t + 16 * c + 16), ["az"])
 
-    def places():
-        tt(T.o1[:, 0:16], T.p2[:, 256:272], cst[:, K_JUNK:K_JUNK + 16], OP.min, ["k_junk"], ["p2", "o1"])
-        tt(T.o1[:, 16:32], T.o1[:, 0:16], T.ts[:, 4:20], OP.max, ["o1", "tsl"], ["o2"])
-        cp(T.off[:], T.o1[:, 16:32], ["o2"], ["off"])
+    def block(name, b, base=0):
+        return at(name, base + 64 * b, base + 64 * b + 64)
 
-    def overwrite(t, c):
-        o = 256 * t + 64 * c
-        add("v", lambda: vec.tensor_copy(T.a[:].indirect(T.off[:, 4 * c:4 * c + 4]), T.l_e[:, o:o + 64]),
-            ["off", "l_e%d_%d" % (t, c), "az"], ["a"], ns=50 + 64 * SCATTER * CYC)
+    def cols(name, c0, c1, base=0):
+        return at(name, base + 16 * c0, base + 16 * c1)
+
+    def states(t):
+        for c0, c1 in BLOCKS if t < LAST else STATES_LAST:
+            known = max(PAR[4 * c0:4 * c1])
+            win = at("x", 0, 4 * known + 4) if c0 else at("l_x", 8 * t, 8 * t + 4)
+            ac(cols("ph", c0, c1), ind(win, at("lst", L_PAR + c0, L_PAR + c1)), scale=0.5)
+            tt(cols("x", c0, c1), ind(at("k"), tokens(t, c0, c1)), cols("ph", c0, c1), OP.add)
+            if c0 == 0:
+                ac(at("x", 0, 4), at("l_x", 8 * t, 8 * t + 4))
+            if t < LAST:
+                ac(at("th", 64 * c0, 64 * c1), ind(cols("x", c0, c1), at("lst", L_TH, L_TH + 16)), bias=cc(C_NK))
+
+    def prepare(t):
+        done = 0
+        for c0, c1, _ in tiles(t):
+            ts(cols("cd", c0, c1), ind(at("q"), tokens(t, c0, c1)), -float(H), None, OP.add)
+            for c in range(c0, c1, 2):
+                for h, src in enumerate(("ide", "ido")):
+                    group([(cols("p2", c + h, c + h + 1), at(src, 16 + 16 * (h - to), 144 + 16 * (h - to)), cols("cd", c + to, c + to + 1))
+                           for to in range(2)])
+            out, a = cols("tr", c0, c1), cols("p2", c0, c1)
+            add("v", lambda out=out, a=a: vec.transpose(ap(out), ap(a)), [out], [a], took(50, out, [a]))
+            end = c1 // 4 * 4
+            ts(cols("ct", done, end), ind(cols("tr", 0, end), at("lst", L_PM + done, L_PM + end)), float(H), None, OP.add)
+            done = end
+
+    def votes(b, kq):
+        o, bank = 1024 * (b % 2) + 256 * kq, "p%d" % (3 + b % 2)
+        numbers, th = ind(at("k"), at("ct", 64 * b + 16 * kq, 64 * b + 16 * kq + 16)), at("th", 256 * b, 256 * b + 256)
+        if (b, kq) in SHARE:
+            kc = at("kc", 256 * (kq % 2), 256 * (kq % 2) + 256)
+            ac(kc, numbers)
+            group([(at("p0", 256, 512), mat("negf"), th), (at("p0", 256, 512), ident, kc)])
+            ac(at("ge", o, o + 256), at("p0", 256, 512), AF.Sign, 2.0 ** -100)
+        else:
+            tt(at("ge", o, o + 256), numbers, th, OP.is_ge)
+        for kk in range(4):
+            k = 4 * kq + kk
+            mm(at(bank, 0, 64), run(k, 1, "runh" if (b, kq) in SHARE else "runs"), at("ge", o + 64 * kk, o + 64 * kk + 64), k == 0, k == 15)
+
+    def ranks(t, b):
+        key, so = block("key", b), 512 * (b % 2)
+        ac(key, at("p%d" % (3 + b % 2), 0, 64), bias=cc(C_K2 + b if any(c == b for c, _ in SHARE) else C_KB), scale=16.0)
+        for bank, lo, hi in [("p5", 0, 4), ("p6", 4, 8)] if b == 3 else [("p%d" % (5 + b % 2), 0, 8)]:
+            for d in range(lo, hi):
+                mm(at(bank, 64 * (d - lo), 64 * (d - lo + 1)), mat("dm", d), key, True, True)
+            if lo:
+                ts(at("sg", so + 64 * lo, so + 64 * hi), at(bank, 0, 64 * (hi - lo)), -1.0, 1.0, OP.max, OP.min)
+            else:
+                ac(at("sg", so + 64 * lo, so + 64 * hi), at(bank, 0, 64 * (hi - lo)), AF.Sign)
+        bank, base = ("p2", 256) if b % 2 else ("p7", 0)
+        out = block(bank, b, base)
+        group([(out, negq, block("cd", b)), (out, ident, at("cb", B_SH, B_SH + 64))]
+              + [(out, mat("dm", 14 - d) if d < 7 else negi, at("sg", so + 64 * d, so + 64 * d + 64)) for d in range(8)])
+        for name, nodes, scale in (("utb", PAR, -1.0), ("uta", [PAR[n] for n in PAR], -float(R))):
+            inner = [4 * n for n in nodes if n // 16 == b]
+            if inner:
+                lo, hi = min(inner), max(inner) + 4
+                ts(at(name, lo, hi), at(bank, base + lo, base + hi), -2.0 * H / R, scale, OP.max, OP.mult)
+        ac(block("es", b, 256 * t), out, bias=cc(C_UC), scale=-R / 2.0)
 
     def commit(t):
-        tw, ch = T.l_ch[:, 32 * t + 16:32 * t + 32], "l_ch%d" % t
-        tt(T.m[:, 48:64], ind(tw, lst[:, L_DA:L_DA + 1]), T.ts[:, 4:20], OP.is_equal, [ch, "tsl", "l_da"], ["ma"])
-        tt(T.m[:, 0:16], ind(tw, lst[:, L_DB:L_DB + 1]), T.ts[:, 0:16], OP.is_equal, [ch, "tsl", "tspad", "l_db"], ["mb"])
-        tt(T.m[:, 16:48], ind(tw, lst[:, L_DC:L_DC + 2]), T.ts[:, 12:44], OP.is_equal, [ch, "tsl", "tsp", "l_dc0", "l_dc1"], ["mc"])
-        tt(T.pp[:, 0:16], T.m[:, 8:24], T.m[:, 24:40], OP.mult, ["mb", "mc"], ["ppa"])
-        tt(T.pp[:, 16:24], T.pp[:, 8:16], T.m[:, 40:48], OP.mult, ["ppa", "mc"], ["ppb"])
-        mm("p1", T.p1[:, 24:28], T.one1[:], T.m[:, 48:52], True, False, ["ma", "one1"])
-        mm("p1", T.p1[:, 24:28], T.one0[:], T.m[:, 52:56], False, True, ["ma", "one0"])
-        mm("p1", T.p1[:, 28:32], ones, T.pp[:, 0:4], True, False, ["ppa"])
-        mm("p1", T.p1[:, 28:32], ones, T.pp[:, 4:8], False, True, ["ppa"])
-        mm("p1", T.p1[:, 32:36], ones, T.pp[:, 16:20], True, False, ["ppb"])
-        mm("p1", T.p1[:, 32:36], ones, T.pp[:, 20:24], False, True, ["ppb"])
-        tt(T.vm[:, 12:24], T.p1[:, 24:36], cst[:, K_DMK:K_DMK + 12], OP.mult, ["k_dmk"], ["p1", "vmb"])
-        ac(T.vm[:, 0:12], T.vm[:, 12:24], AF.Sign, 0.0, 1.0, ["vmb"], ["vma"], acc=T.vm[:, 24:25])
-        ts(T.ix[:, 0:1], T.vm[:, 24:25], 4.0, cc(C_IX), OP.mult, OP.add, ["vma", "c_ix"], ["ix"])
-        o, nk = 16 * (t + 1), "nx%d" % (t + 1)
-        cp(T.nx[:, o:o + 16], ind(T.l_ch[:, 32 * t:32 * t + 32], T.ix[:, 0:1]), [ch, "ix"], [nk])
-        if t < NSTEP - 1:
-            send(verifier(t + 1), T.l_xt[:, 8 * t + 8:8 * t + 16], T.nx[:, o:o + 8], "a_xt%d" % (t + 1), [nk], 32)
-        ac(T.ytb[:, 4 * t:4 * t + 4], T.nx[:, o + 4:o + 8], AF.Identity, 0.0, 1.0, [nk], ["yt%d" % t])
-        if t < NSTEP - 1:
-            cp(T.rt[:], T.nx[:, o + 4:o + 8], [nk], ["rt"])
-            ts(T.u[:, 320:324], T.nx[:, o + 4:o + 8], -float(H), cc(C_0), OP.add, OP.mult, [nk, "c_0"], ["rd"])
+        o = 48 * t
 
-    def chain(t):
-        xt, xk = T.l_xt[:, 8 * t:8 * t + 8], "l_xt%d" % t
-        o = 32 * t
-        rep = lst[:, L_REP:L_REP + 4]
-        cp(T.ctl[:, 0:4], T.l_xt[:, 8 * t + 4:8 * t + 8], [xk], ["ctl0_%d" % s for s in range(4)])
-        ac(T.thr[:, 0:64], ind(xt, rep), AF.Identity, cc(C_NK), 1.0, [xk, "l_rep", "c_nk"], ["thr0"])
-        ac(T.xrh[:, 0:64], ind(xt, rep), AF.Identity, 0.0, 0.5, [xk, "l_rep"], ["xrh0"])
-        ac(T.cs[:, o:o + 4], T.l_xt[:, 8 * t:8 * t + 4], AF.Identity, 0.0, 1.0, [xk], ["csx0"])
-        for d in range(4):
-            lo, hi, tl, n = 64 * d, 64 * d + 64, T.ctl[:, 4 * d:4 * d + 4], str(d)
-            tk = ["ctl%d_%d" % (d, s) for s in range(4)]
-            ts(T.g1[:, lo:hi], ind(T.q[:], tl), -float(H), None, OP.add, None, ["q"] + tk, ["g1" + n])
-            if d:
-                tt(T.xr[:, lo:hi], ind(T.k[:, 0:V], tl), T.xrh[:, lo - 64:lo], OP.add, ["k", "xrh%d" % (d - 1)] + tk, ["xr" + n])
-                ac(T.thr[:, lo:hi], T.xr[:, lo:hi], AF.Identity, cc(C_NK), 1.0, ["xr" + n, "c_nk"], ["thr" + n])
-                if d < 3:
-                    ac(T.xrh[:, lo:hi], T.xr[:, lo:hi], AF.Identity, 0.0, 0.5, ["xr" + n], ["xrh" + n])
-                if d == 3:
-                    ac(T.cs[:, o + 4:o + 16], T.xr[:, 64:256:16], AF.Identity, 0.0, 1.0, ["xr1", "xr2", "xr3"], ["csx1"])
-            ts(T.c16[:, 4 * d:4 * d + 4], T.g1[:, lo:hi:16], float(H), None, OP.add, None, ["g1" + n], ["c16" + n])
-            tt(T.dg[:, lo:hi], T.g1[:, lo:hi], T.diag[:], OP.mult, ["g1" + n, "diag"], ["dg" + n])
-            mm("p3", T.p3[:, 0:128], ident, T.tie[:], True, False, ["tie"])
-            mm("p3", T.p3[:, 0:64], ones, T.dg[:, lo:hi], False, False, ["dg" + n])
-            tt(T.gec[:, lo:hi], ind(T.k[:, 0:V], T.c16[:, 4 * d:4 * d + 4]), T.thr[:, lo:hi], OP.is_ge,
-               ["k", "c16" + n, "thr" + n], ["gec" + n])
-            mm("p3", T.p3[:, 0:64], T.onew[:], T.gec[:, lo:hi], False, False, ["gec" + n, "onew"])
-            mm("p3", T.p3[:, 64:128], T.onew[:], T.gec[:, lo:hi], False, True, ["gec" + n, "onew"])
-            scan(T.zs[:, 2 * lo:2 * hi], T.rst[:], T.p3[:, 0:128], 0.0, OP.mult, OP.max, ["rst"], ["p3", "zs" + n])
-            for s in range(4):
-                out = T.ctl[:, 4 * d + 4 + s:4 * d + 5 + s] if d < 3 else T.cs[:, o + 28 + s:o + 29 + s]
-                at = 2 * lo + 16 * s + 15
-                ts(out, T.zs[:, at:at + 1], T.zs[:, at + 64:at + 65], float(H), OP.subtract, OP.add, ["zs" + n], ["ctl%d_%d" % (d + 1, s)])
-        cp(T.cs[:, o + 16:o + 28], T.ctl[:, 4:16], ["ctl%d_%d" % (d, s) for d in (1, 2, 3) for s in range(4)], ["cst"])
-        send(drafter(t), T.l_ch[:, o:o + 32], T.cs[:, o:o + 32], "a_ch%d" % t,
-             ["cst", "csx0", "csx1"] + ["ctl4_%d" % s for s in range(4)], 128)
+        def dd(lo, hi, step=1):
+            return at("p1", 160 + lo, 160 + hi, step)
 
-    def roots(t):
-        xk = "l_xt%d" % t
-        ac(T.xh[:, 0:4], T.l_xt[:, 8 * t:8 * t + 4], AF.Identity, 0.0, 1.0, [xk], ["xha"])
-        ac(T.xh[:, 4:8], T.l_xt[:, 8 * t:8 * t + 4], AF.Identity, 0.0, 0.5, [xk], ["xhb"])
+        def top(name, n):
+            return at(name, 4 * n, 4 * n + 4)
 
-    def numbers_list(t, c0, c1):
-        o = 24 * t + (4 if c0 else 0)
-        return T.l_lt[:, o + 4 * c0:o + 4 * c1]
-
-    PREP = sorted(set([(0, 1)] + [(max(a, 1), b) for a, b in PARTS if b > 1]))
+        terms = [(dd(0, 20), mat("negw"), at("cb", B_3, B_3 + 20)), (dd(12, 20), mat("negw"), at("l_ct", o + 36, o + 44))]
+        terms += [(dd(12 + h, 20, 2), mat("onew"), top("uta", 0)) for h in range(2)]
+        terms += [(dd(4, 20), mat("neg2"), at("cb", B_15, B_15 + 16)), (dd(4, 20), mat("neg2"), at("l_ct", o + 20, o + 36))]
+        terms += [(dd(4 + h, 12, 2), ones, top("uta", 0)) for h in range(2)]
+        terms += [(dd(12 + h, 20, 2), run(lo, ln), top("uta", p)) for p, h, lo, ln in runs_of(3, 2)]
+        terms += [(dd(0, 20), negq, at("cb", B_15, B_15 + 20)), (dd(0, 20), negq, at("l_ct", o, o + 20)), (dd(0, 4), ones, top("utb", 0))]
+        for d in (2, 3):
+            terms += [(dd(8 * d - 12 + h, 8 * d - 4, 2), run(lo, ln), top("utb", p)) for p, h, lo, ln in runs_of(d, 1)]
+        group(terms)
+        ts(at("m", 0, 20), dd(0, 20), 0.0, None, OP.is_equal)
+        later = [((4, 20, 2), (5, 20, 2)), ((0, 4), (4, 12, 2)), ((0, 4), (5, 12, 2)), ((4, 12), (12, 20)), ((4, 12, 2), (13, 20, 2)),
+                 ((5, 12, 2), (12, 20, 2))]
+        group([(dd(20, 40), ident, at("cb", B_NC, B_NC + 20)), (dd(20, 40), negi, at("m", 0, 20)), (dd(20, 40), mat("upper"), at("m", 0, 20))]
+              + [(dd(20 + a[0], 20 + a[1], *a[2:]), ones, at("m", *b)) for a, b in later])
+        ts(at("one"), dd(20, 40), 0.0, -256.0, OP.min, OP.mult)
+        parts = [(0, 4, 1), (4, 12, 2), (5, 12, 2), (12, 20, 2), (13, 20, 2)]
+        group([(dd(40, 44), ident, at("cb", B_S, B_S + 4))] + [(dd(40, 44), ones, at("one", *a)) for a in parts])
+        ix = at("ix", 4 * t, 4 * t + 4)
+        ts(ix, dd(40, 44), 4.0, None, OP.mult)
+        send(drafter(t), at("l_j", 4 * t, 4 * t + 4), ix, "a_e%d_4" % t)
+        ac(at("xg"), ind(at("x"), ix))
+        o, to = 8 * t + 8, verifier(t + 1, drafter(t))
+        ac(at("xs", o, o + 4), at("xg", 0, 64, 16))
+        send(to, at("l_x", o, o + 4), at("xs", o, o + 4), "a_x%d" % (t + 1))
+        if t + 1 == LAST:
+            top_of(at("u0"), at("es", 256 * t, 256 * t + 256), ix)
+            mm(dd(44, 48), ones, at("u0", 0, 64, 16), True, True)
+            ts(at("ix", 16, 20), dd(44, 48), -14.0 * H, None, OP.add)
+            send(to, at("l_j", 12, 16), at("ix", 16, 20), "a_r")
 
     def verify(t):
-        def prepare(bank, c0, c1):
-            lk, o = "l_lt%d_%d" % (t, c0), 24 * t + 4
-            cs = range(c0, c1)
-            ts(T.cd[:, 64 * c0:64 * c1], ind(T.q[:], T.l_lt[:, o + 4 * c0:o + 4 * c1]), -float(H), None, OP.add, None, ["q", lk],
-               ["cd%d" % c for c in cs])
-            ac(T.kn[:, 64 * c0:64 * c1], ind(T.k[:], numbers_list(t, c0, c1)), AF.Identity, 0.0, 1.0, ["k", "kz", lk], ["kn%d" % c for c in cs])
-            mix(bank, c0, c1)
-            add("v", lambda: vec.transpose(T.tr[:, 64 * c0:64 * c1], T[bank][:, 64 * c0:64 * c1]), [], [bank] + ["tr%d" % c for c in cs],
-                ns=50 + 64 * (c1 - c0) * CYC)
-            ts(T.ct[:, 64 * c0:64 * c1], ind(T.tr[:, 0:64 * c1], lst[:, L_PM + 4 * c0:L_PM + 4 * c1]), float(H), None, OP.add, None,
-               ["tr%d" % c for c in range(c1)] + ["l_pm"], ["ct%d" % c for c in cs])
-
-        def mix(bank, c0, c1):
-            for b in range(2 * c0, 2 * c1):
-                for h in range(2):
-                    at = 32 * b + 16 * h
-                    src = T.ide if h == 0 else T.ido
-                    for to in range(2):
-                        lo = 16 + 16 * (h - to)
-                        mm(bank, T[bank][:, at:at + 16], src[:, lo:lo + 128], T.cd[:, 32 * b + 16 * to:32 * b + 16 * to + 16],
-                           to == 0, to == 1, ["cd%d" % c0, "ide", "ido"])
-
-        def state(c):
-            at = 64 * c
-            tt(T.x[:, at:at + 64], ind(T.xh[:, 0:8 + at], lst[:, L_PAR + 4 * c:L_PAR + 4 * c + 4]), T.kn[:, at:at + 64],
-               OP.add, ["xha", "xhb", "l_par0", "l_par1", "kn%d" % c] + ["xh%d" % j for j in range(c)], ["x%d" % c])
-
-        def half(c):
-            ac(T.xh[:, 8 + 64 * c:72 + 64 * c], T.x[:, 64 * c:64 * c + 64], AF.Identity, 0.0, 0.5, ["x%d" % c], ["xh%d" % c])
-
-        def limits(c):
-            ac(T.th[:, 256 * c:256 * c + 256], ind(T.x[:, 64 * c:64 * c + 64], lst[:, L_TH:L_TH + 16]), AF.Identity, cc(C_NK), 1.0,
-               ["x%d" % c, "c_nk", "l_th"], ["th%d" % c])
-
-        def votes(c, kq):
-            at, gk = 1024 * (c % 2) + 256 * kq, "ge%d_%d" % (c % 2, kq)
-            bank = "p4" if c % 2 == 0 else "p0"
-            numbers, th = ind(T.k[:, 0:V], T.ct[:, 64 * c + 16 * kq:64 * c + 16 * kq + 16]), T.th[:, 256 * c:256 * c + 256]
-            tk = ["th%d" % c]
-            if (c, kq) in SHARE:
-                kc = T.kc[:, 256 * c:256 * c + 256]
-                ac(kc, numbers, AF.Identity, 0.0, 1.0, ["k", "ct%d" % c], ["kc%d" % c])
-                add("t", lambda: pe.matmul(T.p1[:, 256:512], T.negf[:], th, True, False), tk + ["negf"], ["p1"], ns=1024 * PE_COL, lat=PE_LAT)
-                mm("p1", T.p1[:, 256:512], ident, kc, False, True, ["kc%d" % c])
-                ac(T.ge[:, at:at + 256], T.p1[:, 256:512], AF.Sign, 2.0 ** -100, 1.0, [], ["p1", gk])
-            else:
-                tt(T.ge[:, at:at + 256], numbers, th, OP.is_ge, ["k", "ct%d" % c] + tk, [gk])
-            for kk in range(4):
-                k = 4 * kq + kk
-                lhs = T.runh[:, 15 - k:143 - k] if (c, kq) in SHARE else run(k, 1)
-                mm(bank, T[bank][:, 0:64], lhs, T.ge[:, at + 64 * kk:at + 64 * kk + 64], k == 0, k == 15, [gk, "runh"])
-
-        def ranks(c):
-            bank = "p4" if c % 2 == 0 else "p0"
-            key, kk = T.key[:, 64 * c:64 * c + 64], "key%d" % c
-            ac(key, T[bank][:, 0:64], AF.Identity, cc(C_K2 + c if SHARE else C_KB), 16.0, ["c_kb", "c_k2%d" % c], [bank, kk])
-            so = 512 * (c % 2)
-            for d in range(1, 9):
-                db = ("p5" if c % 2 == 0 else "p6") if c < 3 else ("p6" if d <= 4 else "p5")
-                mm(db, T[db][:, 64 * d - 64:64 * d], T.dm[:, 128 * d - 128:128 * d], key, True, True, [kk, "dm4", "dm8"])
-            mm("p7", T.p7[:, 0:64], ident, T.cd[:, 64 * c:64 * c + 64], True, False, ["cd%d" % c])
-            if c < 3:
-                db = "p5" if c % 2 == 0 else "p6"
-                ac(T.sg[:, so:so + 512], T[db][:, 0:512], AF.Sign, 0.0, 1.0, [], [db, "sga%d" % (c % 2), "sgb%d" % (c % 2)])
-            else:
-                ts(T.sg[:, so:so + 256], T.p6[:, 0:256], -1.0, 1.0, OP.max, OP.min, [], ["p6", "sga1"])
-                ac(T.sg[:, so + 256:so + 512], T.p5[:, 256:512], AF.Sign, 0.0, 1.0, [], ["p5", "sgb1"])
-            for d in range(1, 9):
-                lhs = T.bigi[:] if d == 8 else T.dm[:, 128 * (15 - d):128 * (16 - d)]
-                mm("p7", T.p7[:, 0:64], lhs, T.sg[:, so + 64 * d - 64:so + 64 * d], False, d == 8,
-                   ["sg%s%d" % ("a" if d <= 4 else "b", c % 2), "dm12", "dm15", "bigi"])
-            at = 256 * t + 64 * c
-            ac(T.es[:, at:at + 64], T.p7[:, 0:64], AF.Identity, cc(C_EB), 1.0, ["c_eb"], ["p7", "es%d" % c])
-            send(drafter(t), T.l_e[:, at:at + 64], T.es[:, at:at + 64], "a_e%d_%d" % (t, c), ["es%d" % c], 256)
-
-        for bank, (c0, c1) in zip(("p7", "p6", "p5"), PREP):
-            prepare(bank, c0, c1)
-        for c in range(4):
-            state(c)
-            limits(c)
-            if c < 3:
-                half(c)
-        for c in range(4):
+        prepare(t)
+        states(t)
+        for b in range(4):
             for kq in range(4):
-                votes(c, kq)
-                gk = last["ge%d_%d" % (c % 2, kq)]
-                if c >= PACE[0] and kq == PACE[1]:
-                    ops[last["es%d" % (c - PACE[0])]]["soon"] = [gk]
-                if t and (c, kq) == EARLY:
-                    ops[last["nx%d" % (t + 1)]]["soon"] = [gk]
-            ranks(c)
-
-    for _ in later_constants():
-        pass
-    last_constants()
-    for t in range(NSTEP):
-        chain(t)
-        draft(t)
-        if t:
-            ops[last["ctl4_3"]]["soon"] = [last[SOON]]
-        after_draft(t)
-        if t < NSTEP - 1:
-            twins()
+                votes(b, kq)
+            ranks(t, b)
         commit(t)
-        if t < NSTEP - 1:
-            roots(t)
+        for lo, hi, sem in back_parts(t):
+            send(drafter(t), at("l_e", lo, hi), at("es", lo, hi), sem)
+
+    def chain():
+        o = 8 * LAST
+        xt, rep = at("l_x", o, o + 4), at("lst", L_REP, L_REP + 4)
+        ac(block("thr", 0), ind(xt, rep), bias=cc(C_NK))
+        ac(block("xrh", 0), ind(xt, rep), scale=0.5)
+        ac(at("cs", 0, 4), at("l_x", o, o + 4))
+        for d in range(4):
+            lo, hi, tl = 64 * d, 64 * d + 64, at("ctl", 4 * d, 4 * d + 4) if d else at("l_j", 12, 16)
+            ts(block("g1", d), ind(at("q"), tl), -float(H), None, OP.add)
+            if d:
+                tt(block("xr", d), ind(at("k"), tl), block("xrh", d - 1), OP.add)
+                ac(block("thr", d), block("xr", d), bias=cc(C_NK))
+                if d < 3:
+                    ac(block("xrh", d), block("xr", d), scale=0.5)
+            ts(at("c16", 4 * d, 4 * d + 4), at("g1", lo, hi, 16), float(H), None, OP.add)
+            tt(block("dg", d), block("g1", d), at("diag"), OP.mult)
+            tt(block("gec", d), ind(at("k"), at("c16", 4 * d, 4 * d + 4)), block("thr", d), OP.is_ge)
+            group([(at("p3", 0, 128), ident, at("tie")), (at("p3", 0, 64), ones, block("dg", d)),
+                   (at("p3", 0, 64), mat("onew"), block("gec", d)), (at("p3", 64, 128), mat("onew"), block("gec", d))])
+            zs = at("zs", 2 * lo, 2 * hi)
+            add("v", lambda zs=zs: vec.tensor_tensor_scan(ap(zs), ap(at("rst")), ap(at("p3", 0, 128)), 0.0, OP.mult, OP.max),
+                [zs], [at("rst"), at("p3", 0, 128)], 50 + 128 * CYC)
+            for s in range(4):
+                out = at("ctl", 4 * d + 4 + s, 4 * d + 5 + s) if d < 3 else at("cs", 28 + s, 29 + s)
+                z = 2 * lo + 16 * s + 15
+                ts(out, at("zs", z, z + 1), at("zs", z + 64, z + 65), float(H), OP.subtract, OP.add)
+            if d < 3:
+                tt(at("cs", 32 + 4 * d, 36 + 4 * d), at("zs", 2 * lo + 15, 2 * lo + 64, 16), at("zs", 2 * lo + 79, 2 * hi, 16), OP.subtract)
+        ac(at("cs", 4, 16), at("xr", 64, 256, 16))
+        ac(at("cs", 16, 28), at("cs", 32, 44), bias=float(H))
+        o = 48 * LAST
+        tt(at("m"), ind(at("cs", 32, 44), at("lst", L_CMP, L_CMP + 3)), at("l_ct", o, o + 48), OP.is_equal)
+        tt(at("pp", 0, 16), at("m", 4, 20), at("m", 20, 36), OP.mult)
+        tt(at("pp", 16, 24), at("pp", 8, 16), at("m", 36, 44), OP.mult)
+        mm(at("p4", 0, 4), ones, at("m", 0, 4), True, True)
+        for j, lo in enumerate((0, 16)):
+            group([(at("p4", 4 * j + 4, 4 * j + 8), ones, at("pp", lo + h, lo + 8, 2)) for h in range(2)])
+        tt(at("vm", 12, 24), at("p4", 0, 12), at("cst", K_DMK, K_DMK + 12), OP.mult)
+        ac(at("vm", 0, 12), at("vm", 12, 24), AF.Sign, acc=at("vm", 24, 25))
+        ts(at("ix", 12, 13), at("vm", 24, 25), 4.0, cc(C_IX), OP.mult, OP.add)
+        cp(at("fin"), ind(at("cs", 0, 32), at("ix", 12, 13)))
+        send(drafter(LAST), at("l_f"), at("fin", 0, 8), "a_f")
+
+    for t in range(NSTEP):
+        root(t)
+        draft(t)
+        if t < LAST:
+            twins()
             verify(t)
-            places()
-            for c in range(4):
-                overwrite(t, c)
-    t = NSTEP - 1
-    ac(T.yw[:, 0:4], T.nx[:, 16 * t:16 * t + 4], AF.Identity, 0.0, 1.0, ["nx%d" % t], ["ywa"])
-    ac(T.yw[:, 4:8], T.nx[:, 16 * t:16 * t + 4], AF.Identity, 0.0, 1.0, ["nx%d" % t], ["ywb"])
-    for c0, c1 in PREP:
-        tt(T.ks[:, 64 * c0:64 * c1], ind(T.k[:], numbers_list(t, c0, c1)), T.sc[:, 64 * c0:64 * c1], OP.mult,
-           ["k", "kz", "l_lt%d_%d" % (t, c0), "sc", "sc2", "sc3", "sca", "scb", "scc"], ["ks%d" % c for c in range(c0, c1)])
-    for a, b in PARTS:
-        send(drafter(t), T.l_kn[:, 64 * a:64 * b], T.ks[:, 64 * a:64 * b], "a_kn%d" % a, ["ks%d" % c for c in range(a, b)], 128 * (b - a))
-    dma("s", T.yx[:], T.nx[:, 16 * NSTEP:16 * NSTEP + 4], "d_yx", ["nx%d" % NSTEP], ["yx"])
-    dma("s", T.yt[:], T.ytb[0:128:16, :], "d_yt", ["yt%d" % j for j in range(NSTEP)], ["yt"])
-    for c in range(4):
-        at = 64 * c
-        tt(T.yw[:, 8 + at:72 + at], ind(T.yw[:, 0:8 + at], lst[:, L_PAR + 4 * c:L_PAR + 4 * c + 4]), T.l_kn[:, at:at + 64],
-           OP.add, ["ywa", "ywb", "l_kn%d" % c, "l_par0", "l_par1"] + ["yw%d" % j for j in range(c)], ["yw%d" % c])
-        if c % 2:
-            lo, hi, e = at - 64, at + 64, "s" if c == 1 else "y"
-            tt(T.yo[:, lo:hi], ind(T.yw[:, 8:8 + hi], lst[:, L_PM + 4 * c - 4:L_PM + 4 * c + 4]), T.isc[:, lo:hi], OP.mult,
-               ["yw%d" % j for j in range(c + 1)] + ["l_pm", "is0", "is1", "is2", "is3"], ["yo%d" % c])
-            dma(e, T.yn[:, lo:hi], T.yo[:, lo:hi], "d_yn%d" % c, ["yo%d" % c], ["yn%d" % c], 128 * 512)
-    add("g", None, ["yx", "yt", "yn1", "yn3", "a"])
+            overwrite(t)
+    chain()
+    states(LAST)
+    dma("s", T.yt[:, 0:12], T.ytb[0:128:16, :], "d_yu", ["yu"], [at("ytb")])
+    for j, (lo, hi) in enumerate(((0, CUT), (CUT, 256))):
+        send(drafter(LAST), at("l_y", lo, hi), at("x", lo, hi), "a_y%d" % j)
+        dma("y", T.yn[:, lo:hi], T.l_y[:, lo:hi], "d_y%d" % j, ["y%d" % j], [at("l_y", lo, hi)], 128 * 4 * (hi - lo))
+    dma("s", T.yx[:], T.l_f[:, 0:4], "d_yx", ["yx"], [at("l_f")])
+    dma("s", T.yt[:, 12:16], T.l_f[0:128:16, 4:8], "d_yt", ["yt"], [at("l_f")])
+    add("g", None, [], ["yx", "yt", "yu", "y0", "y1"], 50)
     emit(g, T, arrange(ops, sends))
     g.wait_ge(T.sem.sent, sent[0])

@@ -18,8 +18,10 @@ TILES = ((0, 4), (4, 10), (10, 16))
 TILES_LAST = ((0, 4), (4, 12), (10, 16))
 BLOCKS = ((0, 4), (4, 8), (8, 12), (12, 16))
 STATES_LAST = ((0, 4), (4, 8), (8, 12), (10, 16))
+PREP = ((0, 4), (4, 10), (10, 12), (12, 16))
 BACK = ((0, 1), (1, 2), (2, 3), (3, 4))
 SHARE = ((0, 3), (1, 3))
+XW = 264
 LT = 18
 
 
@@ -29,23 +31,24 @@ def _sb(cols, dtype):
 
 F, B, HF, I, U = "float32", "bfloat16", "float16", "int32", "uint16"
 SCRATCH = {
-    "q": _sb(V, I), "a": _sb(V + 16, I), "k": _sb(V, B), "kp": _sb(4, F), "tk": _sb(4, I), "xi": _sb(4, F),
+    "q": _sb(V, I), "a": _sb(V + 32, I), "k": _sb(V, B), "kp": _sb(4, F), "tk": _sb(4, I), "xi": _sb(8, F),
     "pi": _sb(8, I), "col": _sb(48, F), "xq": _sb(160, F), "ab": _sb(160 * 4, B), "idw": _sb(160, B), "ide": _sb(160, B), "ido": _sb(160, B),
     "runs": _sb(160 * len(LENS), B), "runh": _sb(160, B), "negi": _sb(128, B), "negq": _sb(128, B),
     "negw": _sb(128, B), "negf": _sb(128, F), "onew": _sb(128, B), "upper": _sb(128, B), "fmi": _sb(128, I), "fm": _sb(256, B),
-    "shf": _sb(128 * 15, B), "dm": _sb(128 * 15, B), "lose": _sb(128 * 8, B), "rowx": _sb(80, F), "uc": _sb(320, F),
-    "cu": _sb(384, B), "zero": _sb(48, B), "hp": _sb(48, F), "neg2": _sb(128, B), "ct0": _sb(48, B), "ct1": _sb(16, B), "rows": _sb(176, B), "cst": _sb(128, F),
-    "cb": _sb(224, B), "lst": _sb(80, U), "i64": _sb(128, F), "diag": _sb(64, F), "rst": _sb(128, F), "tie": _sb(128, B),
+    "shf": _sb(128 * 8, B), "dm": _sb(128 * 15, B), "lose": _sb(128 * 8, B), "rowx": _sb(80, F), "uc": _sb(320, F),
+    "cu": _sb(384, B), "zero": _sb(48, B), "hp": _sb(48, F), "neg2": _sb(128, B), "bigi": _sb(128, B), "ct0": _sb(48, B), "ct1": _sb(16, B), "rows": _sb(176, B), "cst": _sb(128, F),
+    "cb": _sb(224, B), "lst": _sb(104, U), "i64": _sb(128, F), "diag": _sb(64, F), "rst": _sb(128, B), "tie": _sb(128, B),
     "w": _sb(320, F), "u": _sb(384, HF), "rt": _sb(4, U), "pl": _sb(16, U), "ls": _sb(LT * NSTEP, U),
-    "cts": _sb(48 * NSTEP, HF), "t16": _sb(16, HF), "eq": _sb(128, B), "off": _sb(32, U), "ytb": _sb(12, F),
-    "cd": _sb(256, HF), "tr": _sb(256, F), "ct": _sb(256, U), "ph": _sb(256, F), "x": _sb(256, F), "th": _sb(1024, F),
+    "cts": _sb(48 * NSTEP, HF), "t16": _sb(16, HF), "eq": _sb(128, B), "off": _sb(16, U),
+    "dl": _sb(8, F), "dr": _sb(128, F), "eq2": _sb(256, B), "ytb": _sb(12, F),
+    "cd": _sb(256, HF), "tr": _sb(256, F), "ct": _sb(256, U), "ph": _sb(256, F), "x": _sb(XW * NSTEP, F), "th": _sb(1024, F),
     "ge": _sb(2048, B), "kc": _sb(512, B), "key": _sb(256, B), "sg": _sb(1024, B), "es": _sb(768, F),
     "uta": _sb(80, HF), "utb": _sb(192, HF), "m": _sb(48, B), "one": _sb(20, B), "ix": _sb(20, U), "xg": _sb(64, F),
     "xs": _sb(32, F), "u0": _sb(64, HF),
     "ctl": _sb(16, U), "g1": _sb(256, HF), "c16": _sb(16, U), "dg": _sb(256, HF), "xr": _sb(256, F), "xrh": _sb(256, F),
-    "thr": _sb(256, F), "gec": _sb(256, B), "zs": _sb(512, F), "cs": _sb(48, F), "pp": _sb(24, B), "vm": _sb(32, F),
+    "thr": _sb(256, F), "gec": _sb(256, B), "zs": _sb(512, F), "cs": _sb(48, F), "pp": _sb(24, B), "vm": _sb(44, F),
     "fin": _sb(16, F),
-    "l_x": _sb(8 * NSTEP, F), "l_lt": _sb(LT * NSTEP, U), "l_j": _sb(16, U), "l_ct": _sb(48 * NSTEP, HF), "l_e": _sb(768, F),
+    "l_lt": _sb(LT * NSTEP, U), "l_j": _sb(16, U), "l_ct": _sb(48 * NSTEP, HF), "l_e": _sb(768, F),
     "l_y": _sb(256, F), "l_f": _sb(8, F),
 }
 for _b in range(8):
@@ -79,21 +82,26 @@ def runs_of(depth, up, first=FIRST):
 
 
 def pieces(vals):
-    out, j = [], 0
-    while j < len(vals):
-        n, step = 1, vals[j + 1] - vals[j] if j + 1 < len(vals) else 0
-        while j + n < len(vals) and n < 16 and vals[j + n] == vals[j] + n * step:
-            n += 1
-        out.append((j, vals[j], step if n > 1 else 0, n))
-        j += n
+    out, todo = [], [j for j, v in enumerate(vals) if v]
+    while todo:
+        best = (todo[0], 1, vals[todo[0]], 0, 1)
+        for j in todo:
+            for k in todo:
+                n, far, step = 1, k - j, vals[k] - vals[j]
+                while far > 0 and n < 16 and j + n * far in todo and vals[j + n * far] == vals[j] + n * step:
+                    n += 1
+                if n > best[4]:
+                    best = (j, far, vals[j], step, n)
+        out.append(best)
+        todo = [j for j in todo if j not in range(best[0], best[0] + best[1] * best[4], best[1])]
     return out
 
 
-CYC, GATHER, SCATTER, PE_COL, PE_LAT, WAKE, ISSUE, HOP, ROW_NS, LINK, DMA0, HBM = 0.85, 1.5, 3.8, 0.43, 100, 190, 250, 750, 25, 20.0, 1500, 250.0
-PASSES = 2500
+CYC, GATHER, SCATTER, PE_COL, PE_LAT, WAKE, ISSUE, HOP, ROW_NS, LINK, DMA0, HBM = 0.85, 1.5, 3.8, 0.43, 100, 200, 250, 750, 25, 20.0, 1200, 600.0
+PASSES = 4000
 STRETCH = 3000
-SHAKE = 1500
-CASES = ((1.0, 190, 0.8), (1.0, 190, 1.5), (1.3, 220, 1.0), (1.0, 130, 1.0))
+SHAKE = 700
+CASES = ((1.0, 200, 0.7, 1.0), (1.0, 200, 1.4, 1.6), (1.3, 220, 1.0, 1.4), (1.0, 150, 1.0, 1.2))
 PLANS = {}
 
 
@@ -157,9 +165,10 @@ def arrange(ops, sends):
 
     if n not in PLANS:
         cases = []
-        for slow, wake, far in CASES:
+        for slow, wake, far, load in CASES:
             ns = [op["ns"] * (slow if op["e"] in "vst" else far) for op in ops]
-            cases.append((ns, [[(d, w and (w + wake - WAKE + (far - 1) * HOP * (ops[d]["e"] == "w"))) for d, w in before[j]] for j in range(n)]))
+            more = [wake - WAKE + op["lat"] * {"w": far - 1, "y": load - 1}.get(op["e"], 0) for op in ops]
+            cases.append((ns, [[(d, w and w + more[d]) for d, w in before[j]] for j in range(n)]))
         back, best, seed = tail, None, 1
         for p in range(PASSES):
             end = fill(sorted(range(n), key=lambda j: -back[j]), before)
@@ -305,7 +314,7 @@ def rank_program(g, core, T, topo):
             return fixed + width(out) * GATHER * CYC
         if each == 1.0 and fixed == 50 and all(SCRATCH[x[0]][2] in (B, HF, U) for x in [out] + ins):
             each = 0.5
-        return max(64 * CYC, fixed + width(out) * each * CYC)
+        return max(64, width(out) * each) * CYC + (fixed > 65) * 20
 
     def ts(out, a, s1, s2, op0, op1=None):
         more = () if op1 is None else (op1,)
@@ -317,6 +326,9 @@ def rank_program(g, core, T, topo):
 
     def cp(out, a, more=()):
         add("v", lambda: vec.tensor_copy(ap(out), ap(a)), [out], [a] + list(more), took(50, out, [a]))
+
+    def scan(out, keep, a):
+        add("v", lambda: vec.tensor_tensor_scan(ap(out), ap(keep), ap(a), 0.0, OP.mult, OP.max), [out], [keep, a], took(50, out, [keep, a]))
 
     def ms(out, val):
         add("v", lambda: vec.memset(ap(out), val), [out], [], took(50, out, []))
@@ -344,14 +356,13 @@ def rank_program(g, core, T, topo):
         add("g", lambda: g.affine_select(ap(out), ap(a), pattern, op, fill, 0, 1), [out], [a], 170 + 2 * width(out) * CYC)
 
     def table(name, lo, vals):
-        for turn, (j, first, step, n) in enumerate(pieces(vals)):
-            out = at(name, lo + j, lo + j + n)
-            if turn % 3 == 2:
-                iota(out, [[step, n]], first)
-            elif step or turn % 3:
+        ms(at(name, lo, lo + len(vals)), 0.0)
+        for turn, (j, far, first, step, n) in enumerate(pieces(vals)):
+            out = at(name, lo + j, lo + j + far * (n - 1) + 1, far)
+            if turn % 2:
                 ac(out, at("i64", 0, n), bias=float(first), scale=float(step))
             else:
-                ms(out, float(first))
+                ts(out, at("i64", 0, n), float(step), float(first), OP.mult, OP.add)
 
     def dma(e, out, a, sem, w, r, nbytes=0):
         add(e, lambda: (g.sync if e == "y" else act).dma_start(out, a), w, r, 50, DMA0 + nbytes / HBM, sem)
@@ -388,14 +399,14 @@ def rank_program(g, core, T, topo):
         return out
 
     def tokens(t, c0, c1):
-        lo = [place - a for a, b, place in tiles(t) if a <= c0][-1 if c1 == 16 else 0 if c0 == 0 else 1]
+        lo = [place - a for a, b, place in tiles(t) if a <= c0][-1 if c1 == 16 or t < LAST else 0 if c0 == 0 else 1]
         return at("l_lt", lo + c0, lo + c1)
 
     def back_parts(t):
         return [(256 * t + 64 * a, 256 * t + 64 * b, "a_e%d_%d" % (t, a)) for a, b in BACK]
 
     for t in range(NSTEP):
-        lands(at("l_x", 8 * t, 8 * t + 4), "a_x%d" % t, verifier(t - 1, drafter(t)) if t else drafter(0))
+        lands(at("x", XW * t, XW * t + 8), "a_x%d" % t, verifier(t - 1, drafter(t)) if t else drafter(0))
         lands(at("l_ct", 48 * t, 48 * t + 48), "a_ct%d" % t, drafter(t))
         for j, (c0, c1, lo) in enumerate(tiles(t)):
             lands(at("l_lt", lo, lo + c1 - c0), "a_lt%d_%d" % (t, j), drafter(t))
@@ -408,11 +419,11 @@ def rank_program(g, core, T, topo):
     lands(at("l_f"), "a_f", verifier(LAST))
     lands(at("l_j", 12, 16), "a_r", verifier(LAST - 1, drafter(LAST)))
 
-    (C_I, C_0, C_TK, C_UC, C_UT, C_KB, C_S, C_Q, C_IX, C_NK, C_JK, C_T, C_EV, C_OD, C_PM) = range(15)
+    (C_I, C_0, C_TK, C_UC, C_UT, C_KB, C_S, C_Q, C_IX, C_NK, C_JK, C_T, C_EV, C_OD, C_PM, C_R, C_J2) = range(17)
     C_K2, C_MID, C_LOSE, C_PAD = 20, 24, 32, 36
     K_A, K_S4, K_TH, K_PM, K_NC, K_R, K_DMK = 0, 20, 24, 40, 56, 76, 92
     B_15, B_3, B_NC, B_S, B_SH, B_H = 0, 36, 56, 76, 80, 144
-    L_UC, L_CMP, L_PAR, L_REP, L_TH, L_PM = 0, 20, 24, 40, 44, 60
+    L_UC, L_CMP, L_PAR, L_REP, L_TH, L_PM, L_TH0, L_8 = 0, 20, 24, 40, 44, 60, 76, 92
 
     def cc(j):
         return at("col", j, j + 1)
@@ -427,17 +438,20 @@ def rank_program(g, core, T, topo):
     ident, ones, negi, negq = at("idw", 16, 144), run(0, 16), mat("negi"), mat("negq")
 
     ms(at("tk"), 0)
-    dma("s", T.xi[:], T.x0[:], "d_x", [at("xi")], [])
+    ms(at("xi", 4, 8), 0.0)
+    ms(at("xs"), 0.0)
+    dma("s", T.xi[:, 0:4], T.x0[:], "d_x", [at("xi", 0, 4)], [])
     dma("s", T.kp[:, 0:1], T.kap[:], "d_kp", [at("kp", 0, 1)], [])
     dma("y", T.tk[0:128:16, :], T.tok[:], "d_tk", [at("tk")], [])
     dma("y", T.q[:], T.qt[:], "d_q", ["q"], [], 128 * V * 4)
     dma("y", T.k[:], T.kt[:], "d_k", ["k"], [], 128 * V * 6)
     dma("y", T.a[:, 0:V], T.qt[:], "d_a", ["a"], ["q"], 128 * V * 6)
-    send(verifier(0), at("l_x", 0, 4), at("xi"), "a_x0")
+    send(verifier(0), at("x", 0, 8), at("xi"), "a_x0")
     ops[-1]["lat"] += 5000
 
     iota(at("pi", 0, 1), [[0, 1]], 0, 1)
-    iota(at("i64"), [[0, 8], [1, 16]], 0)
+    iota(at("i64", 0, 16), [[1, 16]], 0)
+    iota(at("i64", 16, 128), [[0, 7], [1, 16]], 0)
     iota(at("xq"), [[1, 160]], 0, -1)
     ts(at("pi", 1, 2), at("pi", 0, 1), 15, None, OP.bitwise_and)
     cp(cc(C_I), at("pi", 1, 2))
@@ -447,15 +461,18 @@ def rank_program(g, core, T, topo):
         ac(cc(C_MID + j), cc(C_I), bias=-15.0 - (ln - 1) / 2)
         ac(at("ab", 160 * j, 160 * j + 160), at("xq"), AF.Abs, cc(C_MID + j))
         ts(at("runs", 160 * j + 160, 160 * j + 320), at("ab", 160 * j, 160 * j + 160), ln / 2, None, OP.is_lt)
-    table("rowx", 0, ROW[1:17] + ROW[16:48] + ROW[40:64] + [0] * 8)
+    cp(at("rowx", 0, 16), at("i64", 0, 16))
+    table("rowx", 16, ROW[16:48])
+    table("rowx", 48, ROW[40:64] + [0] * 8)
     iota(at("cst", K_A, K_A + 4), [[0, 4]], 0)
     iota(at("cst", K_A + 4, K_A + 20), [[32, 2], [0, 4], [16, 2]], 16)
     ts(at("lst", L_UC, L_UC + 20), at("cst", K_A, K_A + 20), cc(C_I), None, OP.add)
     ac(cc(C_UC), cc(C_I), bias=float(H), scale=-float(R))
     ac(cc(C_UT), cc(C_I), bias=-float(H), scale=float(R))
-    rows = ind(at("rowx"), at("lst", L_UC, L_UC + 20))
-    ac(at("cu", 0, 320), rows, bias=-7.0 * 144, scale=144.0)
-    ac(at("uc"), rows, bias=cc(C_UC), scale=float(R))
+    for lo, hi in ((0, 4), (4, 12), (12, 20)):
+        rows = ind(at("rowx", 0, 4 * hi), at("lst", L_UC + lo, L_UC + hi))
+        ac(at("cu", 16 * lo, 16 * hi), rows, bias=-7.0 * 144, scale=144.0)
+        ac(at("uc", 16 * lo, 16 * hi), rows, bias=cc(C_UC), scale=float(R))
     ms(at("cu", 320, 384, 16), -7.0 * 144)
     ms(at("zero"), 0.0)
     ts(cc(C_0), cc(C_I), 0.0, None, OP.is_equal)
@@ -475,13 +492,13 @@ def rank_program(g, core, T, topo):
     def pe_root(src, init):
         group([(at("p0", 44, 48), ident, at(init, 44, 48)), (at("p0", 44, 48), ones, node(src, 0))])
 
-    def pe_parents(src, init, depth, up, lo):
-        group([(at("p0", lo, lo + 8), ident, at(init, lo, lo + 8))]
-              + [(at("p0", lo + h, lo + 8, 2), run(first, ln), node(src, p))
+    def pe_parents(src, init, depth, up, lo, bank="p0"):
+        group([(at(bank, lo, lo + 8), ident, at(init, lo, lo + 8))]
+              + [(at(bank, lo + h, lo + 8, 2), run(first, ln), node(src, p))
                  for p, h, first, ln in runs_of(depth, up, FIRST if up > 1 else START)])
 
-    def pe_nodes(src, init):
-        group([(at("p0", 0, 20), ident, at(init, 0, 20))] + [(at("p0", 0, 20), run(i, 1), at(src, i, 320, 16)) for i in range(16)])
+    def pe_nodes(src, init, bank="p0"):
+        group([(at(bank, 0, 20), ident, at(init, 0, 20))] + [(at(bank, 0, 20), run(i, 1), at(src, i, 320, 16)) for i in range(16)])
 
     def pe_tile(c0, c1, level):
         terms = [(at("p1", c0, c1), ident, at("ct1", c0, c1))]
@@ -493,17 +510,18 @@ def rank_program(g, core, T, topo):
                 terms.append((at("p1", first, c1), run(4 * r + s, 1), at("u", lo, lo + 4 * (c1 - first) - 3, 4)))
         group(terms)
 
-    pe_root("cu", "zero")
-    pe_parents("cu", "zero", 2, 1, 20)
-    pe_parents("cu", "zero", 3, 1, 28)
-    pe_parents("cu", "zero", 3, 2, 36)
-    pe_nodes("cu", "zero")
-    ac(at("ct0"), at("p0", 0, 48))
+    ms(at("ct0", 44, 48), -14.0 * H)
+    for depth, up, lo in ((2, 1, 20), (3, 1, 28), (3, 2, 36)):
+        pe_parents("cu", "zero", depth, up, lo, "p%d" % (depth + up - 1))
+        ac(at("ct0", lo, lo + 8), at("p%d" % (depth + up - 1), lo, lo + 8))
+    pe_nodes("cu", "zero", "p5")
+    ac(at("ct0", 0, 20), at("p5", 0, 20))
     ms(at("rows", 64, 65), -7.0 * 144)
     for d, (lo, hi) in enumerate(zip(START[1:], START[2:] + (64,))):
         ac(at("rows", 64 + lo, 64 + hi), at("rowx", (0, 16, 48)[d], (0, 16, 48)[d] + hi - lo), bias=-7.0 * 144, scale=144.0)
-    group([(at("p1", 0, 16), run(4 * r, 4), at("rows", 64 + r, 128, 4)) for r in range(4)])
-    ac(at("ct1"), at("p1", 0, 16))
+    for bank, lo, hi in (("p1", 0, 4), ("p6", 4, 16)):
+        group([(at(bank, lo, hi), run(4 * r, 4), at("rows", 64 + 4 * lo + r, 64 + 4 * hi, 4)) for r in range(4)])
+        ac(at("ct1", lo, hi), at(bank, lo, hi))
 
     ts(at("pi", 3, 4), at("pi", 0, 1), 3, None, OP.bitwise_and)
     ts(at("pi", 4, 5), at("pi", 1, 2), 2, None, OP.logical_shift_right)
@@ -511,11 +529,14 @@ def rank_program(g, core, T, topo):
     cp(cc(C_Q), at("pi", 4, 5))
     iota(at("cst", K_TH, K_TH + 16), [[0, 4], [16, 4]], 0)
     ts(at("lst", L_TH, L_TH + 16), at("cst", K_TH, K_TH + 16), cc(C_I), None, OP.add)
-    table("rows", 0, PAR)
-    group([(at("p2", 0, 16), run(4 * r, 4), at("rows", r, 64, 4)) for r in range(4)])
-    ts(at("lst", L_PAR, L_PAR + 16), at("p2", 0, 16), 0.25, cc(C_S), OP.mult, OP.add)
+    ts(at("lst", L_TH0, L_TH0 + 16), at("cst", K_TH, K_TH + 16), cc(C_I), 8.0, OP.add, OP.add)
+    ts(cc(C_R), cc(C_I), 4.0, 8.0, OP.is_ge, OP.mult)
+    ts(at("lst", L_TH0, L_TH0 + 16, 4), at("cst", K_TH, K_TH + 16, 4), cc(C_I), cc(C_R), OP.add, OP.add)
+    table("rows", 0, [p and p + 2 for p in PAR])
+    group([(at("p3", 0, 16), run(4 * r, 4), at("rows", r, 64, 4)) for r in range(4)])
+    ts(at("lst", L_PAR, L_PAR + 16), at("p3", 0, 16), 0.25, cc(C_S), OP.mult, OP.add)
     iota(at("rows", 128, 132), [[1, 4]], 0)
-    iota(at("rows", 132, 148), [[4, 2], [1, 4], [0, 2]], 4)
+    iota(at("rows", 132, 148), [[0, 2], [1, 4], [0, 2]], 4)
     iota(at("rows", 148, 164), [[4, 2], [1, 4], [0, 2]], 0)
     iota(at("rows", 164, 176), [[1, 6], [0, 2]], 0)
     group([(at("p7", 0, 3), run(i, 1), at("rows", 128 + i, 176, 16)) for i in range(16)])
@@ -536,9 +557,12 @@ def rank_program(g, core, T, topo):
     ac(negi, ident, scale=-1.0)
     ac(negq, ident, scale=-2.0 / R)
     for d in range(1, 16):
-        ts(mat("shf", d - 1), mat("fm"), d + 1.0, None, OP.is_equal)
         bank, o = "p%d" % (3 + (d - 1) // 4), 128 * ((d - 1) % 4)
-        group([(at(bank, o, o + 128), ident, mat("shf", d - 1)), (at(bank, o, o + 128), ident, negi)])
+        if d <= 8:
+            ts(mat("shf", d - 1), mat("fm"), d + 1.0, None, OP.is_equal)
+            group([(at(bank, o, o + 128), ident, mat("shf", d - 1)), (at(bank, o, o + 128), ident, negi)])
+        else:
+            mm(at(bank, o, o + 128), mat("dm", 15 - d), ident, True, True)
         if d % 4 == 0 or d == 15:
             ac(at("dm", 128 * d - o - 128, 128 * d), at(bank, 0, o + 128))
     ac(cc(C_KB), cc(C_I), bias=-128.0, scale=-1.0)
@@ -557,7 +581,11 @@ def rank_program(g, core, T, topo):
     for d in range(8):
         ts(mat("lose", d), mat("fm"), cc(C_LOSE + d), float(R), OP.is_equal, OP.mult)
     ac(cc(C_JK), cc(C_I), bias=float(V))
-    add("g", lambda: g.iota(T.a[:, V:V + 16], [[0, 16]], 0, 0), ["az"], [], 160)
+    ac(cc(C_J2), cc(C_I), bias=V + 16.0)
+    ac(mat("bigi"), ident, scale=float(R))
+    cp(at("lst", L_8, L_8 + 8), at("i64", 0, 8))
+    ts(at("rst"), at("i64"), 0.0, None, OP.not_equal)
+    add("g", lambda: g.iota(T.a[:, V:V + 32], [[0, 32]], 0, 0), ["az"], [], 190)
     ac(mat("onew"), ones, scale=65536.0)
     ac(mat("negw"), ident, scale=-131072.0)
     keep(mat("upper"), ones, [[-1, 128]], OP.is_gt, 0.0)
@@ -573,7 +601,6 @@ def rank_program(g, core, T, topo):
     ac(at("cb", B_S, B_S + 4), at("cst", K_S4, K_S4 + 4), scale=0.25)
     iota(at("cst", K_DMK, K_DMK + 12), [[0, 3], [1, 4]], 0)
     ts(at("diag"), at("i64", 0, 64), cc(C_I), None, OP.is_equal)
-    ts(at("rst"), at("i64"), 0.0, None, OP.not_equal)
     ac(at("tie"), at("i64"), bias=15.0 * 4096, scale=-4096.0)
     cp(at("lst", L_REP, L_REP + 4), at("cst", K_S4, K_S4 + 4))
     ts(at("cst", K_DMK, K_DMK + 12), at("cst", K_DMK, K_DMK + 12), cc(C_S), None, OP.is_equal)
@@ -614,13 +641,22 @@ def rank_program(g, core, T, topo):
         for d in range(8):
             mm(at("p1", 16 + 16 * d, 32 + 16 * d), mat("dm", d), at("t16"), True, True)
         ts(at("eq"), at("p1", 16, 144), 0.0, None, OP.is_equal)
+        tt(at("dl"), at("t16", 0, 16, 2), at("t16", 1, 16, 2), OP.subtract)
+        ac(at("dr"), ind(at("dl"), at("lst", L_8, L_8 + 8)))
+        mm(at("p1", 256, 384, 16), ident, at("zero", 0, 8), True, True)
+        for d in range(15):
+            mm(at("p1", 257 + d, 384, 16), mat("dm", d), at("t16", 1, 16, 2), True, True)
+        tt(at("eq2", 0, 128), at("p1", 256, 384), at("dr"), OP.is_equal)
+        scan(at("eq2", 128, 256), at("rst"), at("eq2", 0, 128))
         out = at("p1", 144, 160)
-        group([(out, ident, at("t16"))] + [(out, mat("lose", d), at("eq", 16 * d, 16 * d + 16)) for d in range(8)])
-        ts(at("off", 0, 32, 2), out, float(H), cc(C_JK), OP.add, OP.min)
+        group([(out, ident, at("t16"))] + [(out, mat("lose", d), at("eq", 16 * d, 16 * d + 16)) for d in range(8)]
+              + [(at("p1", 144, 160, 2), mat("bigi"), at("eq2", 143, 256, 16))])
+        for h, c in enumerate((C_JK, C_J2)):
+            ts(at("off", h, 16, 2), at("p1", 144 + h, 160, 2), float(H), cc(c), OP.add, OP.min)
 
     def overwrite(t):
-        for c in range(16):
-            cp(ind(at("a"), at("off", 2 * c, 2 * c + 1)), at("l_e", 256 * t + 16 * c, 256 * t + 16 * c + 16), ["az"])
+        for c in range(0, 16, 2):
+            cp(ind(at("a"), at("off", c, c + 2)), at("l_e", 256 * t + 16 * c, 256 * t + 16 * c + 32), ["az"])
 
     def block(name, b, base=0):
         return at(name, base + 64 * b, base + 64 * b + 64)
@@ -631,17 +667,19 @@ def rank_program(g, core, T, topo):
     def states(t):
         for c0, c1 in BLOCKS if t < LAST else STATES_LAST:
             known = max(PAR[4 * c0:4 * c1])
-            win = at("x", 0, 4 * known + 4) if c0 else at("l_x", 8 * t, 8 * t + 4)
+            o = XW * t
+            win = at("x", o, o + (4 * known + 12 if c0 else 4))
             ac(cols("ph", c0, c1), ind(win, at("lst", L_PAR + c0, L_PAR + c1)), scale=0.5)
-            tt(cols("x", c0, c1), ind(at("k"), tokens(t, c0, c1)), cols("ph", c0, c1), OP.add)
-            if c0 == 0:
-                ac(at("x", 0, 4), at("l_x", 8 * t, 8 * t + 4))
+            tt(cols("x", c0, c1, o + 8), ind(at("k"), tokens(t, c0, c1)), cols("ph", c0, c1), OP.add)
             if t < LAST:
-                ac(at("th", 64 * c0, 64 * c1), ind(cols("x", c0, c1), at("lst", L_TH, L_TH + 16)), bias=cc(C_NK))
+                win, first = (cols("x", c0, c1, o + 8), L_TH) if c0 else (at("x", o, o + 72), L_TH0)
+                ac(at("th", 64 * c0, 64 * c1), ind(win, at("lst", first, first + 16)), bias=cc(C_NK))
+            if c0 == 0:
+                ac(at("x", o + 8, o + 12), at("x", o, o + 4))
 
     def prepare(t):
         done = 0
-        for c0, c1, _ in tiles(t):
+        for c0, c1 in PREP:
             ts(cols("cd", c0, c1), ind(at("q"), tokens(t, c0, c1)), -float(H), None, OP.add)
             for c in range(c0, c1, 2):
                 for h, src in enumerate(("ide", "ido")):
@@ -686,7 +724,10 @@ def rank_program(g, core, T, topo):
             if inner:
                 lo, hi = min(inner), max(inner) + 4
                 ts(at(name, lo, hi), at(bank, base + lo, base + hi), -2.0 * H / R, scale, OP.max, OP.mult)
-        ac(block("es", b, 256 * t), out, bias=cc(C_UC), scale=-R / 2.0)
+        if b < 3:
+            ac(block("es", b, 256 * t), out, bias=cc(C_UC), scale=-R / 2.0)
+        else:
+            ts(block("es", b, 256 * t), out, -R / 2.0, cc(C_UC), OP.mult, OP.add)
 
     def commit(t):
         o = 48 * t
@@ -717,10 +758,10 @@ def rank_program(g, core, T, topo):
         ix = at("ix", 4 * t, 4 * t + 4)
         ts(ix, dd(40, 44), 4.0, None, OP.mult)
         send(drafter(t), at("l_j", 4 * t, 4 * t + 4), ix, "a_e%d_4" % t)
-        ac(at("xg"), ind(at("x"), ix))
+        ac(at("xg"), ind(at("x", XW * t + 8, XW * t + XW), ix))
         o, to = 8 * t + 8, verifier(t + 1, drafter(t))
         ac(at("xs", o, o + 4), at("xg", 0, 64, 16))
-        send(to, at("l_x", o, o + 4), at("xs", o, o + 4), "a_x%d" % (t + 1))
+        send(to, at("x", XW * t + XW, XW * t + XW + 8), at("xs", o, o + 8), "a_x%d" % (t + 1))
         if t + 1 == LAST:
             top_of(at("u0"), at("es", 256 * t, 256 * t + 256), ix)
             mm(dd(44, 48), ones, at("u0", 0, 64, 16), True, True)
@@ -739,11 +780,10 @@ def rank_program(g, core, T, topo):
             send(drafter(t), at("l_e", lo, hi), at("es", lo, hi), sem)
 
     def chain():
-        o = 8 * LAST
-        xt, rep = at("l_x", o, o + 4), at("lst", L_REP, L_REP + 4)
+        xt, rep = at("x", XW * LAST, XW * LAST + 4), at("lst", L_REP, L_REP + 4)
         ac(block("thr", 0), ind(xt, rep), bias=cc(C_NK))
         ac(block("xrh", 0), ind(xt, rep), scale=0.5)
-        ac(at("cs", 0, 4), at("l_x", o, o + 4))
+        ac(at("cs", 0, 4), xt)
         for d in range(4):
             lo, hi, tl = 64 * d, 64 * d + 64, at("ctl", 4 * d, 4 * d + 4) if d else at("l_j", 12, 16)
             ts(block("g1", d), ind(at("q"), tl), -float(H), None, OP.add)
@@ -757,9 +797,7 @@ def rank_program(g, core, T, topo):
             tt(block("gec", d), ind(at("k"), at("c16", 4 * d, 4 * d + 4)), block("thr", d), OP.is_ge)
             group([(at("p3", 0, 128), ident, at("tie")), (at("p3", 0, 64), ones, block("dg", d)),
                    (at("p3", 0, 64), mat("onew"), block("gec", d)), (at("p3", 64, 128), mat("onew"), block("gec", d))])
-            zs = at("zs", 2 * lo, 2 * hi)
-            add("v", lambda zs=zs: vec.tensor_tensor_scan(ap(zs), ap(at("rst")), ap(at("p3", 0, 128)), 0.0, OP.mult, OP.max),
-                [zs], [at("rst"), at("p3", 0, 128)], 50 + 128 * CYC)
+            scan(at("zs", 2 * lo, 2 * hi), at("rst"), at("p3", 0, 128))
             for s in range(4):
                 out = at("ctl", 4 * d + 4 + s, 4 * d + 5 + s) if d < 3 else at("cs", 28 + s, 29 + s)
                 z = 2 * lo + 16 * s + 15
@@ -769,9 +807,13 @@ def rank_program(g, core, T, topo):
         ac(at("cs", 4, 16), at("xr", 64, 256, 16))
         ac(at("cs", 16, 28), at("cs", 32, 44), bias=float(H))
         o = 48 * LAST
-        tt(at("m"), ind(at("cs", 32, 44), at("lst", L_CMP, L_CMP + 3)), at("l_ct", o, o + 48), OP.is_equal)
-        tt(at("pp", 0, 16), at("m", 4, 20), at("m", 20, 36), OP.mult)
-        tt(at("pp", 16, 24), at("pp", 8, 16), at("m", 36, 44), OP.mult)
+        tt(at("m"), ind(at("cs", 32, 40), at("lst", L_CMP, L_CMP + 3)), at("l_ct", o, o + 48), OP.is_equal)
+        tt(at("pp", 0, 8), at("m", 4, 12), at("m", 20, 28), OP.mult)
+        tt(at("pp", 8, 16), at("m", 28, 36), at("m", 36, 44), OP.mult)
+        ts(at("vm", 28, 36), at("pp", 8, 16), -float(R), float(R), OP.mult, OP.add)
+        tt(at("vm", 36, 44), at("vm", 28, 36), at("l_ct", o + 12, o + 20), OP.add)
+        for h in range(2):
+            tt(at("pp", 16 + h, 24, 2), at("vm", 36 + h, 44, 2), at("cs", 40, 44), OP.is_equal)
         mm(at("p4", 0, 4), ones, at("m", 0, 4), True, True)
         for j, lo in enumerate((0, 16)):
             group([(at("p4", 4 * j + 4, 4 * j + 8), ones, at("pp", lo + h, lo + 8, 2)) for h in range(2)])
@@ -792,7 +834,7 @@ def rank_program(g, core, T, topo):
     states(LAST)
     dma("s", T.yt[:, 0:12], T.ytb[0:128:16, :], "d_yu", ["yu"], [at("ytb")])
     for j, (lo, hi) in enumerate(((0, CUT), (CUT, 256))):
-        send(drafter(LAST), at("l_y", lo, hi), at("x", lo, hi), "a_y%d" % j)
+        send(drafter(LAST), at("l_y", lo, hi), at("x", XW * LAST + 8 + lo, XW * LAST + 8 + hi), "a_y%d" % j)
         dma("y", T.yn[:, lo:hi], T.l_y[:, lo:hi], "d_y%d" % j, ["y%d" % j], [at("l_y", lo, hi)], 128 * 4 * (hi - lo))
     dma("s", T.yx[:], T.l_f[:, 0:4], "d_yx", ["yx"], [at("l_f")])
     dma("s", T.yt[:, 12:16], T.l_f[0:128:16, 4:8], "d_yt", ["yt"], [at("l_f")])

@@ -12,15 +12,25 @@ DEPTH = [0] * 64
 for _n in range(1, 64):
     DEPTH[_n] = DEPTH[PAR[_n]] + 1
 FIRST = [DEPTH.index(_d) for _d in range(4)] + [64]
-UCOL, USTEP, START = (320, 0, 64, 192), (16, 16, 32, 32), (0, 1, 16, 40)
-LENS = (1, 2, 4, 8, 16)
+UCOL, USTEP, START, USED = (320, 0, 64, 192), (16, 16, 32, 32), (0, 1, 16, 39), (0, 1, 16, 40)
+LENS = (1, 2, 3, 4, 8, 16)
 TILES = ((0, 4), (4, 10), (10, 16))
 TILES_LAST = ((0, 4), (4, 12), (10, 16))
 BLOCKS = ((0, 4), (4, 8), (8, 12), (12, 16))
+STATES = BLOCKS
 STATES_LAST = ((0, 4), (4, 8), (8, 12), (10, 16))
-PREP = ((0, 4), (4, 10), (10, 12), (12, 16))
-BACK = ((0, 1), (1, 2), (2, 3), (3, 4))
-SHARE = ((0, 3), (1, 3))
+CALLS = (((4, None), (4, None), (4, None), (4, "p7")), ((4, None), (4, None), (4, None), (4, "p7")),
+         ((4, None), (4, None), (4, None), (4, None)), ((4, None), (4, None), (4, None), (4, None)))
+TURN = "vttt"
+CANDS = "vsss"
+COUNT = ("p3", "p4", "p3", "p4")
+DIFFS = (((0, 8, "p5", "s"),), ((0, 8, "p6", "s"),), ((0, 4, "p5", "s"), (4, 8, "p2", "s")), ((0, 4, "p7", "s"), (4, 8, "p6", "v")))
+PLACES = ("p5", "p6", "p5", "p6")
+ENTRY = "sssv"
+COMMIT = "p0"
+TOPS = ((0, 128), (128, 192), (192, 256))
+MID = 14
+LAID = ()
 XW = 264
 LT = 18
 
@@ -32,20 +42,21 @@ def _sb(cols, dtype):
 F, B, HF, I, U = "float32", "bfloat16", "float16", "int32", "uint16"
 SCRATCH = {
     "q": _sb(V, I), "a": _sb(V + 32, I), "k": _sb(V, B), "kp": _sb(4, F), "tk": _sb(4, I), "xi": _sb(8, F),
-    "pi": _sb(8, I), "col": _sb(48, F), "xq": _sb(160, F), "ab": _sb(160 * 4, B), "idw": _sb(160, B), "ide": _sb(160, B), "ido": _sb(160, B),
+    "pi": _sb(8, I), "col": _sb(48, F), "xq": _sb(160, F), "ab": _sb(160 * 5, B), "idw": _sb(160, B), "ide": _sb(160, B), "ido": _sb(160, B),
     "runs": _sb(160 * len(LENS), B), "runh": _sb(160, B), "negi": _sb(128, B), "negq": _sb(128, B),
     "negw": _sb(128, B), "negf": _sb(128, F), "onew": _sb(128, B), "upper": _sb(128, B), "fmi": _sb(128, I), "fm": _sb(256, B),
     "shf": _sb(128 * 8, B), "dm": _sb(128 * 15, B), "lose": _sb(128 * 8, B), "rowx": _sb(80, F), "uc": _sb(320, F),
     "cu": _sb(384, B), "zero": _sb(48, B), "hp": _sb(48, F), "neg2": _sb(128, B), "bigi": _sb(128, B), "ct0": _sb(48, B), "ct1": _sb(16, B), "rows": _sb(176, B), "cst": _sb(128, F),
-    "cb": _sb(224, B), "lst": _sb(104, U), "i64": _sb(128, F), "diag": _sb(64, F), "rst": _sb(128, B), "tie": _sb(128, B),
-    "w": _sb(320, F), "u": _sb(384, HF), "rt": _sb(4, U), "pl": _sb(16, U), "ls": _sb(LT * NSTEP, U),
+    "cb": _sb(224, B), "lst": _sb(104, U), "i64": _sb(128, F), "diag": _sb(64, F), "rst": _sb(128, B), "tie": _sb(128, B), "sh": _sb(128, B),
+    "w": _sb(320, F), "u": _sb(384, HF), "rt": _sb(32, U), "rf": _sb(32, F), "pl": _sb(16, U), "ls": _sb(LT * NSTEP, U),
     "cts": _sb(48 * NSTEP, HF), "t16": _sb(16, HF), "eq": _sb(128, B), "off": _sb(16, U),
     "dl": _sb(8, F), "dr": _sb(128, F), "eq2": _sb(256, B), "ytb": _sb(12, F),
-    "cd": _sb(256, HF), "tr": _sb(256, F), "ct": _sb(256, U), "ph": _sb(256, F), "x": _sb(XW * NSTEP, F), "th": _sb(1024, F),
-    "ge": _sb(2048, B), "kc": _sb(512, B), "key": _sb(256, B), "sg": _sb(1024, B), "es": _sb(768, F),
-    "uta": _sb(80, HF), "utb": _sb(192, HF), "m": _sb(48, B), "one": _sb(20, B), "ix": _sb(20, U), "xg": _sb(64, F),
-    "xs": _sb(32, F), "u0": _sb(64, HF),
-    "ctl": _sb(16, U), "g1": _sb(256, HF), "c16": _sb(16, U), "dg": _sb(256, HF), "xr": _sb(256, F), "xrh": _sb(256, F),
+    "cd": _sb(256, HF), "cf": _sb(384, F), "tr": _sb(256, F), "tw": _sb(768, F), "ct": _sb(256, U), "ph": _sb(256, F),
+    "x": _sb(XW * NSTEP, F), "th": _sb(2048, F),
+    "ge": _sb(4096, B), "kc": _sb(4096, B), "key": _sb(256, B), "sg": _sb(2048, B), "es": _sb(768, F),
+    "uta": _sb(80, HF), "utb": _sb(192, HF), "m": _sb(48, B), "one": _sb(20, B), "ix": _sb(16, U), "xg": _sb(120, F),
+    "ut": _sb(512, HF), "tb": _sb(512, F), "rq": _sb(32, U),
+    "ctl": _sb(16, U), "g1": _sb(256, F), "c16": _sb(16, U), "dg": _sb(256, HF), "xr": _sb(256, F), "xrh": _sb(256, F),
     "thr": _sb(256, F), "gec": _sb(256, B), "zs": _sb(512, F), "cs": _sb(48, F), "pp": _sb(24, B), "vm": _sb(44, F),
     "fin": _sb(16, F),
     "l_lt": _sb(LT * NSTEP, U), "l_j": _sb(16, U), "l_ct": _sb(48 * NSTEP, HF), "l_e": _sb(768, F),
@@ -98,101 +109,230 @@ def pieces(vals):
 
 
 CYC, GATHER, SCATTER, PE_COL, PE_LAT, WAKE, ISSUE, HOP, ROW_NS, LINK, DMA0, HBM = 0.85, 1.5, 3.8, 0.43, 100, 200, 250, 750, 25, 20.0, 1200, 600.0
-PASSES = 4000
-STRETCH = 3000
-SHAKE = 700
-CASES = ((1.0, 200, 0.7, 1.0), (1.0, 200, 1.4, 1.6), (1.3, 220, 1.0, 1.4), (1.0, 150, 1.0, 1.2))
+CHUNK = 8
+SWEEPS, STRETCH, MOVES, REACH = 41, 110, 400, 24
+HEAT, SLACK, SEED, FLIPS, COPY = 300.0, 0.1, 2, 0.2, 5
+CASES = ((1.0, 1.0, 1.0, 1.0, 200, 0.7, 1.0), (1.0, 0.8, 1.3, 1.0, 200, 1.4, 1.6), (1.3, 1.2, 1.0, 1.3, 220, 1.0, 1.4), (1.1, 0.8, 0.7, 1.1, 150, 1.0, 1.2))
 PLANS = {}
 
 
 def arrange(ops, sends):
-    n = len(ops)
-    pre = [sorted(set(sends[d[0]] if isinstance(d, tuple) else d for d in op["deps"])) for op in ops]
-    kept = [j for j in range(n) if ops[j]["e"] == "y"]
-    kept = set((d, j) for d, j in zip(kept, kept[1:]) if d not in pre[j])
-    for d, j in kept:
-        pre[j].append(d)
+    if len(ops) not in PLANS:
+        PLANS[len(ops)] = plan(ops, sends)
+    scalar, turn = PLANS[len(ops)]
+    for j in scalar:
+        ops[j].update(e="s", fn=ops[j]["other"][0], ns=ops[j]["other"][1])
+    out = [j for j in turn if ops[j]["e"] != "w"]
+    new = {j: i for i, j in enumerate(out)}
+    return [dict(ops[j], deps=[d if isinstance(d, tuple) else new[d] for d in ops[j]["deps"]
+                               if not (d in ops[j]["turns"] and ops[d]["e"] == ops[j]["e"])]) for j in out]
+
+
+def plan(ops, sends):
+    deps = [set(sends[d[0]] if isinstance(d, tuple) else d for d in op["deps"]) for op in ops]
+    jobs, job, seen = [], [], set()
+    for j, op in enumerate(ops):
+        if op["e"] == "t" and j and ops[j - 1]["e"] == "t" and j - 1 in deps[j] and deps[j] <= seen and len(jobs[-1]) < CHUNK:
+            jobs[-1].append(j)
+        else:
+            jobs.append([j])
+            seen = set(deps[j])
+        seen.add(j)
+        job.append(len(jobs) - 1)
+    n = len(jobs)
+    eng = ["vstgyw".index(ops[m[0]]["e"]) for m in jobs]
+    pre = [set(job[d] for j in m for d in deps[j]) - {i} for i, m in enumerate(jobs)]
+    loads = [i for i in range(n) if eng[i] == 4]
+    kept = set((d, i) for d, i in zip(loads, loads[1:]) if d not in pre[i])
+    for d, i in kept:
+        pre[i].add(d)
     succ = [[] for _ in range(n)]
-    left = [len(p) for p in pre]
-    for j, p in enumerate(pre):
-        for d in p:
-            succ[d].append(j)
+    for i in range(n):
+        for d in pre[i]:
+            succ[d].append(i)
+    order, left = [i for i in range(n) if not pre[i]], [len(p) for p in pre]
+    for i in order:
+        for k in succ[i]:
+            left[k] -= 1
+            if not left[k]:
+                order.append(k)
+    above = [0] * n
+    for i in order:
+        for d in pre[i]:
+            above[i] |= above[d]
+        pre[i] = sorted(d for d in pre[i] if not above[i] >> d & 1 or (eng[d] >= 4))
+        for d in pre[i]:
+            above[i] |= 1 << d
+    succ = [[] for _ in range(n)]
+    for i in range(n):
+        for d in pre[i]:
+            succ[d].append(i)
+    turns = set((job[d], job[j]) for j, op in enumerate(ops) for d in op["turns"])
+    free_to_move = [ops[m[0]]["other"] is not None for m in jobs]
+    cases = [([0.0] * n, [[] for _ in range(n)], [[] for _ in range(n)]) for _ in CASES]
 
-    def lag(d, j):
-        if (ops[d]["e"] == "t" and ops[j]["e"] == "t") or (d, j) in kept:
-            return 0
-        return ops[d]["lat"] + WAKE
+    def price(i):
+        for (slow, gather, scatter, pe, wake, far, load), (ns, needs, gives) in zip(CASES, cases):
+            def lag(d, k):
+                if eng[d] == eng[k] and (eng[d] == 2 or (d, k) in turns) or (d, k) in kept:
+                    return 0.0
+                lat = ops[jobs[d][-1]]["lat"]
+                return lat * (1, 1, 1, 1, load, far)[eng[d]] + (wake if lat >= 0 else WAKE)
 
-    order, todo, stack = [], list(left), [j for j in range(n) if not left[j]]
-    while stack:
-        j = stack.pop()
-        order.append(j)
-        for k in succ[j]:
-            todo[k] -= 1
-            if not todo[k]:
-                stack.append(k)
-    tail = [0.0] * n
-    for j in reversed(order):
-        tail[j] = ops[j]["ns"] + max([lag(j, k) + tail[k] for k in succ[j]] + [0])
-    before = [[(d, lag(d, j)) for d in pre[j]] for j in range(n)]
-    after = [[(k, lag(j, k)) for k in succ[j]] for j in range(n)]
+            parts = [ops[j]["other"][1] if eng[i] == 1 and ops[j]["other"] else ops[j]["ns"] for j in jobs[i]]
+            ns[i] = sum(a + b * gather + c * scatter for a, b, c in parts) * (slow, slow, pe, far, far, far)[eng[i]]
+            needs[i], gives[i] = [(d, lag(d, i)) for d in pre[i]], [(k, lag(i, k)) for k in succ[i]]
 
-    def fill(turn, needs):
-        gaps = {e: [[0.0, 1e18]] for e in "vstgyw"}
-        end = [0.0] * n
-        for j in turn:
-            start, ns, room = max([end[d] + w for d, w in needs[j]] + [0.0]), ops[j]["ns"], gaps[ops[j]["e"]]
-            i = len(room) - 1
-            while i and room[i - 1][1] >= start + ns:
-                i -= 1
-            while max(room[i][0], start) + ns > room[i][1]:
-                i += 1
-            lo, hi = room[i]
-            start = max(lo, start)
-            end[j] = start + ns
-            room[i:i + 1] = [x for x in ([lo, start], [start + ns, hi]) if x[1] - x[0] >= 6]
-        return end
+    def flip(i):
+        eng[i] = 1 - eng[i]
+        for k in [i] + [d for d in pre[i] if (d, i) in turns] + [k for k in succ[i] if (i, k) in turns]:
+            price(k)
 
-    def replay(turn, ns, needs):
-        free, end = dict.fromkeys("vstgyw", 0.0), [0.0] * n
-        for j in turn:
-            start = free[ops[j]["e"]]
-            for d, w in needs[j]:
+    for i in range(n):
+        eng[i] = 1 if free_to_move[i] else eng[i]
+    for i in range(n):
+        price(i)
+
+    def replay(turn, ns, needs, end, free):
+        for i in turn:
+            start = free[eng[i]]
+            for d, w in needs[i]:
                 if end[d] + w > start:
                     start = end[d] + w
-            end[j] = free[ops[j]["e"]] = start + ns[j]
-        return max(end)
+            end[i] = free[eng[i]] = start + ns[i]
 
-    if n not in PLANS:
-        cases = []
-        for slow, wake, far, load in CASES:
-            ns = [op["ns"] * (slow if op["e"] in "vst" else far) for op in ops]
-            more = [wake - WAKE + op["lat"] * {"w": far - 1, "y": load - 1}.get(op["e"], 0) for op in ops]
-            cases.append((ns, [[(d, w and w + more[d]) for d, w in before[j]] for j in range(n)]))
-        back, best, seed = tail, None, 1
-        for p in range(PASSES):
-            end = fill(sorted(range(n), key=lambda j: -back[j]), before)
-            turn = sorted(range(n), key=lambda j: (end[j] - ops[j]["ns"], j))
-            total = sum(replay(turn, *case) for case in cases) / len(cases)
-            if best is None or total <= best[0]:
-                best = (total, turn, back)
-            if p % 4 == 0:
-                back = fill(sorted(range(n), key=lambda j: -end[j]), after)
-                continue
-            back = list(best[2])
-            seed = (seed * 1103515245 + 12345) % 2147483648
-            lo = seed / 2147483648 * best[0] - STRETCH / 2
-            for j in reversed(order):
-                if lo <= back[j] < lo + STRETCH:
-                    seed = (seed * 1103515245 + 12345) % 2147483648
-                    back[j] += (seed / 2147483648 - 0.5) * SHAKE
-                for k in succ[j]:
-                    if back[j] <= back[k]:
-                        back[j] = back[k] + 1
-        PLANS[n] = best
-    out = [j for j in PLANS[n][1] if ops[j]["e"] != "w"]
-    new = {j: i for i, j in enumerate(out)}
-    return [dict(ops[j], deps=[d if isinstance(d, tuple) else new[d] for d in ops[j]["deps"]]) for j in out]
+    def fill(first, needs, ns):
+        gaps, end = [[[0.0, 1e18]] for _ in range(6)], [0.0] * n
+        for i in sorted(range(n), key=lambda i: -first[i]):
+            start, room = max([end[d] + w for d, w in needs[i]] + [0.0]), gaps[eng[i]]
+            k = len(room) - 1
+            while k and room[k - 1][1] >= start + ns[i]:
+                k -= 1
+            while max(room[k][0], start) + ns[i] > room[k][1]:
+                k += 1
+            lo, hi = room[k]
+            start = max(lo, start)
+            end[i] = start + ns[i]
+            room[k:k + 1] = [x for x in ([lo, start], [end[i], hi]) if x[1] - x[0] >= 6]
+        return end
+
+    ns, needs, gives = cases[0]
+    back, best = [0.0] * n, None
+    for i in reversed(order):
+        back[i] = ns[i] + max([w + back[k] for k, w in gives[i]] + [0.0])
+    for _ in range(12):
+        end = fill(back, needs, ns)
+        if best is None or max(end) < best[0]:
+            best = (max(end), sorted(range(n), key=lambda i: (end[i] - ns[i], end[i])))
+        back = fill(end, gives, ns)
+    turn, seed = best[1], [SEED]
+
+    def draw():
+        seed[0] = (seed[0] * 1103515245 + 12345) % 2147483648
+        return seed[0] / 2147483648
+
+    ends = [[0.0] * n for _ in cases]
+    tags = [ops[m[0]]["tag"] for m in jobs]
+    named = {tag: i for i, tag in enumerate(tags)}
+    marks = [named[t, "draft", 0] for t in range(NSTEP)]
+
+    def alike(turn):
+        for (ns, needs, gives), end in zip(cases, ends):
+            replay(turn, ns, needs, end, [0.0] * 6)
+        best = min(range(NSTEP - 1), key=lambda t: sum(end[marks[t + 1]] - end[marks[t]] for end in ends))
+        end, ns = ends[0], cases[0][0]
+        period, key = end[marks[best + 1]] - end[marks[best]], []
+        for i, (t, part, j) in enumerate(tags):
+            k = named.get((best, part, j), i) if t is not None else i
+            key.append(end[k] - ns[k] + (0 if t is None else end[marks[0]] + t * period - end[marks[tags[k][0]]]))
+            if free_to_move[i] and eng[i] != eng[k]:
+                flip(i)
+        for i in order:
+            key[i] = max([key[i]] + [key[d] + 0.01 for d in pre[i]])
+        return sorted(range(n), key=lambda i: key[i])
+
+    for sweep in range(SWEEPS):
+        heat = HEAT * (1 - sweep / SWEEPS) ** 2
+        for lo in range(-int(draw() * STRETCH / 2), n, STRETCH // 2):
+            hi, lo = min(n, lo + STRETCH), max(lo, 0)
+            part, inside, rest, frees = turn[lo:hi], set(turn[lo:hi]), [], []
+            for (ns, needs, gives), end in zip(cases, ends):
+                free, tail, after = [0.0] * 6, [0.0] * n, [0.0] * 6
+                replay(turn[:lo], ns, needs, end, free)
+                replay(turn[:hi - 1:-1], ns, gives, tail, after)
+                frees.append(free)
+                rest.append(([(i, max([w + tail[k] for k, w in gives[i] if k not in inside] + [0.0])) for i in part], after))
+            rest = [([x for x in out if x[1]], after) for out, after in rest]
+
+            def cost(part, a, limit):
+                total, ways, new, last = 0.0, [], [], {eng[i]: i for i in part[:a]}
+                for c, ((ns, needs, gives), end, free, (out, after)) in enumerate(zip(cases, ends, frees, rest)):
+                    free, end = [end[last[e]] if e in last else x for e, x in enumerate(free)], end[:]
+                    replay(part[a:], ns, needs, end, free)
+                    far = [end[i] + w for i, w in out] + [x + y for x, y in zip(free, after)]
+                    ways.append(max(far))
+                    new.append(end)
+                    total += ways[-1] + SLACK * sum(far) / len(far)
+                    if limit and ways[-1] > limit[c]:
+                        return None
+                return total / len(cases), ways, new
+
+            def held(part, ways):
+                c = int(draw() * len(cases))
+                (ns, needs, gives), end, (out, after) = cases[c], ends[c], rest[c]
+                place, before, last = {i: p for p, i in enumerate(part)}, {}, [None] * 6
+                for i in part:
+                    before[i], last[eng[i]] = last[eng[i]], i
+                at_end = [i for i, w in out if end[i] + w > ways[c] - 1] + [i for e, i in enumerate(last) if i is not None and end[i] + after[e] > ways[c] - 1]
+                i, pairs = at_end[0] if at_end else None, []
+                while i is not None:
+                    start, d = end[i] - ns[i] - 1, before[i]
+                    if d is not None and end[d] > start:
+                        if not above[i] >> d & 1:
+                            pairs.append((place[d], place[i]))
+                        i = d
+                    else:
+                        i = ([d for d, w in needs[i] if d in place and end[d] + w > start] + [None])[0]
+                return pairs
+
+            now, ways, ends[:] = cost(part, 0, None)
+            pairs = held(part, ways)
+            for _ in range(MOVES):
+                if pairs and draw() < 0.7:
+                    a, b = pairs[int(draw() * len(pairs))]
+                    far = int(draw() ** 2 * REACH)
+                    a, b = (max(a - far, 0), b) if draw() < 0.5 else (a, min(b + far, len(part) - 1))
+                else:
+                    a = int(draw() * (len(part) - 1))
+                    b = min(a + 1 + int(draw() * REACH), len(part) - 1)
+                seg = part[a:b + 1]
+                if draw() < 0.5:
+                    bits = above[seg[-1]] | 1 << seg[-1]
+                    moved = [i for i in seg if bits >> i & 1] + [i for i in seg if not bits >> i & 1]
+                else:
+                    moved = [i for i in seg[1:] if not above[i] >> seg[0] & 1] + seg[:1] + [i for i in seg if above[i] >> seg[0] & 1]
+                other = seg[-1] if draw() < 0.5 else seg[0]
+                other = other if free_to_move[other] and draw() < FLIPS else None
+                if other is not None:
+                    flip(other)
+                    moved = seg if draw() < 0.5 else moved
+                elif moved == seg:
+                    continue
+                tried = part[:a] + moved + part[b + 1:]
+                more = heat * draw() ** 3
+                then = cost(tried, a, [x + 2 * more + 150 for x in ways])
+                if then and then[0] <= now + more:
+                    part, (now, ways, ends[:]) = tried, then
+                    pairs = held(part, ways)
+                elif other is not None:
+                    flip(other)
+            turn[lo:hi] = part
+        replay(turn, cases[0][0], cases[0][1], ends[0], [0.0] * 6)
+        place = {i: p for p, i in enumerate(turn)}
+        turn.sort(key=lambda i: (ends[0][i] - cases[0][0][i], place[i]))
+        if sweep % COPY == COPY - 1 and sweep + 2 < SWEEPS:
+            turn = alike(turn)
+    return [jobs[i][0] for i in range(n) if free_to_move[i] and eng[i] == 1], [j for i in turn for j in jobs[i]]
 
 
 def emit(g, T, ops):
@@ -287,7 +427,7 @@ def rank_program(g, core, T, topo):
     def width(x):
         return len(x[1]) if x[2] is None else 16 * len(x[2][1])
 
-    def add(e, fn, w, r, ns, lat=0.0, sem=None, remote=False):
+    def add(e, fn, w, r, ns, lat=0.0, sem=None, remote=False, other=None):
         r = [x for x in r if isinstance(x, (tuple, str))]
         r += [x[2] for x in r + w if isinstance(x, tuple) and x[2] is not None]
         rd = set(c for x in r for c in cells(x))
@@ -295,11 +435,11 @@ def rank_program(g, core, T, topo):
         deps = set(last[c] for c in rd | wr if c in last)
         for c in wr:
             deps.update(readers.get(c, ()))
-        for x in r:
-            if isinstance(x, tuple) and psum(x):
-                deps.update(j for j in readers.get(x[0], ()) if ops[j]["e"] != e)
+        turns = set(j for x in r if isinstance(x, tuple) and psum(x) for j in readers.get(x[0], ())
+                    if ops[j]["e"] != e or other or ops[j]["other"]) - deps
         n = len(ops)
-        ops.append({"e": e, "fn": fn, "deps": deps, "sem": sem, "ns": ns, "lat": lat})
+        ops.append({"e": e, "fn": fn, "deps": deps | turns, "turns": turns, "sem": sem, "ns": ns if isinstance(ns, tuple) else (ns, 0, 0),
+                    "lat": lat, "other": other})
         if not remote:
             for c in rd:
                 readers.setdefault(c, []).append(n)
@@ -309,22 +449,37 @@ def rank_program(g, core, T, topo):
 
     def took(fixed, out, ins, each=1.0):
         if out[2] is not None:
-            return fixed + width(out) * SCATTER * CYC
+            return fixed, 0, width(out) * SCATTER * CYC
         if any(x[2] is not None for x in ins):
-            return fixed + width(out) * GATHER * CYC
+            return fixed, width(out) * GATHER * CYC, 0
         if each == 1.0 and fixed == 50 and all(SCRATCH[x[0]][2] in (B, HF, U) for x in [out] + ins):
             each = 0.5
-        return max(64, width(out) * each) * CYC + (fixed > 65) * 20
+        return max(64, width(out) * each) * CYC + (fixed > 65) * 20, 0, 0
 
-    def ts(out, a, s1, s2, op0, op1=None):
+    def ts(out, a, s1, s2, op0, op1=None, other=None):
+        if other is None and (op0, op1) in ((OP.add, None), (OP.mult, None), (OP.mult, OP.add)) and SCRATCH[out[0]][2] != I:
+            return either(out, a, bias=s1 if op0 == OP.add else s2 or 0.0, scale=s1 if op0 == OP.mult else 1.0)
         more = () if op1 is None else (op1,)
-        add("v", lambda: vec.tensor_scalar(ap(out), ap(a), ap(s1), ap(s2), op0, *more), [out], [a, s1, s2], took(50, out, [a]))
+        add("v", lambda: vec.tensor_scalar(ap(out), ap(a), ap(s1), ap(s2), op0, *more), [out], [a, s1, s2], took(50, out, [a]), other=other)
+
+    def either(out, a, func=AF.Identity, bias=0.0, scale=1.0):
+        other = (lambda: act.activation(ap(out), ap(a), func, bias=ap(bias), scale=ap(scale)), took(65, out, [a]))
+        if func == AF.Sign:
+            ts(out, a, -1.0, 1.0, OP.max, OP.min, other)
+        elif func == AF.Relu:
+            ts(out, a, 0.0, scale, OP.min, OP.mult, other)
+        elif scale == 1.0:
+            ts(out, a, bias, None, OP.add, None, other)
+        else:
+            ts(out, a, scale, bias, OP.mult, OP.add, other)
 
     def tt(out, a, b, op):
         add("v", lambda: vec.tensor_tensor(ap(out), ap(a), ap(b), op), [out], [a, b],
             took(50, out, [a, b], 1.01 if psum(a) or psum(b) else 2.0))
 
     def cp(out, a, more=()):
+        if out[2] is None:
+            return either(out, a)
         add("v", lambda: vec.tensor_copy(ap(out), ap(a)), [out], [a] + list(more), took(50, out, [a]))
 
     def scan(out, keep, a):
@@ -334,7 +489,9 @@ def rank_program(g, core, T, topo):
         add("v", lambda: vec.memset(ap(out), val), [out], [], took(50, out, []))
 
     def ac(out, a, func=AF.Identity, bias=0.0, scale=1.0, acc=None):
-        if acc is None:
+        if acc is None and func == AF.Identity:
+            either(out, a, func, bias, scale)
+        elif acc is None:
             add("s", lambda: act.activation(ap(out), ap(a), func, bias=ap(bias), scale=ap(scale)), [out], [a, bias, scale], took(65, out, [a]))
         else:
             add("s", lambda: act.activation(ap(out), ap(a), func, bias=ap(bias), scale=ap(scale), accum_out=ap(acc)),
@@ -376,7 +533,7 @@ def rank_program(g, core, T, topo):
         add("g", lambda: g.remote_dma(ap(out), ap(a), T.sem[sem], T.sem.sent, pid, rid, topo.mask(core, dst)), [], [a],
             ISSUE, -WAKE, remote=True)
         sends[sem] = len(ops)
-        ops.append({"e": "w", "deps": {len(ops) - 1}, "ns": 128 / ways * (ROW_NS + nbytes / LINK), "lat": HOP})
+        ops.append({"e": "w", "deps": {len(ops) - 1}, "turns": (), "ns": (128 / ways * (ROW_NS + nbytes / LINK), 0, 0), "lat": HOP, "other": None})
 
     def lands(place, sem, frm):
         for c in cells(place):
@@ -403,7 +560,7 @@ def rank_program(g, core, T, topo):
         return at("l_lt", lo + c0, lo + c1)
 
     def back_parts(t):
-        return [(256 * t + 64 * a, 256 * t + 64 * b, "a_e%d_%d" % (t, a)) for a, b in BACK]
+        return [(256 * t + 16 * c0, 256 * t + 16 * c1, "a_e%d_%d" % (t, b)) for b, (c0, c1) in enumerate(BLOCKS)]
 
     for t in range(NSTEP):
         lands(at("x", XW * t, XW * t + 8), "a_x%d" % t, verifier(t - 1, drafter(t)) if t else drafter(0))
@@ -411,7 +568,7 @@ def rank_program(g, core, T, topo):
         for j, (c0, c1, lo) in enumerate(tiles(t)):
             lands(at("l_lt", lo, lo + c1 - c0), "a_lt%d_%d" % (t, j), drafter(t))
         if t < LAST:
-            lands(at("l_j", 4 * t, 4 * t + 4), "a_e%d_4" % t, verifier(t))
+            lands(at("l_j", 4 * t, 4 * t + 2), "a_e%d_4" % t, verifier(t))
             for lo, hi, sem in back_parts(t):
                 lands(at("l_e", lo, hi), sem, verifier(t))
     lands(at("l_y", 0, CUT), "a_y0", verifier(LAST))
@@ -419,7 +576,7 @@ def rank_program(g, core, T, topo):
     lands(at("l_f"), "a_f", verifier(LAST))
     lands(at("l_j", 12, 16), "a_r", verifier(LAST - 1, drafter(LAST)))
 
-    (C_I, C_0, C_TK, C_UC, C_UT, C_KB, C_S, C_Q, C_IX, C_NK, C_JK, C_T, C_EV, C_OD, C_PM, C_R, C_J2) = range(17)
+    (C_I, C_0, C_TK, C_UC, C_UT, C_KB, C_S, C_Q, C_IX, C_NK, C_JK, C_T, C_EV, C_OD, C_PM, C_R, C_J2, C_B) = range(18)
     C_K2, C_MID, C_LOSE, C_PAD = 20, 24, 32, 36
     K_A, K_S4, K_TH, K_PM, K_NC, K_R, K_DMK = 0, 20, 24, 40, 56, 76, 92
     B_15, B_3, B_NC, B_S, B_SH, B_H = 0, 36, 56, 76, 80, 144
@@ -439,7 +596,6 @@ def rank_program(g, core, T, topo):
 
     ms(at("tk"), 0)
     ms(at("xi", 4, 8), 0.0)
-    ms(at("xs"), 0.0)
     dma("s", T.xi[:, 0:4], T.x0[:], "d_x", [at("xi", 0, 4)], [])
     dma("s", T.kp[:, 0:1], T.kap[:], "d_kp", [at("kp", 0, 1)], [])
     dma("y", T.tk[0:128:16, :], T.tok[:], "d_tk", [at("tk")], [])
@@ -463,7 +619,7 @@ def rank_program(g, core, T, topo):
         ts(at("runs", 160 * j + 160, 160 * j + 320), at("ab", 160 * j, 160 * j + 160), ln / 2, None, OP.is_lt)
     cp(at("rowx", 0, 16), at("i64", 0, 16))
     table("rowx", 16, ROW[16:48])
-    table("rowx", 48, ROW[40:64] + [0] * 8)
+    table("rowx", 48, ROW[START[3]:] + [0] * (START[3] - 32))
     iota(at("cst", K_A, K_A + 4), [[0, 4]], 0)
     iota(at("cst", K_A + 4, K_A + 20), [[32, 2], [0, 4], [16, 2]], 16)
     ts(at("lst", L_UC, L_UC + 20), at("cst", K_A, K_A + 20), cc(C_I), None, OP.add)
@@ -495,7 +651,7 @@ def rank_program(g, core, T, topo):
     def pe_parents(src, init, depth, up, lo, bank="p0"):
         group([(at(bank, lo, lo + 8), ident, at(init, lo, lo + 8))]
               + [(at(bank, lo + h, lo + 8, 2), run(first, ln), node(src, p))
-                 for p, h, first, ln in runs_of(depth, up, FIRST if up > 1 else START)])
+                 for p, h, first, ln in runs_of(depth, up, FIRST if up > 1 else USED)])
 
     def pe_nodes(src, init, bank="p0"):
         group([(at(bank, 0, 20), ident, at(init, 0, 20))] + [(at(bank, 0, 20), run(i, 1), at(src, i, 320, 16)) for i in range(16)])
@@ -527,11 +683,6 @@ def rank_program(g, core, T, topo):
     ts(at("pi", 4, 5), at("pi", 1, 2), 2, None, OP.logical_shift_right)
     cp(cc(C_S), at("pi", 3, 4))
     cp(cc(C_Q), at("pi", 4, 5))
-    iota(at("cst", K_TH, K_TH + 16), [[0, 4], [16, 4]], 0)
-    ts(at("lst", L_TH, L_TH + 16), at("cst", K_TH, K_TH + 16), cc(C_I), None, OP.add)
-    ts(at("lst", L_TH0, L_TH0 + 16), at("cst", K_TH, K_TH + 16), cc(C_I), 8.0, OP.add, OP.add)
-    ts(cc(C_R), cc(C_I), 4.0, 8.0, OP.is_ge, OP.mult)
-    ts(at("lst", L_TH0, L_TH0 + 16, 4), at("cst", K_TH, K_TH + 16, 4), cc(C_I), cc(C_R), OP.add, OP.add)
     table("rows", 0, [p and p + 2 for p in PAR])
     group([(at("p3", 0, 16), run(4 * r, 4), at("rows", r, 64, 4)) for r in range(4)])
     ts(at("lst", L_PAR, L_PAR + 16), at("p3", 0, 16), 0.25, cc(C_S), OP.mult, OP.add)
@@ -544,11 +695,26 @@ def rank_program(g, core, T, topo):
     ts(at("pi", 2, 3), at("pi", 0, 1), 4, 1, OP.logical_shift_right, OP.bitwise_and)
     cp(cc(C_OD), at("pi", 2, 3))
     ac(cc(C_EV), cc(C_OD), bias=1.0, scale=-1.0)
-    ac(at("ide"), at("idw"), scale=cc(C_EV))
-    ac(at("ido"), at("idw"), scale=cc(C_OD))
-    ac(cc(C_PM), cc(C_S), bias=cc(C_Q), scale=16.0)
-    iota(at("cst", K_PM, K_PM + 16), [[64, 4], [4, 4]], 0)
-    ts(at("lst", L_PM, L_PM + 16), at("cst", K_PM, K_PM + 16), cc(C_PM), None, OP.add)
+    if "t" in TURN:
+        ts(cc(C_R), cc(C_OD), -16.0, cc(C_I), OP.mult, OP.add)
+        ac(cc(C_R), cc(C_R), bias=1.0)
+        ts(at("ide", 0, 129), at("xq", 0, 129), cc(C_R), cc(C_EV), OP.is_equal, OP.mult)
+        ts(at("ido", 0, 129), at("xq", 0, 129), cc(C_R), cc(C_OD), OP.is_equal, OP.mult)
+    ts(at("pi", 5, 6), at("pi", 0, 1), 1, None, OP.bitwise_and)
+    cp(cc(C_B), at("pi", 5, 6))
+    for w in sorted(set(c1 - c0 for (c0, c1), how in zip(BLOCKS, TURN) if how == "v")):
+        if w == 4:
+            ac(cc(C_PM), cc(C_S), bias=cc(C_Q), scale=16.0)
+        else:
+            ts(cc(C_PM), cc(C_B), 15.5, None, OP.mult)
+            ac(cc(C_PM), cc(C_I), bias=cc(C_PM), scale=0.5)
+        ts(cc(C_T), cc(C_B), cc(C_OD), 16.0 * w + 16, OP.not_equal, OP.mult)
+        tt(cc(C_PM), cc(C_PM), cc(C_T), OP.add)
+        ts(at("lst", L_PM + w, L_PM + 2 * w), at("i64", 0, w), 16.0 / w, cc(C_PM), OP.mult, OP.add)
+    for b, (c0, c1) in enumerate(BLOCKS):
+        if TURN[b] == "v":
+            for c in (c0 - 1, c1):
+                ms(at("cf", 16 * c + 32 * b + 16, 16 * c + 32 * b + 32), 0.0)
     ac(cc(C_NK), at("kp", 0, 1), scale=-1.0)
     iota(at("fmi"), [[-1, 128]], 128, 1)
     ts(at("fmi"), at("fmi"), 15, None, OP.bitwise_and)
@@ -568,12 +734,13 @@ def rank_program(g, core, T, topo):
     ac(cc(C_KB), cc(C_I), bias=-128.0, scale=-1.0)
     ac(at("runh"), at("runs", 0, 160), scale=0.5)
     ac(mat("negf"), ident, scale=-1.0)
-    for c in range(4):
-        mine = [kq for b, kq in SHARE if b == c]
-        for j, kq in enumerate(mine):
-            ts(cc(C_T), cc(C_Q), float(kq), 128.0, OP.is_equal, OP.mult)
-            tt(cc(C_K2 + c), cc(C_K2 + c if j else C_KB), cc(C_T), OP.add)
-    ms(at("cb", B_SH, B_SH + 64), -15.0)
+    signed = [sum(m for m, bank in calls if bank is None) for calls in CALLS]
+    for first in set(signed) - {16}:
+        ts(cc(C_T), cc(C_I), float(first), 128.0, OP.is_ge, OP.mult)
+        tt(cc(C_K2 + signed.index(first)), cc(C_KB), cc(C_T), OP.add)
+    ms(at("sh"), -15.0)
+    for bank in LAID:
+        mm(at(bank), ident, at("dm", 0, 512), True, True)
     iota(at("cst", K_R, K_R + 8), [[-1, 8]], 15)
     ts(at("cst", K_R + 8, K_R + 16), at("cst", K_R, K_R + 8), cc(C_I), None, OP.is_le)
     tt(at("cst", K_R + 8, K_R + 16), at("cst", K_R + 8, K_R + 16), at("cst", K_R, K_R + 8), OP.mult)
@@ -589,6 +756,7 @@ def rank_program(g, core, T, topo):
     ac(mat("onew"), ones, scale=65536.0)
     ac(mat("negw"), ident, scale=-131072.0)
     keep(mat("upper"), ones, [[-1, 128]], OP.is_gt, 0.0)
+    keep(mat("upper"), mat("upper"), [[-1, 128]], OP.not_equal, -1.0)
     ms(at("cb", B_15, B_15 + 20), 15.0 * H)
     ms(at("cb", B_3, B_3 + 12), 0.0)
     ms(at("cb", B_3 + 12, B_3 + 20), 15.0 * H)
@@ -598,38 +766,49 @@ def rank_program(g, core, T, topo):
     ts(at("cst", K_NC, K_NC + 20), at("cst", K_NC, K_NC + 20), cc(C_I), -1.0 / 256, OP.add, OP.mult)
     ac(at("cb", B_NC, B_NC + 20), at("cst", K_NC, K_NC + 20), bias=1.0)
     iota(at("cst", K_S4, K_S4 + 4), [[1, 4]], 0)
-    ac(at("cb", B_S, B_S + 4), at("cst", K_S4, K_S4 + 4), scale=0.25)
+    iota(at("cst", K_PM, K_PM + 4), [[0, 2], [1, 2]], 0)
+    ts(at("cst", K_PM, K_PM + 4), at("cst", K_PM, K_PM + 4), cc(C_B), -1024.0, OP.not_equal, OP.mult)
+    tt(at("cst", K_PM, K_PM + 4), at("cst", K_PM, K_PM + 4), at("cst", K_S4, K_S4 + 4), OP.add)
+    ac(at("cb", B_S, B_S + 4), at("cst", K_PM, K_PM + 4), scale=0.25)
     iota(at("cst", K_DMK, K_DMK + 12), [[0, 3], [1, 4]], 0)
-    ts(at("diag"), at("i64", 0, 64), cc(C_I), None, OP.is_equal)
+    ts(at("diag", 0, 16), at("i64", 0, 16), cc(C_I), None, OP.is_equal)
+    ms(at("cb", B_H, B_H + 64), float(H))
     ac(at("tie"), at("i64"), bias=15.0 * 4096, scale=-4096.0)
     cp(at("lst", L_REP, L_REP + 4), at("cst", K_S4, K_S4 + 4))
     ts(at("cst", K_DMK, K_DMK + 12), at("cst", K_DMK, K_DMK + 12), cc(C_S), None, OP.is_equal)
     ts(cc(C_IX), cc(C_Q), 1.0, 16.0, OP.is_equal, OP.mult)
     tt(cc(C_IX), cc(C_IX), cc(C_S), OP.add)
 
-    def top_of(out, entries, places):
-        ts(out, ind(entries, places), cc(C_UT), float(H), OP.add, OP.min)
+    def tops(entries, t, o):
+        for (lo, hi), bank in zip(TOPS, COUNT):
+            ts(at("ut", o + lo, o + hi), at(entries, 256 * t + lo, 256 * t + hi), cc(C_UT), float(H), OP.add, OP.min)
+            mm(at(bank, lo, hi), ones, at("ut", o + lo, o + hi), True, True)
+            ac(at("tb", o + lo, o + hi), at(bank, lo, hi), bias=-14.0 * H)
+        return at("tb", o, o + 256)
 
     def root(t):
         if t:
-            top_of(at("u", 320, 384), at("l_e", 256 * t - 256, 256 * t), at("l_j", 4 * t - 4, 4 * t))
-        pe_root("u", "ct0")
-        cp(at("rt"), at("p0", 44, 48))
-        if t:
-            ac(at("ytb", 4 * t - 4, 4 * t), at("p0", 44, 48))
+            picked = ind(tops("l_e", t - 1, 0), at("l_j", 4 * t - 4, 4 * t - 2))
+            cp(at("rt"), picked)
+            cp(at("rf"), picked)
+            ts(at("u", 320, 384, 16), at("rf", MID, MID + 4), cc(C_TK), float(H), OP.add, OP.min)
+            ac(at("ytb", 4 * t - 4, 4 * t), at("rf", MID, MID + 4))
+        else:
+            pe_root("u", "ct0")
+            cp(at("rt", MID, MID + 4), at("p0", 44, 48))
 
     def draft(t):
         win = at("a", 0, V) if t else at("q")
         for level, (c0, c1, place) in enumerate(tiles(t)):
             lo, hi = UCOL[level + 1], UCOL[level + 1] + 4 * USTEP[level + 1]
-            tile = at("pl", 8 * level - 8, 8 * level) if level else at("rt")
+            tile = at("pl", 8 * level - 8, 8 * level) if level else at("rt", MID, MID + 4)
             tt(at("w", lo, hi), ind(win, tile), at("uc", lo, hi), OP.subtract)
             ts(at("u", lo, hi), at("w", lo, hi), -float(H), float(H), OP.max, OP.min)
             if level < 2:
                 pe_parents("u", "ct0", level + 2, 1, 20 + 8 * level)
                 cp(at("pl", 8 * level, 8 * level + 8), at("p0", 20 + 8 * level, 28 + 8 * level))
             pe_tile(c0, c1, level + 1)
-            cp(at("ls", place, place + c1 - c0), at("p1", c0, c1))
+            ac(at("ls", place, place + c1 - c0), at("p1", c0, c1))
             send(verifier(t), at("l_lt", place, place + c1 - c0), at("ls", place, place + c1 - c0), "a_lt%d_%d" % (t, level))
         pe_parents("u", "ct0", 3, 2, 36)
         pe_nodes("u", "ct0")
@@ -665,75 +844,97 @@ def rank_program(g, core, T, topo):
         return at(name, base + 16 * c0, base + 16 * c1)
 
     def states(t):
-        for c0, c1 in BLOCKS if t < LAST else STATES_LAST:
+        o = XW * t
+        for c0, c1 in STATES if t < LAST else STATES_LAST:
             known = max(PAR[4 * c0:4 * c1])
-            o = XW * t
             win = at("x", o, o + (4 * known + 12 if c0 else 4))
             ac(cols("ph", c0, c1), ind(win, at("lst", L_PAR + c0, L_PAR + c1)), scale=0.5)
             tt(cols("x", c0, c1, o + 8), ind(at("k"), tokens(t, c0, c1)), cols("ph", c0, c1), OP.add)
-            if t < LAST:
-                win, first = (cols("x", c0, c1, o + 8), L_TH) if c0 else (at("x", o, o + 72), L_TH0)
-                ac(at("th", 64 * c0, 64 * c1), ind(win, at("lst", first, first + 16)), bias=cc(C_NK))
             if c0 == 0:
                 ac(at("x", o + 8, o + 12), at("x", o, o + 4))
 
-    def prepare(t):
-        done = 0
-        for c0, c1 in PREP:
-            ts(cols("cd", c0, c1), ind(at("q"), tokens(t, c0, c1)), -float(H), None, OP.add)
-            for c in range(c0, c1, 2):
-                for h, src in enumerate(("ide", "ido")):
-                    group([(cols("p2", c + h, c + h + 1), at(src, 16 + 16 * (h - to), 144 + 16 * (h - to)), cols("cd", c + to, c + to + 1))
-                           for to in range(2)])
-            out, a = cols("tr", c0, c1), cols("p2", c0, c1)
-            add("v", lambda out=out, a=a: vec.transpose(ap(out), ap(a)), [out], [a], took(50, out, [a]))
-            end = c1 // 4 * 4
-            ts(cols("ct", done, end), ind(cols("tr", 0, end), at("lst", L_PM + done, L_PM + end)), float(H), None, OP.add)
-            done = end
+    def bounds(t, b):
+        (c0, c1), o = BLOCKS[b], XW * t
+        for r in range(max(m for m, bank in CALLS[b])):
+            lo = 128 * c0 + 16 * (c1 - c0) * r
+            if c0:
+                ac(at("th", lo, lo + 16 * (c1 - c0)), cols("x", c0, c1, o + 8), bias=cc(C_NK))
+            else:
+                ac(at("th", lo, lo + 4), at("x", o, o + 4), bias=cc(C_NK))
+                ac(at("th", lo + 4, lo + 16 * c1), at("x", o + 12, o + 8 + 16 * c1), bias=cc(C_NK))
 
-    def votes(b, kq):
-        o, bank = 1024 * (b % 2) + 256 * kq, "p%d" % (3 + b % 2)
-        numbers, th = ind(at("k"), at("ct", 64 * b + 16 * kq, 64 * b + 16 * kq + 16)), at("th", 256 * b, 256 * b + 256)
-        if (b, kq) in SHARE:
-            kc = at("kc", 256 * (kq % 2), 256 * (kq % 2) + 256)
-            ac(kc, numbers)
-            group([(at("p0", 256, 512), mat("negf"), th), (at("p0", 256, 512), ident, kc)])
-            ac(at("ge", o, o + 256), at("p0", 256, 512), AF.Sign, 2.0 ** -100)
-        else:
-            tt(at("ge", o, o + 256), numbers, th, OP.is_ge)
-        for kk in range(4):
-            k = 4 * kq + kk
-            mm(at(bank, 0, 64), run(k, 1, "runh" if (b, kq) in SHARE else "runs"), at("ge", o + 64 * kk, o + 64 * kk + 64), k == 0, k == 15)
+    def turn(out, a):
+        add("v", lambda: vec.transpose(ap(out), ap(a)), [out], [a], took(50, out, [a]))
+
+    def cands(b):
+        c0, c1 = BLOCKS[b]
+        return cols("cd", c0, c1) if TURN[b] == "t" else cols("cf", c0, c1, 32 * b + 16)
+
+    def prepare(t, b):
+        c0, c1 = BLOCKS[b]
+        w, picked, scale = c1 - c0, ind(at("q"), tokens(t, c0, c1)), 1.0 if TURN[b] == "t" else 2.0 / R
+        ac(cands(b), picked, bias=-H * scale, scale=scale)
+        if TURN[b] == "v":
+            o = 32 * c0 + 32 * b
+            turn(at("tw", o, o + 16 * w), cands(b))
+            turn(at("tw", o + 16 * w, o + 32 * w + 32), cols("cf", c0 - 1, c1 + 1, 32 * b + 16))
+            ts(cols("ct", c0, c1), ind(at("tw", o, o + 32 * w + 32), at("lst", L_PM + w, L_PM + 2 * w)), R / 2.0, float(H), OP.mult, OP.add)
+            return
+        for j in range(w // 2):
+            for h, src in enumerate(("ide", "ido")):
+                group([(cols("p2", c0 + 2 * j + h, c0 + 2 * j + h + 1), at(src, 1 - to, 129 - to),
+                        cols("cd", c0 + j + to * w // 2, c0 + j + to * w // 2 + 1)) for to in range(2)])
+        turn(cols("tr", c0, c1), cols("p2", c0, c1))
+        for j in range(w // 2):
+            ts(at("ct", 16 * c0 + j, 16 * c1, w // 2), cols("tr", c0 + 2 * j, c0 + 2 * j + 2), float(H), None, OP.add)
+
+    def votes(b):
+        c0, c1 = BLOCKS[b]
+        w, n, nxt, done = c1 - c0, 16 * (c1 - c0), {True: 0, False: signed[b]}, 0
+        for m, bank in CALLS[b]:
+            k0 = nxt[bank is None]
+            nxt[bank is None] += m
+            lo, hi = 256 * c0 + n * k0, 256 * c0 + n * (k0 + m)
+            numbers, th = ind(at("k"), at("ct", 16 * c0 + w * k0, 16 * c0 + w * (k0 + m))), at("th", 128 * c0, 128 * c0 + n * m)
+            if bank:
+                diff = at(bank, 512 - n * m, 512)
+                ac(at("kc", lo, hi), numbers)
+                if bank in LAID:
+                    ac(diff, th, scale=-1.0)
+                    mm(diff, ident, at("kc", lo, hi), False, True)
+                else:
+                    group([(diff, mat("negf"), th), (diff, ident, at("kc", lo, hi))])
+                ac(at("ge", lo, hi), diff, AF.Sign, 2.0 ** -100)
+            else:
+                tt(at("ge", lo, hi), numbers, th, OP.is_ge)
+            for k in range(k0, k0 + m):
+                mm(at(COUNT[b], 0, n), run(k, 1, "runh" if bank else "runs"), at("ge", 256 * c0 + n * k, 256 * c0 + n * k + n), done == 0, done == 15)
+                done += 1
 
     def ranks(t, b):
-        key, so = block("key", b), 512 * (b % 2)
-        ac(key, at("p%d" % (3 + b % 2), 0, 64), bias=cc(C_K2 + b if any(c == b for c, _ in SHARE) else C_KB), scale=16.0)
-        for bank, lo, hi in [("p5", 0, 4), ("p6", 4, 8)] if b == 3 else [("p%d" % (5 + b % 2), 0, 8)]:
+        c0, c1 = BLOCKS[b]
+        key, so, n = cols("key", c0, c1), 128 * c0, 16 * (c1 - c0)
+        ac(key, at(COUNT[b], 0, n), bias=cc(C_K2 + signed.index(signed[b]) if signed[b] < 16 else C_KB), scale=16.0)
+        for lo, hi, bank, e in DIFFS[b]:
             for d in range(lo, hi):
-                mm(at(bank, 64 * (d - lo), 64 * (d - lo + 1)), mat("dm", d), key, True, True)
-            if lo:
-                ts(at("sg", so + 64 * lo, so + 64 * hi), at(bank, 0, 64 * (hi - lo)), -1.0, 1.0, OP.max, OP.min)
-            else:
-                ac(at("sg", so + 64 * lo, so + 64 * hi), at(bank, 0, 64 * (hi - lo)), AF.Sign)
-        bank, base = ("p2", 256) if b % 2 else ("p7", 0)
-        out = block(bank, b, base)
-        group([(out, negq, block("cd", b)), (out, ident, at("cb", B_SH, B_SH + 64))]
-              + [(out, mat("dm", 14 - d) if d < 7 else negi, at("sg", so + 64 * d, so + 64 * d + 64)) for d in range(8)])
-        for name, nodes, scale in (("utb", PAR, -1.0), ("uta", [PAR[n] for n in PAR], -float(R))):
-            inner = [4 * n for n in nodes if n // 16 == b]
+                mm(at(bank, n * (d - lo), n * (d - lo + 1)), mat("dm", d), key, True, True)
+            either(at("sg", so + n * lo, so + n * hi), at(bank, 0, n * (hi - lo)), AF.Sign)
+        bank, base = PLACES[b], 256
+        out = cols(bank, c0, c1, base)
+        group([(out, negq if TURN[b] == "t" else mat("negf"), cands(b)), (out, ident, at("sh", 0, n))]
+              + [(out, mat("dm", 14 - d) if d < 7 else negi, at("sg", so + n * d, so + n * d + n)) for d in range(8)])
+        for name, nodes, scale in (("utb", PAR, -1.0), ("uta", [PAR[p] for p in PAR], -float(R))):
+            inner = [4 * p for p in nodes if c0 <= p // 4 < c1]
             if inner:
                 lo, hi = min(inner), max(inner) + 4
                 ts(at(name, lo, hi), at(bank, base + lo, base + hi), -2.0 * H / R, scale, OP.max, OP.mult)
-        if b < 3:
-            ac(block("es", b, 256 * t), out, bias=cc(C_UC), scale=-R / 2.0)
-        else:
-            ts(block("es", b, 256 * t), out, -R / 2.0, cc(C_UC), OP.mult, OP.add)
+        ac(cols("es", c0, c1, 256 * t), out, bias=cc(C_UC), scale=-R / 2.0)
 
     def commit(t):
         o = 48 * t
 
         def dd(lo, hi, step=1):
-            return at("p1", 160 + lo, 160 + hi, step)
+            return at(COMMIT, 160 + lo, 160 + hi, step)
 
         def top(name, n):
             return at(name, 4 * n, 4 * n + 4)
@@ -750,30 +951,29 @@ def rank_program(g, core, T, topo):
         ts(at("m", 0, 20), dd(0, 20), 0.0, None, OP.is_equal)
         later = [((4, 20, 2), (5, 20, 2)), ((0, 4), (4, 12, 2)), ((0, 4), (5, 12, 2)), ((4, 12), (12, 20)), ((4, 12, 2), (13, 20, 2)),
                  ((5, 12, 2), (12, 20, 2))]
-        group([(dd(20, 40), ident, at("cb", B_NC, B_NC + 20)), (dd(20, 40), negi, at("m", 0, 20)), (dd(20, 40), mat("upper"), at("m", 0, 20))]
+        group([(dd(20, 40), ident, at("cb", B_NC, B_NC + 20)), (dd(20, 40), mat("upper"), at("m", 0, 20))]
               + [(dd(20 + a[0], 20 + a[1], *a[2:]), ones, at("m", *b)) for a, b in later])
-        ts(at("one"), dd(20, 40), 0.0, -256.0, OP.min, OP.mult)
+        either(at("one"), dd(20, 40), AF.Relu, scale=-256.0)
         parts = [(0, 4, 1), (4, 12, 2), (5, 12, 2), (12, 20, 2), (13, 20, 2)]
         group([(dd(40, 44), ident, at("cb", B_S, B_S + 4))] + [(dd(40, 44), ones, at("one", *a)) for a in parts])
-        ix = at("ix", 4 * t, 4 * t + 4)
-        ts(ix, dd(40, 44), 4.0, None, OP.mult)
-        send(drafter(t), at("l_j", 4 * t, 4 * t + 4), ix, "a_e%d_4" % t)
-        ac(at("xg"), ind(at("x", XW * t + 8, XW * t + XW), ix))
-        o, to = 8 * t + 8, verifier(t + 1, drafter(t))
-        ac(at("xs", o, o + 4), at("xg", 0, 64, 16))
-        send(to, at("x", XW * t + XW, XW * t + XW + 8), at("xs", o, o + 8), "a_x%d" % (t + 1))
+        ix = at("ix", 4 * t, 4 * t + 2)
+        for j in range(2):
+            ts(at("ix", 4 * t + j, 4 * t + j + 1), dd(40 + 2 * j, 41 + 2 * j), dd(41 + 2 * j, 42 + 2 * j), 4.0, OP.max, OP.mult)
+        send(drafter(t), at("l_j", 4 * t, 4 * t + 2), ix, "a_e%d_4" % t)
+        o, to = 40 * t + 16, verifier(t + 1, drafter(t))
+        ac(at("xg", o - MID, o - MID + 32), ind(at("x", XW * t + 8, XW * t + XW), ix))
+        send(to, at("x", XW * t + XW, XW * t + XW + 8), at("xg", o, o + 8), "a_x%d" % (t + 1))
         if t + 1 == LAST:
-            top_of(at("u0"), at("es", 256 * t, 256 * t + 256), ix)
-            mm(dd(44, 48), ones, at("u0", 0, 64, 16), True, True)
-            ts(at("ix", 16, 20), dd(44, 48), -14.0 * H, None, OP.add)
-            send(to, at("l_j", 12, 16), at("ix", 16, 20), "a_r")
+            cp(at("rq"), ind(tops("es", t, 256), ix))
+            send(to, at("l_j", 12, 16), at("rq", MID, MID + 4), "a_r")
 
     def verify(t):
-        prepare(t)
         states(t)
-        for b in range(4):
-            for kq in range(4):
-                votes(b, kq)
+        for b in range(len(BLOCKS)):
+            prepare(t, b)
+            bounds(t, b)
+        for b in range(len(BLOCKS)):
+            votes(b)
             ranks(t, b)
         commit(t)
         for lo, hi, sem in back_parts(t):
@@ -793,19 +993,19 @@ def rank_program(g, core, T, topo):
                 if d < 3:
                     ac(block("xrh", d), block("xr", d), scale=0.5)
             ts(at("c16", 4 * d, 4 * d + 4), at("g1", lo, hi, 16), float(H), None, OP.add)
-            tt(block("dg", d), block("g1", d), at("diag"), OP.mult)
+            for s in range(lo, hi, 16):
+                ac(at("dg", s, s + 16), at("diag", 0, 16), scale=at("g1", s, s + 1))
             tt(block("gec", d), ind(at("k"), at("c16", 4 * d, 4 * d + 4)), block("thr", d), OP.is_ge)
-            group([(at("p3", 0, 128), ident, at("tie")), (at("p3", 0, 64), ones, block("dg", d)),
+            group([(at("p3", 0, 128), ident, at("tie")), (at("p3", 0, 64), ident, at("cb", B_H, B_H + 64)), (at("p3", 0, 64), ones, block("dg", d)),
                    (at("p3", 0, 64), mat("onew"), block("gec", d)), (at("p3", 64, 128), mat("onew"), block("gec", d))])
             scan(at("zs", 2 * lo, 2 * hi), at("rst"), at("p3", 0, 128))
-            for s in range(4):
-                out = at("ctl", 4 * d + 4 + s, 4 * d + 5 + s) if d < 3 else at("cs", 28 + s, 29 + s)
+            for s in range(4 if d < 3 else 0):
                 z = 2 * lo + 16 * s + 15
-                ts(out, at("zs", z, z + 1), at("zs", z + 64, z + 65), float(H), OP.subtract, OP.add)
+                ac(at("ctl", 4 * d + 4 + s, 4 * d + 5 + s), at("zs", z + 64, z + 65), bias=at("zs", z, z + 1), scale=-1.0)
+            tt(at("cs", 16 + 4 * d, 20 + 4 * d), at("zs", 2 * lo + 15, 2 * lo + 64, 16), at("zs", 2 * lo + 79, 2 * hi, 16), OP.subtract)
             if d < 3:
-                tt(at("cs", 32 + 4 * d, 36 + 4 * d), at("zs", 2 * lo + 15, 2 * lo + 64, 16), at("zs", 2 * lo + 79, 2 * hi, 16), OP.subtract)
+                ac(at("cs", 32 + 4 * d, 36 + 4 * d), at("cs", 16 + 4 * d, 20 + 4 * d), bias=-float(H))
         ac(at("cs", 4, 16), at("xr", 64, 256, 16))
-        ac(at("cs", 16, 28), at("cs", 32, 44), bias=float(H))
         o = 48 * LAST
         tt(at("m"), ind(at("cs", 32, 40), at("lst", L_CMP, L_CMP + 3)), at("l_ct", o, o + 48), OP.is_equal)
         tt(at("pp", 0, 8), at("m", 4, 12), at("m", 20, 28), OP.mult)
@@ -823,21 +1023,32 @@ def rank_program(g, core, T, topo):
         cp(at("fin"), ind(at("cs", 0, 32), at("ix", 12, 13)))
         send(drafter(LAST), at("l_f"), at("fin", 0, 8), "a_f")
 
+    def results():
+        dma("s", T.yt[:, 0:12], T.ytb[0:128:16, :], "d_yu", ["yu"], [at("ytb")])
+        for j, (lo, hi) in enumerate(((0, CUT), (CUT, 256))):
+            send(drafter(LAST), at("l_y", lo, hi), at("x", XW * LAST + 8 + lo, XW * LAST + 8 + hi), "a_y%d" % j)
+            dma("y", T.yn[:, lo:hi], T.l_y[:, lo:hi], "d_y%d" % j, ["y%d" % j], [at("l_y", lo, hi)], 128 * 4 * (hi - lo))
+        dma("s", T.yx[:], T.l_f[:, 0:4], "d_yx", ["yx"], [at("l_f")])
+        dma("s", T.yt[:, 12:16], T.l_f[0:128:16, 4:8], "d_yt", ["yt"], [at("l_f")])
+        add("g", None, [], ["yx", "yt", "yu", "y0", "y1"], 50)
+
+    def part(t, name, fn, *args):
+        first = len(ops)
+        fn(*args)
+        for j in range(first, len(ops)):
+            ops[j]["tag"] = (t, name, j - first)
+
+    for op in ops:
+        op["tag"] = (None, None, None)
     for t in range(NSTEP):
-        root(t)
-        draft(t)
+        part(t, "root" if t else "start", root, t)
+        part(t, "draft", draft, t)
         if t < LAST:
-            twins()
-            verify(t)
-            overwrite(t)
-    chain()
-    states(LAST)
-    dma("s", T.yt[:, 0:12], T.ytb[0:128:16, :], "d_yu", ["yu"], [at("ytb")])
-    for j, (lo, hi) in enumerate(((0, CUT), (CUT, 256))):
-        send(drafter(LAST), at("l_y", lo, hi), at("x", XW * LAST + 8 + lo, XW * LAST + 8 + hi), "a_y%d" % j)
-        dma("y", T.yn[:, lo:hi], T.l_y[:, lo:hi], "d_y%d" % j, ["y%d" % j], [at("l_y", lo, hi)], 128 * 4 * (hi - lo))
-    dma("s", T.yx[:], T.l_f[:, 0:4], "d_yx", ["yx"], [at("l_f")])
-    dma("s", T.yt[:, 12:16], T.l_f[0:128:16, 4:8], "d_yt", ["yt"], [at("l_f")])
-    add("g", None, [], ["yx", "yt", "yu", "y0", "y1"], 50)
+            part(t, "twins", twins)
+            part(t, "verify", verify, t)
+            part(t, "overwrite", overwrite, t)
+    part(LAST, "chain", chain)
+    part(LAST, "states", states, LAST)
+    part(LAST, "results", results)
     emit(g, T, arrange(ops, sends))
     g.wait_ge(T.sem.sent, sent[0])

from concourse.mybir import AluOpType as OP, ActivationFunctionType as AF

V = 2304
H = V // 2
R = 4096
NSTEP = 4
PAR = [0] * 17 + [1] * 8 + [2] * 4 + [3] * 4 + [4] * 4 + [6] * 3 + [9, 9, 13, 13, 16, 16, 17, 17, 17, 17, 18, 18, 19, 19, 20,
                                                                  25, 25, 29, 29, 33, 33, 37, 40, 44]
ROW = [0] + list(range(16)) + list(range(8)) + [0, 1, 8, 9, 0, 2, 10, 11, 0, 3, 12, 13, 0, 14, 15, 0, 5, 0, 6, 0, 15,
                                                0, 1, 2, 3, 0, 4, 0, 5, 0, 0, 1, 0, 7, 0, 14, 0, 0, 0]
DEPTH = [0] * 64
for _n in range(1, 64):
    DEPTH[_n] = DEPTH[PAR[_n]] + 1
FIRST = [DEPTH.index(_d) for _d in range(4)] + [64]
UCOL, USTEP, START, USED = (320, 0, 64, 192), (16, 16, 32, 32), (0, 1, 16, 39), (0, 1, 16, 40)
LENS = (1, 2, 3, 4, 8, 16)
TILES = ((0, 4), (4, 10), (10, 16))
TILES_LAST = ((0, 4), (4, 12), (10, 16))
BLOCKS = ((0, 4), (4, 8), (8, 12), (12, 16))
STATES = BLOCKS
STATES_LAST = ((0, 4), (4, 8), (8, 12), (10, 16))
CALLS = (((4, None), (4, None), (4, None), (4, "p7")), ((4, None), (4, None), (4, None), (4, "p7")),
         ((4, None), (4, None), (4, None), (4, None)), ((4, None), (4, None), (4, None), (4, None)))
TURN = "vttt"
CANDS = "vsss"
COUNT = ("p3", "p4", "p3", "p4")
DIFFS = (((0, 8, "p5", "s"),), ((0, 8, "p6", "s"),), ((0, 4, "p5", "s"), (4, 8, "p2", "s")), ((0, 4, "p7", "s"), (4, 8, "p6", "v")))
PLACES = ("p5", "p6", "p5", "p6")
ENTRY = "sssv"
COMMIT = "p0"
TOPS = ((0, 128), (128, 192), (192, 256))
MID = 14
LAID = ()
XW = 264
LT = 18


def _sb(cols, dtype):
    return ("sbuf", [128, cols], dtype)


F, B, HF, I, U = "float32", "bfloat16", "float16", "int32", "uint16"
SCRATCH = {
    "q": _sb(V, I), "a": _sb(V + 32, I), "k": _sb(V, B), "kp": _sb(4, F), "tk": _sb(4, I), "xi": _sb(8, F),
    "pi": _sb(8, I), "col": _sb(48, F), "xq": _sb(160, F), "ab": _sb(160 * 5, B), "idw": _sb(160, B), "ide": _sb(160, B), "ido": _sb(160, B),
    "runs": _sb(160 * len(LENS), B), "runh": _sb(160, B), "negi": _sb(128, B), "negq": _sb(128, B),
    "negw": _sb(128, B), "negf": _sb(128, F), "onew": _sb(128, B), "upper": _sb(128, B), "fmi": _sb(128, I), "fm": _sb(256, B),
    "shf": _sb(128 * 8, B), "dm": _sb(128 * 15, B), "lose": _sb(128 * 8, B), "rowx": _sb(80, F), "uc": _sb(320, F),
    "cu": _sb(384, B), "zero": _sb(48, B), "hp": _sb(48, F), "neg2": _sb(128, B), "bigi": _sb(128, B), "ct0": _sb(48, B), "ct1": _sb(16, B), "rows": _sb(176, B), "cst": _sb(128, F),
    "cb": _sb(224, B), "lst": _sb(104, U), "i64": _sb(128, F), "diag": _sb(64, F), "rst": _sb(128, B), "tie": _sb(128, B), "sh": _sb(128, B),
    "w": _sb(320, F), "u": _sb(384, HF), "rt": _sb(32, U), "rf": _sb(32, F), "pl": _sb(16, U), "ls": _sb(LT * NSTEP, U),
    "cts": _sb(48 * NSTEP, HF), "t16": _sb(16, HF), "eq": _sb(128, B), "off": _sb(16, U),
    "dl": _sb(8, F), "dr": _sb(128, F), "eq2": _sb(256, B), "ytb": _sb(12, F),
    "cd": _sb(256, HF), "cf": _sb(384, F), "tr": _sb(256, F), "tw": _sb(768, F), "ct": _sb(256, U), "ph": _sb(256, F),
    "x": _sb(XW * NSTEP, F), "th": _sb(2048, F),
    "ge": _sb(4096, B), "kc": _sb(4096, B), "key": _sb(256, B), "sg": _sb(2048, B), "es": _sb(768, F),
    "uta": _sb(80, HF), "utb": _sb(192, HF), "m": _sb(48, B), "one": _sb(20, B), "ix": _sb(16, U), "xg": _sb(120, F),
    "ut": _sb(512, HF), "tb": _sb(512, F), "rq": _sb(32, U),
    "ctl": _sb(16, U), "g1": _sb(256, F), "c16": _sb(16, U), "dg": _sb(256, HF), "xr": _sb(256, F), "xrh": _sb(256, F),
    "thr": _sb(256, F), "gec": _sb(256, B), "zs": _sb(512, F), "cs": _sb(48, F), "pp": _sb(24, B), "vm": _sb(44, F),
    "fin": _sb(16, F),
    "l_lt": _sb(LT * NSTEP, U), "l_j": _sb(16, U), "l_ct": _sb(48 * NSTEP, HF), "l_e": _sb(768, F),
    "l_y": _sb(256, F), "l_f": _sb(8, F),
}
for _b in range(8):
    SCRATCH["p%d" % _b] = ("psum", [128, 512], F)
SEMAPHORES = (["ev", "es_", "et", "eg", "sent", "d_q", "d_k", "d_a", "d_x", "d_kp", "d_tk", "d_yt", "d_yu", "d_yx", "d_y0", "d_y1",
               "a_y0", "a_y1", "a_f", "a_r"]
              + ["a_x%d" % t for t in range(NSTEP)] + ["a_ct%d" % t for t in range(NSTEP)]
              + ["a_lt%d_%d" % (t, j) for t in range(NSTEP) for j in range(3)]
              + ["a_e%d_%d" % (t, c) for t in range(NSTEP - 1) for c in range(5)])
WHOLE = ("q", "a", "k")
ENGINE_SEM = {"v": "ev", "s": "es_", "t": "et", "g": "eg"}


def runs_of(depth, up, first=FIRST):
    out = []
    for n in range(first[depth], FIRST[depth + 1]):
        p, slot = n, n - START[depth]
        for _ in range(up):
            p = PAR[p]
        if out and out[-1][0] == p and out[-1][1] == slot // 16:
            out[-1][3] += 1
        else:
            out.append([p, slot // 16, slot % 16, 1])
    cut = []
    for p, h, lo, ln in out:
        while ln:
            part = max(x for x in LENS if x <= ln)
            cut.append((p, h, lo, part))
            lo, ln = lo + part, ln - part
    return cut


def pieces(vals):
    out, todo = [], [j for j, v in enumerate(vals) if v]
    while todo:
        best = (todo[0], 1, vals[todo[0]], 0, 1)
        for j in todo:
            for k in todo:
                n, far, step = 1, k - j, vals[k] - vals[j]
                while far > 0 and n < 16 and j + n * far in todo and vals[j + n * far] == vals[j] + n * step:
                    n += 1
                if n > best[4]:
                    best = (j, far, vals[j], step, n)
        out.append(best)
        todo = [j for j in todo if j not in range(best[0], best[0] + best[1] * best[4], best[1])]
    return out


CYC, GATHER, SCATTER, PE_COL, PE_LAT, WAKE, ISSUE, HOP, ROW_NS, LINK, DMA0, HBM = 0.85, 1.5, 3.8, 0.43, 100, 200, 250, 750, 25, 20.0, 1200, 600.0
CHUNK = 8
SWEEPS, STRETCH, MOVES, REACH = 41, 110, 400, 24
HEAT, SLACK, SEED, FLIPS, COPY = 300.0, 0.1, 2, 0.2, 5
CASES = ((1.0, 1.0, 1.0, 1.0, 200, 0.7, 1.0), (1.0, 0.8, 1.3, 1.0, 200, 1.4, 1.6), (1.3, 1.2, 1.0, 1.3, 220, 1.0, 1.4), (1.1, 0.8, 0.7, 1.1, 150, 1.0, 1.2))
PLANS = {}


def arrange(ops, sends):
    if len(ops) not in PLANS:
        PLANS[len(ops)] = plan(ops, sends)
    scalar, turn = PLANS[len(ops)]
    for j in scalar:
        ops[j].update(e="s", fn=ops[j]["other"][0], ns=ops[j]["other"][1])
    out = [j for j in turn if ops[j]["e"] != "w"]
    new = {j: i for i, j in enumerate(out)}
    return [dict(ops[j], deps=[d if isinstance(d, tuple) else new[d] for d in ops[j]["deps"]
                               if not (d in ops[j]["turns"] and ops[d]["e"] == ops[j]["e"])]) for j in out]


def plan(ops, sends):
    deps = [set(sends[d[0]] if isinstance(d, tuple) else d for d in op["deps"]) for op in ops]
    jobs, job, seen = [], [], set()
    for j, op in enumerate(ops):
        if op["e"] == "t" and j and ops[j - 1]["e"] == "t" and j - 1 in deps[j] and deps[j] <= seen and len(jobs[-1]) < CHUNK:
            jobs[-1].append(j)
        else:
            jobs.append([j])
            seen = set(deps[j])
        seen.add(j)
        job.append(len(jobs) - 1)
    n = len(jobs)
    eng = ["vstgyw".index(ops[m[0]]["e"]) for m in jobs]
    pre = [set(job[d] for j in m for d in deps[j]) - {i} for i, m in enumerate(jobs)]
    loads = [i for i in range(n) if eng[i] == 4]
    kept = set((d, i) for d, i in zip(loads, loads[1:]) if d not in pre[i])
    for d, i in kept:
        pre[i].add(d)
    succ = [[] for _ in range(n)]
    for i in range(n):
        for d in pre[i]:
            succ[d].append(i)
    order, left = [i for i in range(n) if not pre[i]], [len(p) for p in pre]
    for i in order:
        for k in succ[i]:
            left[k] -= 1
            if not left[k]:
                order.append(k)
    above = [0] * n
    for i in order:
        for d in pre[i]:
            above[i] |= above[d]
        pre[i] = sorted(d for d in pre[i] if not above[i] >> d & 1 or (eng[d] >= 4))
        for d in pre[i]:
            above[i] |= 1 << d
    succ = [[] for _ in range(n)]
    for i in range(n):
        for d in pre[i]:
            succ[d].append(i)
    turns = set((job[d], job[j]) for j, op in enumerate(ops) for d in op["turns"])
    free_to_move = [ops[m[0]]["other"] is not None for m in jobs]
    cases = [([0.0] * n, [[] for _ in range(n)], [[] for _ in range(n)]) for _ in CASES]

    def price(i):
        for (slow, gather, scatter, pe, wake, far, load), (ns, needs, gives) in zip(CASES, cases):
            def lag(d, k):
                if eng[d] == eng[k] and (eng[d] == 2 or (d, k) in turns) or (d, k) in kept:
                    return 0.0
                lat = ops[jobs[d][-1]]["lat"]
                return lat * (1, 1, 1, 1, load, far)[eng[d]] + (wake if lat >= 0 else WAKE)

            parts = [ops[j]["other"][1] if eng[i] == 1 and ops[j]["other"] else ops[j]["ns"] for j in jobs[i]]
            ns[i] = sum(a + b * gather + c * scatter for a, b, c in parts) * (slow, slow, pe, far, far, far)[eng[i]]
            needs[i], gives[i] = [(d, lag(d, i)) for d in pre[i]], [(k, lag(i, k)) for k in succ[i]]

    def flip(i):
        eng[i] = 1 - eng[i]
        for k in [i] + [d for d in pre[i] if (d, i) in turns] + [k for k in succ[i] if (i, k) in turns]:
            price(k)

    for i in range(n):
        eng[i] = 1 if free_to_move[i] else eng[i]
    for i in range(n):
        price(i)

    def replay(turn, ns, needs, end, free):
        for i in turn:
            start = free[eng[i]]
            for d, w in needs[i]:
                if end[d] + w > start:
                    start = end[d] + w
            end[i] = free[eng[i]] = start + ns[i]

    def fill(first, needs, ns):
        gaps, end = [[[0.0, 1e18]] for _ in range(6)], [0.0] * n
        for i in sorted(range(n), key=lambda i: -first[i]):
            start, room = max([end[d] + w for d, w in needs[i]] + [0.0]), gaps[eng[i]]
            k = len(room) - 1
            while k and room[k - 1][1] >= start + ns[i]:
                k -= 1
            while max(room[k][0], start) + ns[i] > room[k][1]:
                k += 1
            lo, hi = room[k]
            start = max(lo, start)
            end[i] = start + ns[i]
            room[k:k + 1] = [x for x in ([lo, start], [end[i], hi]) if x[1] - x[0] >= 6]
        return end

    ns, needs, gives = cases[0]
    back, best = [0.0] * n, None
    for i in reversed(order):
        back[i] = ns[i] + max([w + back[k] for k, w in gives[i]] + [0.0])
    for _ in range(12):
        end = fill(back, needs, ns)
        if best is None or max(end) < best[0]:
            best = (max(end), sorted(range(n), key=lambda i: (end[i] - ns[i], end[i])))
        back = fill(end, gives, ns)
    turn, seed = best[1], [SEED]

    def draw():
        seed[0] = (seed[0] * 1103515245 + 12345) % 2147483648
        return seed[0] / 2147483648

    ends = [[0.0] * n for _ in cases]
    tags = [ops[m[0]]["tag"] for m in jobs]
    named = {tag: i for i, tag in enumerate(tags)}
    marks = [named[t, "draft", 0] for t in range(NSTEP)]

    def alike(turn):
        for (ns, needs, gives), end in zip(cases, ends):
            replay(turn, ns, needs, end, [0.0] * 6)
        best = min(range(NSTEP - 1), key=lambda t: sum(end[marks[t + 1]] - end[marks[t]] for end in ends))
        end, ns = ends[0], cases[0][0]
        period, key = end[marks[best + 1]] - end[marks[best]], []
        for i, (t, part, j) in enumerate(tags):
            k = named.get((best, part, j), i) if t is not None else i
            key.append(end[k] - ns[k] + (0 if t is None else end[marks[0]] + t * period - end[marks[tags[k][0]]]))
            if free_to_move[i] and eng[i] != eng[k]:
                flip(i)
        for i in order:
            key[i] = max([key[i]] + [key[d] + 0.01 for d in pre[i]])
        return sorted(range(n), key=lambda i: key[i])

    for sweep in range(SWEEPS):
        heat = HEAT * (1 - sweep / SWEEPS) ** 2
        for lo in range(-int(draw() * STRETCH / 2), n, STRETCH // 2):
            hi, lo = min(n, lo + STRETCH), max(lo, 0)
            part, inside, rest, frees = turn[lo:hi], set(turn[lo:hi]), [], []
            for (ns, needs, gives), end in zip(cases, ends):
                free, tail, after = [0.0] * 6, [0.0] * n, [0.0] * 6
                replay(turn[:lo], ns, needs, end, free)
                replay(turn[:hi - 1:-1], ns, gives, tail, after)
                frees.append(free)
                rest.append(([(i, max([w + tail[k] for k, w in gives[i] if k not in inside] + [0.0])) for i in part], after))
            rest = [([x for x in out if x[1]], after) for out, after in rest]

            def cost(part, a, limit):
                total, ways, new, last = 0.0, [], [], {eng[i]: i for i in part[:a]}
                for c, ((ns, needs, gives), end, free, (out, after)) in enumerate(zip(cases, ends, frees, rest)):
                    free, end = [end[last[e]] if e in last else x for e, x in enumerate(free)], end[:]
                    replay(part[a:], ns, needs, end, free)
                    far = [end[i] + w for i, w in out] + [x + y for x, y in zip(free, after)]
                    ways.append(max(far))
                    new.append(end)
                    total += ways[-1] + SLACK * sum(far) / len(far)
                    if limit and ways[-1] > limit[c]:
                        return None
                return total / len(cases), ways, new

            def held(part, ways):
                c = int(draw() * len(cases))
                (ns, needs, gives), end, (out, after) = cases[c], ends[c], rest[c]
                place, before, last = {i: p for p, i in enumerate(part)}, {}, [None] * 6
                for i in part:
                    before[i], last[eng[i]] = last[eng[i]], i
                at_end = [i for i, w in out if end[i] + w > ways[c] - 1] + [i for e, i in enumerate(last) if i is not None and end[i] + after[e] > ways[c] - 1]
                i, pairs = at_end[0] if at_end else None, []
                while i is not None:
                    start, d = end[i] - ns[i] - 1, before[i]
                    if d is not None and end[d] > start:
                        if not above[i] >> d & 1:
                            pairs.append((place[d], place[i]))
                        i = d
                    else:
                        i = ([d for d, w in needs[i] if d in place and end[d] + w > start] + [None])[0]
                return pairs

            now, ways, ends[:] = cost(part, 0, None)
            pairs = held(part, ways)
            for _ in range(MOVES):
                if pairs and draw() < 0.7:
                    a, b = pairs[int(draw() * len(pairs))]
                    far = int(draw() ** 2 * REACH)
                    a, b = (max(a - far, 0), b) if draw() < 0.5 else (a, min(b + far, len(part) - 1))
                else:
                    a = int(draw() * (len(part) - 1))
                    b = min(a + 1 + int(draw() * REACH), len(part) - 1)
                seg = part[a:b + 1]
                if draw() < 0.5:
                    bits = above[seg[-1]] | 1 << seg[-1]
                    moved = [i for i in seg if bits >> i & 1] + [i for i in seg if not bits >> i & 1]
                else:
                    moved = [i for i in seg[1:] if not above[i] >> seg[0] & 1] + seg[:1] + [i for i in seg if above[i] >> seg[0] & 1]
                other = seg[-1] if draw() < 0.5 else seg[0]
                other = other if free_to_move[other] and draw() < FLIPS else None
                if other is not None:
                    flip(other)
                    moved = seg if draw() < 0.5 else moved
                elif moved == seg:
                    continue
                tried = part[:a] + moved + part[b + 1:]
                more = heat * draw() ** 3
                then = cost(tried, a, [x + 2 * more + 150 for x in ways])
                if then and then[0] <= now + more:
                    part, (now, ways, ends[:]) = tried, then
                    pairs = held(part, ways)
                elif other is not None:
                    flip(other)
            turn[lo:hi] = part
        replay(turn, cases[0][0], cases[0][1], ends[0], [0.0] * 6)
        place = {i: p for p, i in enumerate(turn)}
        turn.sort(key=lambda i: (ends[0][i] - cases[0][0][i], place[i]))
        if sweep % COPY == COPY - 1 and sweep + 2 < SWEEPS:
            turn = alike(turn)
    return [jobs[i][0] for i in range(n) if free_to_move[i] and eng[i] == 1], [j for i in turn for j in jobs[i]]


def emit(g, T, ops):
    queue = {"v": g.vector, "s": g.scalar, "t": g.tensor, "g": g, "y": g.sync}
    clock = {e: {} for e in queue}
    number, needed, waits, snaps = {e: 0 for e in queue}, set(), [], []
    place = []
    for op in ops:
        e = op["e"]
        mine, ck = [], clock[e]
        deps = sorted(op["deps"], key=lambda d: -d if isinstance(d, int) else 1)
        for d in deps:
            if isinstance(d, tuple):
                if d[0] not in ck:
                    ck[d[0]] = 1
                    mine.append(d)
                continue
            src = ops[d]
            if src["sem"] is not None:
                if src["sem"] in ck:
                    continue
                mine.append((src["sem"], 16))
                ck[src["sem"]] = 1
            else:
                if src["e"] == "t" and e == "t":
                    continue
                if ck.get(src["e"], -1) >= place[d]:
                    continue
                mine.append(d)
                needed.add(d)
                ck[src["e"]] = place[d]
            for key, val in snaps[d].items():
                if ck.get(key, -1) < val:
                    ck[key] = val
        waits.append(mine)
        snaps.append(dict(ck))
        place.append(number[e])
        number[e] += 1
    count, seen = {}, {e: 0 for e in queue}
    for n, op in enumerate(ops):
        if n in needed:
            seen[op["e"]] += 1
            count[n] = seen[op["e"]]
    for n, op in enumerate(ops):
        q = queue[op["e"]]
        for d in waits[n]:
            if isinstance(d, tuple):
                q.wait_ge(T.sem[d[0]], d[1])
            else:
                q.wait_ge(T.sem[ENGINE_SEM[ops[d]["e"]]], count[d])
        if op["fn"] is None:
            continue
        ins = op["fn"]()
        if op["sem"] is not None:
            ins.then_inc(T.sem[op["sem"]], 16)
        elif n in needed:
            ins.then_inc(T.sem[ENGINE_SEM[op["e"]]], 1)


def at(name, lo=0, hi=None, step=1):
    return (name, range(lo, SCRATCH[name][1][1] if hi is None else hi, step), None)


def ind(win, off):
    return (win[0], win[1], off)


def rank_program(g, core, T, topo):
    rank = T.rank_of(core)
    if rank is None:
        return
    N = len(T.cores)
    vec, act, pe = g.vector, g.scalar, g.tensor
    ops, last, readers, sent, sends = [], {}, {}, [0], {}

    def ap(x):
        if not isinstance(x, tuple):
            return x
        view = T[x[0]][:, x[1].start:x[1][-1] + 1:x[1].step]
        return view if x[2] is None else view.indirect(ap(x[2]))

    def cells(x):
        if isinstance(x, str):
            return [x]
        if x[0] in WHOLE or psum(x):
            return [x[0]]
        return [(x[0], c) for c in x[1]]

    def psum(x):
        return SCRATCH[x[0]][0] == "psum"

    def width(x):
        return len(x[1]) if x[2] is None else 16 * len(x[2][1])

    def add(e, fn, w, r, ns, lat=0.0, sem=None, remote=False, other=None):
        r = [x for x in r if isinstance(x, (tuple, str))]
        r += [x[2] for x in r + w if isinstance(x, tuple) and x[2] is not None]
        rd = set(c for x in r for c in cells(x))
        wr = set(c for x in w for c in cells(x))
        deps = set(last[c] for c in rd | wr if c in last)
        for c in wr:
            deps.update(readers.get(c, ()))
        turns = set(j for x in r if isinstance(x, tuple) and psum(x) for j in readers.get(x[0], ())
                    if ops[j]["e"] != e or other or ops[j]["other"]) - deps
        n = len(ops)
        ops.append({"e": e, "fn": fn, "deps": deps | turns, "turns": turns, "sem": sem, "ns": ns if isinstance(ns, tuple) else (ns, 0, 0),
                    "lat": lat, "other": other})
        if not remote:
            for c in rd:
                readers.setdefault(c, []).append(n)
        for c in wr:
            last[c] = n
            readers[c] = []

    def took(fixed, out, ins, each=1.0):
        if out[2] is not None:
            return fixed, 0, width(out) * SCATTER * CYC
        if any(x[2] is not None for x in ins):
            return fixed, width(out) * GATHER * CYC, 0
        if each == 1.0 and fixed == 50 and all(SCRATCH[x[0]][2] in (B, HF, U) for x in [out] + ins):
            each = 0.5
        return max(64, width(out) * each) * CYC + (fixed > 65) * 20, 0, 0

    def ts(out, a, s1, s2, op0, op1=None, other=None):
        if other is None and (op0, op1) in ((OP.add, None), (OP.mult, None), (OP.mult, OP.add)) and SCRATCH[out[0]][2] != I:
            return either(out, a, bias=s1 if op0 == OP.add else s2 or 0.0, scale=s1 if op0 == OP.mult else 1.0)
        more = () if op1 is None else (op1,)
        add("v", lambda: vec.tensor_scalar(ap(out), ap(a), ap(s1), ap(s2), op0, *more), [out], [a, s1, s2], took(50, out, [a]), other=other)

    def either(out, a, func=AF.Identity, bias=0.0, scale=1.0):
        other = (lambda: act.activation(ap(out), ap(a), func, bias=ap(bias), scale=ap(scale)), took(65, out, [a]))
        if func == AF.Sign:
            ts(out, a, -1.0, 1.0, OP.max, OP.min, other)
        elif func == AF.Relu:
            ts(out, a, 0.0, scale, OP.min, OP.mult, other)
        elif scale == 1.0:
            ts(out, a, bias, None, OP.add, None, other)
        else:
            ts(out, a, scale, bias, OP.mult, OP.add, other)

    def tt(out, a, b, op):
        add("v", lambda: vec.tensor_tensor(ap(out), ap(a), ap(b), op), [out], [a, b],
            took(50, out, [a, b], 1.01 if psum(a) or psum(b) else 2.0))

    def cp(out, a, more=()):
        if out[2] is None:
            return either(out, a)
        add("v", lambda: vec.tensor_copy(ap(out), ap(a)), [out], [a] + list(more), took(50, out, [a]))

    def scan(out, keep, a):
        add("v", lambda: vec.tensor_tensor_scan(ap(out), ap(keep), ap(a), 0.0, OP.mult, OP.max), [out], [keep, a], took(50, out, [keep, a]))

    def ms(out, val):
        add("v", lambda: vec.memset(ap(out), val), [out], [], took(50, out, []))

    def ac(out, a, func=AF.Identity, bias=0.0, scale=1.0, acc=None):
        if acc is None and func == AF.Identity:
            either(out, a, func, bias, scale)
        elif acc is None:
            add("s", lambda: act.activation(ap(out), ap(a), func, bias=ap(bias), scale=ap(scale)), [out], [a, bias, scale], took(65, out, [a]))
        else:
            add("s", lambda: act.activation(ap(out), ap(a), func, bias=ap(bias), scale=ap(scale), accum_out=ap(acc)),
                [out, acc], [a, bias, scale], took(85, out, [a]))

    def mm(out, lhsT, rhs, start=False, stop=False):
        slow = 4 if SCRATCH[rhs[0]][2] == F else 1
        add("t", lambda: pe.matmul(ap(out), ap(lhsT), ap(rhs), start, stop), [out], [lhsT, rhs], max(64, width(out)) * slow * PE_COL, PE_LAT)

    def group(terms):
        for n, (out, lhsT, rhs) in enumerate(terms):
            mm(out, lhsT, rhs, n == 0, n == len(terms) - 1)

    def iota(out, pattern, base, mult=0):
        more = {} if SCRATCH[out[0]][2] == I else {"allow_small_or_imprecise_dtypes": True}
        add("g", lambda: g.iota(ap(out), pattern, base, mult, **more), [out], [], 130 + 2 * width(out) * CYC)

    def keep(out, a, pattern, op, fill):
        add("g", lambda: g.affine_select(ap(out), ap(a), pattern, op, fill, 0, 1), [out], [a], 170 + 2 * width(out) * CYC)

    def table(name, lo, vals):
        ms(at(name, lo, lo + len(vals)), 0.0)
        for turn, (j, far, first, step, n) in enumerate(pieces(vals)):
            out = at(name, lo + j, lo + j + far * (n - 1) + 1, far)
            if turn % 2:
                ac(out, at("i64", 0, n), bias=float(first), scale=float(step))
            else:
                ts(out, at("i64", 0, n), float(step), float(first), OP.mult, OP.add)

    def dma(e, out, a, sem, w, r, nbytes=0):
        add(e, lambda: (g.sync if e == "y" else act).dma_start(out, a), w, r, 50, DMA0 + nbytes / HBM, sem)

    def send(to, out, a, sem):
        dst = T.cores[to]
        rid, pid = topo.addr(dst, core)
        ways = len(topo.engines(core, dst))
        sent[0] += ways
        nbytes = width(a) * (4 if SCRATCH[a[0]][2] == F else 2)
        add("g", lambda: g.remote_dma(ap(out), ap(a), T.sem[sem], T.sem.sent, pid, rid, topo.mask(core, dst)), [], [a],
            ISSUE, -WAKE, remote=True)
        sends[sem] = len(ops)
        ops.append({"e": "w", "deps": {len(ops) - 1}, "turns": (), "ns": (128 / ways * (ROW_NS + nbytes / LINK), 0, 0), "lat": HOP, "other": None})

    def lands(place, sem, frm):
        for c in cells(place):
            last[c] = (sem, len(topo.engines(T.cores[frm], core)))

    def verifier(t, r=rank):
        return (r + 1 + t % (N - 1)) % N

    def drafter(t):
        return (rank - 1 - t % (N - 1)) % N

    LAST = NSTEP - 1
    CUT = 16 * STATES_LAST[-1][0]

    def tiles(t):
        out, lo = [], LT * t
        for c0, c1 in TILES if t < LAST else TILES_LAST:
            out.append((c0, c1, lo))
            lo += c1 - c0
        return out

    def tokens(t, c0, c1):
        lo = [place - a for a, b, place in tiles(t) if a <= c0][-1 if c1 == 16 or t < LAST else 0 if c0 == 0 else 1]
        return at("l_lt", lo + c0, lo + c1)

    def back_parts(t):
        return [(256 * t + 16 * c0, 256 * t + 16 * c1, "a_e%d_%d" % (t, b)) for b, (c0, c1) in enumerate(BLOCKS)]

    for t in range(NSTEP):
        lands(at("x", XW * t, XW * t + 8), "a_x%d" % t, verifier(t - 1, drafter(t)) if t else drafter(0))
        lands(at("l_ct", 48 * t, 48 * t + 48), "a_ct%d" % t, drafter(t))
        for j, (c0, c1, lo) in enumerate(tiles(t)):
            lands(at("l_lt", lo, lo + c1 - c0), "a_lt%d_%d" % (t, j), drafter(t))
        if t < LAST:
            lands(at("l_j", 4 * t, 4 * t + 2), "a_e%d_4" % t, verifier(t))
            for lo, hi, sem in back_parts(t):
                lands(at("l_e", lo, hi), sem, verifier(t))
    lands(at("l_y", 0, CUT), "a_y0", verifier(LAST))
    lands(at("l_y", CUT, 256), "a_y1", verifier(LAST))
    lands(at("l_f"), "a_f", verifier(LAST))
    lands(at("l_j", 12, 16), "a_r", verifier(LAST - 1, drafter(LAST)))

    (C_I, C_0, C_TK, C_UC, C_UT, C_KB, C_S, C_Q, C_IX, C_NK, C_JK, C_T, C_EV, C_OD, C_PM, C_R, C_J2, C_B) = range(18)
    C_K2, C_MID, C_LOSE, C_PAD = 20, 24, 32, 36
    K_A, K_S4, K_TH, K_PM, K_NC, K_R, K_DMK = 0, 20, 24, 40, 56, 76, 92
    B_15, B_3, B_NC, B_S, B_SH, B_H = 0, 36, 56, 76, 80, 144
    L_UC, L_CMP, L_PAR, L_REP, L_TH, L_PM, L_TH0, L_8 = 0, 20, 24, 40, 44, 60, 76, 92

    def cc(j):
        return at("col", j, j + 1)

    def run(lo, ln, name="runs"):
        first = (160 * LENS.index(ln) if name == "runs" else 0) + 15 - lo
        return at(name, first, first + 128)

    def mat(name, j=0):
        return at(name, 128 * j, 128 * j + 128)

    ident, ones, negi, negq = at("idw", 16, 144), run(0, 16), mat("negi"), mat("negq")

    ms(at("tk"), 0)
    ms(at("xi", 4, 8), 0.0)
    dma("s", T.xi[:, 0:4], T.x0[:], "d_x", [at("xi", 0, 4)], [])
    dma("s", T.kp[:, 0:1], T.kap[:], "d_kp", [at("kp", 0, 1)], [])
    dma("y", T.tk[0:128:16, :], T.tok[:], "d_tk", [at("tk")], [])
    dma("y", T.q[:], T.qt[:], "d_q", ["q"], [], 128 * V * 4)
    dma("y", T.k[:], T.kt[:], "d_k", ["k"], [], 128 * V * 6)
    dma("y", T.a[:, 0:V], T.qt[:], "d_a", ["a"], ["q"], 128 * V * 6)
    send(verifier(0), at("x", 0, 8), at("xi"), "a_x0")
    ops[-1]["lat"] += 5000

    iota(at("pi", 0, 1), [[0, 1]], 0, 1)
    iota(at("i64", 0, 16), [[1, 16]], 0)
    iota(at("i64", 16, 128), [[0, 7], [1, 16]], 0)
    iota(at("xq"), [[1, 160]], 0, -1)
    ts(at("pi", 1, 2), at("pi", 0, 1), 15, None, OP.bitwise_and)
    cp(cc(C_I), at("pi", 1, 2))
    ts(at("idw"), at("xq"), 16.0, None, OP.is_equal)
    ts(at("runs", 0, 160), at("xq"), cc(C_I), 15.0, OP.add, OP.is_equal)
    for j, ln in enumerate(LENS[1:]):
        ac(cc(C_MID + j), cc(C_I), bias=-15.0 - (ln - 1) / 2)
        ac(at("ab", 160 * j, 160 * j + 160), at("xq"), AF.Abs, cc(C_MID + j))
        ts(at("runs", 160 * j + 160, 160 * j + 320), at("ab", 160 * j, 160 * j + 160), ln / 2, None, OP.is_lt)
    cp(at("rowx", 0, 16), at("i64", 0, 16))
    table("rowx", 16, ROW[16:48])
    table("rowx", 48, ROW[START[3]:] + [0] * (START[3] - 32))
    iota(at("cst", K_A, K_A + 4), [[0, 4]], 0)
    iota(at("cst", K_A + 4, K_A + 20), [[32, 2], [0, 4], [16, 2]], 16)
    ts(at("lst", L_UC, L_UC + 20), at("cst", K_A, K_A + 20), cc(C_I), None, OP.add)
    ac(cc(C_UC), cc(C_I), bias=float(H), scale=-float(R))
    ac(cc(C_UT), cc(C_I), bias=-float(H), scale=float(R))
    for lo, hi in ((0, 4), (4, 12), (12, 20)):
        rows = ind(at("rowx", 0, 4 * hi), at("lst", L_UC + lo, L_UC + hi))
        ac(at("cu", 16 * lo, 16 * hi), rows, bias=-7.0 * 144, scale=144.0)
        ac(at("uc", 16 * lo, 16 * hi), rows, bias=cc(C_UC), scale=float(R))
    ms(at("cu", 320, 384, 16), -7.0 * 144)
    ms(at("zero"), 0.0)
    ts(cc(C_0), cc(C_I), 0.0, None, OP.is_equal)
    ts(cc(C_TK), cc(C_0), -2.0 * H, float(H), OP.mult, OP.add)
    ts(at("u", 320, 384, 16), at("tk"), cc(C_TK), None, OP.add)
    ms(at("hp"), float(H))
    for d in (2, 3):
        for h, (bound, op) in enumerate(((FIRST[d] - START[d], OP.is_lt), (FIRST[d + 1] - START[d] - 16, OP.is_ge))):
            ts(cc(C_PAD + 2 * d + h), cc(C_I), float(bound), float(R), op, OP.mult)
            half = at("hp", 8 * d + 4 + h, 8 * d + 12, 2)
            ac(half, half, bias=cc(C_PAD + 2 * d + h))

    def node(src, n):
        lo, step = UCOL[DEPTH[n]] + n - START[DEPTH[n]], USTEP[DEPTH[n]]
        return at(src, lo, lo + 3 * step + 1, step)

    def pe_root(src, init):
        group([(at("p0", 44, 48), ident, at(init, 44, 48)), (at("p0", 44, 48), ones, node(src, 0))])

    def pe_parents(src, init, depth, up, lo, bank="p0"):
        group([(at(bank, lo, lo + 8), ident, at(init, lo, lo + 8))]
              + [(at(bank, lo + h, lo + 8, 2), run(first, ln), node(src, p))
                 for p, h, first, ln in runs_of(depth, up, FIRST if up > 1 else USED)])

    def pe_nodes(src, init, bank="p0"):
        group([(at(bank, 0, 20), ident, at(init, 0, 20))] + [(at(bank, 0, 20), run(i, 1), at(src, i, 320, 16)) for i in range(16)])

    def pe_tile(c0, c1, level):
        terms = [(at("p1", c0, c1), ident, at("ct1", c0, c1))]
        terms += [(at("p1", 0, 1), run(s, 1), at("u", UCOL[0] + 16 * s, UCOL[0] + 16 * s + 1)) for s in range(0 if c0 else 4)]
        for r in range(4):
            first = c0 if c0 or r else 1
            for s in range(4):
                lo = UCOL[level] + s * USTEP[level] + 4 * first + r - START[level]
                terms.append((at("p1", first, c1), run(4 * r + s, 1), at("u", lo, lo + 4 * (c1 - first) - 3, 4)))
        group(terms)

    ms(at("ct0", 44, 48), -14.0 * H)
    for depth, up, lo in ((2, 1, 20), (3, 1, 28), (3, 2, 36)):
        pe_parents("cu", "zero", depth, up, lo, "p%d" % (depth + up - 1))
        ac(at("ct0", lo, lo + 8), at("p%d" % (depth + up - 1), lo, lo + 8))
    pe_nodes("cu", "zero", "p5")
    ac(at("ct0", 0, 20), at("p5", 0, 20))
    ms(at("rows", 64, 65), -7.0 * 144)
    for d, (lo, hi) in enumerate(zip(START[1:], START[2:] + (64,))):
        ac(at("rows", 64 + lo, 64 + hi), at("rowx", (0, 16, 48)[d], (0, 16, 48)[d] + hi - lo), bias=-7.0 * 144, scale=144.0)
    for bank, lo, hi in (("p1", 0, 4), ("p6", 4, 16)):
        group([(at(bank, lo, hi), run(4 * r, 4), at("rows", 64 + 4 * lo + r, 64 + 4 * hi, 4)) for r in range(4)])
        ac(at("ct1", lo, hi), at(bank, lo, hi))

    ts(at("pi", 3, 4), at("pi", 0, 1), 3, None, OP.bitwise_and)
    ts(at("pi", 4, 5), at("pi", 1, 2), 2, None, OP.logical_shift_right)
    cp(cc(C_S), at("pi", 3, 4))
    cp(cc(C_Q), at("pi", 4, 5))
    table("rows", 0, [p and p + 2 for p in PAR])
    group([(at("p3", 0, 16), run(4 * r, 4), at("rows", r, 64, 4)) for r in range(4)])
    ts(at("lst", L_PAR, L_PAR + 16), at("p3", 0, 16), 0.25, cc(C_S), OP.mult, OP.add)
    iota(at("rows", 128, 132), [[1, 4]], 0)
    iota(at("rows", 132, 148), [[0, 2], [1, 4], [0, 2]], 4)
    iota(at("rows", 148, 164), [[4, 2], [1, 4], [0, 2]], 0)
    iota(at("rows", 164, 176), [[1, 6], [0, 2]], 0)
    group([(at("p7", 0, 3), run(i, 1), at("rows", 128 + i, 176, 16)) for i in range(16)])
    ts(at("lst", L_CMP, L_CMP + 3), at("p7", 0, 3), 1.0 / 16, None, OP.mult)
    ts(at("pi", 2, 3), at("pi", 0, 1), 4, 1, OP.logical_shift_right, OP.bitwise_and)
    cp(cc(C_OD), at("pi", 2, 3))
    ac(cc(C_EV), cc(C_OD), bias=1.0, scale=-1.0)
    if "t" in TURN:
        ts(cc(C_R), cc(C_OD), -16.0, cc(C_I), OP.mult, OP.add)
        ac(cc(C_R), cc(C_R), bias=1.0)
        ts(at("ide", 0, 129), at("xq", 0, 129), cc(C_R), cc(C_EV), OP.is_equal, OP.mult)
        ts(at("ido", 0, 129), at("xq", 0, 129), cc(C_R), cc(C_OD), OP.is_equal, OP.mult)
    ts(at("pi", 5, 6), at("pi", 0, 1), 1, None, OP.bitwise_and)
    cp(cc(C_B), at("pi", 5, 6))
    for w in sorted(set(c1 - c0 for (c0, c1), how in zip(BLOCKS, TURN) if how == "v")):
        if w == 4:
            ac(cc(C_PM), cc(C_S), bias=cc(C_Q), scale=16.0)
        else:
            ts(cc(C_PM), cc(C_B), 15.5, None, OP.mult)
            ac(cc(C_PM), cc(C_I), bias=cc(C_PM), scale=0.5)
        ts(cc(C_T), cc(C_B), cc(C_OD), 16.0 * w + 16, OP.not_equal, OP.mult)
        tt(cc(C_PM), cc(C_PM), cc(C_T), OP.add)
        ts(at("lst", L_PM + w, L_PM + 2 * w), at("i64", 0, w), 16.0 / w, cc(C_PM), OP.mult, OP.add)
    for b, (c0, c1) in enumerate(BLOCKS):
        if TURN[b] == "v":
            for c in (c0 - 1, c1):
                ms(at("cf", 16 * c + 32 * b + 16, 16 * c + 32 * b + 32), 0.0)
    ac(cc(C_NK), at("kp", 0, 1), scale=-1.0)
    iota(at("fmi"), [[-1, 128]], 128, 1)
    ts(at("fmi"), at("fmi"), 15, None, OP.bitwise_and)
    ts(at("fm", 128, 256), at("fmi"), 1.0, None, OP.add)
    tt(mat("fm"), at("fm", 128, 256), ones, OP.mult)
    ac(negi, ident, scale=-1.0)
    ac(negq, ident, scale=-2.0 / R)
    for d in range(1, 16):
        bank, o = "p%d" % (3 + (d - 1) // 4), 128 * ((d - 1) % 4)
        if d <= 8:
            ts(mat("shf", d - 1), mat("fm"), d + 1.0, None, OP.is_equal)
            group([(at(bank, o, o + 128), ident, mat("shf", d - 1)), (at(bank, o, o + 128), ident, negi)])
        else:
            mm(at(bank, o, o + 128), mat("dm", 15 - d), ident, True, True)
        if d % 4 == 0 or d == 15:
            ac(at("dm", 128 * d - o - 128, 128 * d), at(bank, 0, o + 128))
    ac(cc(C_KB), cc(C_I), bias=-128.0, scale=-1.0)
    ac(at("runh"), at("runs", 0, 160), scale=0.5)
    ac(mat("negf"), ident, scale=-1.0)
    signed = [sum(m for m, bank in calls if bank is None) for calls in CALLS]
    for first in set(signed) - {16}:
        ts(cc(C_T), cc(C_I), float(first), 128.0, OP.is_ge, OP.mult)
        tt(cc(C_K2 + signed.index(first)), cc(C_KB), cc(C_T), OP.add)
    ms(at("sh"), -15.0)
    for bank in LAID:
        mm(at(bank), ident, at("dm", 0, 512), True, True)
    iota(at("cst", K_R, K_R + 8), [[-1, 8]], 15)
    ts(at("cst", K_R + 8, K_R + 16), at("cst", K_R, K_R + 8), cc(C_I), None, OP.is_le)
    tt(at("cst", K_R + 8, K_R + 16), at("cst", K_R + 8, K_R + 16), at("cst", K_R, K_R + 8), OP.mult)
    ts(at("col", C_LOSE, C_LOSE + 8), at("cst", K_R + 8, K_R + 16), 1.0, None, OP.add)
    for d in range(8):
        ts(mat("lose", d), mat("fm"), cc(C_LOSE + d), float(R), OP.is_equal, OP.mult)
    ac(cc(C_JK), cc(C_I), bias=float(V))
    ac(cc(C_J2), cc(C_I), bias=V + 16.0)
    ac(mat("bigi"), ident, scale=float(R))
    cp(at("lst", L_8, L_8 + 8), at("i64", 0, 8))
    ts(at("rst"), at("i64"), 0.0, None, OP.not_equal)
    add("g", lambda: g.iota(T.a[:, V:V + 32], [[0, 32]], 0, 0), ["az"], [], 190)
    ac(mat("onew"), ones, scale=65536.0)
    ac(mat("negw"), ident, scale=-131072.0)
    keep(mat("upper"), ones, [[-1, 128]], OP.is_gt, 0.0)
    keep(mat("upper"), mat("upper"), [[-1, 128]], OP.not_equal, -1.0)
    ms(at("cb", B_15, B_15 + 20), 15.0 * H)
    ms(at("cb", B_3, B_3 + 12), 0.0)
    ms(at("cb", B_3 + 12, B_3 + 20), 15.0 * H)
    ac(mat("neg2"), ident, scale=-2.0)
    iota(at("cst", K_NC, K_NC + 4), [[0, 4]], START[1])
    iota(at("cst", K_NC + 4, K_NC + 20), [[START[3] - START[2], 2], [0, 4], [16, 2]], START[2])
    ts(at("cst", K_NC, K_NC + 20), at("cst", K_NC, K_NC + 20), cc(C_I), -1.0 / 256, OP.add, OP.mult)
    ac(at("cb", B_NC, B_NC + 20), at("cst", K_NC, K_NC + 20), bias=1.0)
    iota(at("cst", K_S4, K_S4 + 4), [[1, 4]], 0)
    iota(at("cst", K_PM, K_PM + 4), [[0, 2], [1, 2]], 0)
    ts(at("cst", K_PM, K_PM + 4), at("cst", K_PM, K_PM + 4), cc(C_B), -1024.0, OP.not_equal, OP.mult)
    tt(at("cst", K_PM, K_PM + 4), at("cst", K_PM, K_PM + 4), at("cst", K_S4, K_S4 + 4), OP.add)
    ac(at("cb", B_S, B_S + 4), at("cst", K_PM, K_PM + 4), scale=0.25)
    iota(at("cst", K_DMK, K_DMK + 12), [[0, 3], [1, 4]], 0)
    ts(at("diag", 0, 16), at("i64", 0, 16), cc(C_I), None, OP.is_equal)
    ms(at("cb", B_H, B_H + 64), float(H))
    ac(at("tie"), at("i64"), bias=15.0 * 4096, scale=-4096.0)
    cp(at("lst", L_REP, L_REP + 4), at("cst", K_S4, K_S4 + 4))
    ts(at("cst", K_DMK, K_DMK + 12), at("cst", K_DMK, K_DMK + 12), cc(C_S), None, OP.is_equal)
    ts(cc(C_IX), cc(C_Q), 1.0, 16.0, OP.is_equal, OP.mult)
    tt(cc(C_IX), cc(C_IX), cc(C_S), OP.add)

    def tops(entries, t, o):
        for (lo, hi), bank in zip(TOPS, COUNT):
            ts(at("ut", o + lo, o + hi), at(entries, 256 * t + lo, 256 * t + hi), cc(C_UT), float(H), OP.add, OP.min)
            mm(at(bank, lo, hi), ones, at("ut", o + lo, o + hi), True, True)
            ac(at("tb", o + lo, o + hi), at(bank, lo, hi), bias=-14.0 * H)
        return at("tb", o, o + 256)

    def root(t):
        if t:
            picked = ind(tops("l_e", t - 1, 0), at("l_j", 4 * t - 4, 4 * t - 2))
            cp(at("rt"), picked)
            cp(at("rf"), picked)
            ts(at("u", 320, 384, 16), at("rf", MID, MID + 4), cc(C_TK), float(H), OP.add, OP.min)
            ac(at("ytb", 4 * t - 4, 4 * t), at("rf", MID, MID + 4))
        else:
            pe_root("u", "ct0")
            cp(at("rt", MID, MID + 4), at("p0", 44, 48))

    def draft(t):
        win = at("a", 0, V) if t else at("q")
        for level, (c0, c1, place) in enumerate(tiles(t)):
            lo, hi = UCOL[level + 1], UCOL[level + 1] + 4 * USTEP[level + 1]
            tile = at("pl", 8 * level - 8, 8 * level) if level else at("rt", MID, MID + 4)
            tt(at("w", lo, hi), ind(win, tile), at("uc", lo, hi), OP.subtract)
            ts(at("u", lo, hi), at("w", lo, hi), -float(H), float(H), OP.max, OP.min)
            if level < 2:
                pe_parents("u", "ct0", level + 2, 1, 20 + 8 * level)
                cp(at("pl", 8 * level, 8 * level + 8), at("p0", 20 + 8 * level, 28 + 8 * level))
            pe_tile(c0, c1, level + 1)
            ac(at("ls", place, place + c1 - c0), at("p1", c0, c1))
            send(verifier(t), at("l_lt", place, place + c1 - c0), at("ls", place, place + c1 - c0), "a_lt%d_%d" % (t, level))
        pe_parents("u", "ct0", 3, 2, 36)
        pe_nodes("u", "ct0")
        tt(at("cts", 48 * t, 48 * t + 48), at("p0", 0, 48), at("hp"), OP.subtract)
        send(verifier(t), at("l_ct", 48 * t, 48 * t + 48), at("cts", 48 * t, 48 * t + 48), "a_ct%d" % t)

    def twins():
        ts(at("t16"), at("p1", 0, 16), -float(H), None, OP.add)
        for d in range(8):
            mm(at("p1", 16 + 16 * d, 32 + 16 * d), mat("dm", d), at("t16"), True, True)
        ts(at("eq"), at("p1", 16, 144), 0.0, None, OP.is_equal)
        tt(at("dl"), at("t16", 0, 16, 2), at("t16", 1, 16, 2), OP.subtract)
        ac(at("dr"), ind(at("dl"), at("lst", L_8, L_8 + 8)))
        mm(at("p1", 256, 384, 16), ident, at("zero", 0, 8), True, True)
        for d in range(15):
            mm(at("p1", 257 + d, 384, 16), mat("dm", d), at("t16", 1, 16, 2), True, True)
        tt(at("eq2", 0, 128), at("p1", 256, 384), at("dr"), OP.is_equal)
        scan(at("eq2", 128, 256), at("rst"), at("eq2", 0, 128))
        out = at("p1", 144, 160)
        group([(out, ident, at("t16"))] + [(out, mat("lose", d), at("eq", 16 * d, 16 * d + 16)) for d in range(8)]
              + [(at("p1", 144, 160, 2), mat("bigi"), at("eq2", 143, 256, 16))])
        for h, c in enumerate((C_JK, C_J2)):
            ts(at("off", h, 16, 2), at("p1", 144 + h, 160, 2), float(H), cc(c), OP.add, OP.min)

    def overwrite(t):
        for c in range(0, 16, 2):
            cp(ind(at("a"), at("off", c, c + 2)), at("l_e", 256 * t + 16 * c, 256 * t + 16 * c + 32), ["az"])

    def block(name, b, base=0):
        return at(name, base + 64 * b, base + 64 * b + 64)

    def cols(name, c0, c1, base=0):
        return at(name, base + 16 * c0, base + 16 * c1)

    def states(t):
        o = XW * t
        for c0, c1 in STATES if t < LAST else STATES_LAST:
            known = max(PAR[4 * c0:4 * c1])
            win = at("x", o, o + (4 * known + 12 if c0 else 4))
            ac(cols("ph", c0, c1), ind(win, at("lst", L_PAR + c0, L_PAR + c1)), scale=0.5)
            tt(cols("x", c0, c1, o + 8), ind(at("k"), tokens(t, c0, c1)), cols("ph", c0, c1), OP.add)
            if c0 == 0:
                ac(at("x", o + 8, o + 12), at("x", o, o + 4))

    def bounds(t, b):
        (c0, c1), o = BLOCKS[b], XW * t
        for r in range(max(m for m, bank in CALLS[b])):
            lo = 128 * c0 + 16 * (c1 - c0) * r
            if c0:
                ac(at("th", lo, lo + 16 * (c1 - c0)), cols("x", c0, c1, o + 8), bias=cc(C_NK))
            else:
                ac(at("th", lo, lo + 4), at("x", o, o + 4), bias=cc(C_NK))
                ac(at("th", lo + 4, lo + 16 * c1), at("x", o + 12, o + 8 + 16 * c1), bias=cc(C_NK))

    def turn(out, a):
        add("v", lambda: vec.transpose(ap(out), ap(a)), [out], [a], took(50, out, [a]))

    def cands(b):
        c0, c1 = BLOCKS[b]
        return cols("cd", c0, c1) if TURN[b] == "t" else cols("cf", c0, c1, 32 * b + 16)

    def prepare(t, b):
        c0, c1 = BLOCKS[b]
        w, picked, scale = c1 - c0, ind(at("q"), tokens(t, c0, c1)), 1.0 if TURN[b] == "t" else 2.0 / R
        ac(cands(b), picked, bias=-H * scale, scale=scale)
        if TURN[b] == "v":
            o = 32 * c0 + 32 * b
            turn(at("tw", o, o + 16 * w), cands(b))
            turn(at("tw", o + 16 * w, o + 32 * w + 32), cols("cf", c0 - 1, c1 + 1, 32 * b + 16))
            ts(cols("ct", c0, c1), ind(at("tw", o, o + 32 * w + 32), at("lst", L_PM + w, L_PM + 2 * w)), R / 2.0, float(H), OP.mult, OP.add)
            return
        for j in range(w // 2):
            for h, src in enumerate(("ide", "ido")):
                group([(cols("p2", c0 + 2 * j + h, c0 + 2 * j + h + 1), at(src, 1 - to, 129 - to),
                        cols("cd", c0 + j + to * w // 2, c0 + j + to * w // 2 + 1)) for to in range(2)])
        turn(cols("tr", c0, c1), cols("p2", c0, c1))
        for j in range(w // 2):
            ts(at("ct", 16 * c0 + j, 16 * c1, w // 2), cols("tr", c0 + 2 * j, c0 + 2 * j + 2), float(H), None, OP.add)

    def votes(b):
        c0, c1 = BLOCKS[b]
        w, n, nxt, done = c1 - c0, 16 * (c1 - c0), {True: 0, False: signed[b]}, 0
        for m, bank in CALLS[b]:
            k0 = nxt[bank is None]
            nxt[bank is None] += m
            lo, hi = 256 * c0 + n * k0, 256 * c0 + n * (k0 + m)
            numbers, th = ind(at("k"), at("ct", 16 * c0 + w * k0, 16 * c0 + w * (k0 + m))), at("th", 128 * c0, 128 * c0 + n * m)
            if bank:
                diff = at(bank, 512 - n * m, 512)
                ac(at("kc", lo, hi), numbers)
                if bank in LAID:
                    ac(diff, th, scale=-1.0)
                    mm(diff, ident, at("kc", lo, hi), False, True)
                else:
                    group([(diff, mat("negf"), th), (diff, ident, at("kc", lo, hi))])
                ac(at("ge", lo, hi), diff, AF.Sign, 2.0 ** -100)
            else:
                tt(at("ge", lo, hi), numbers, th, OP.is_ge)
            for k in range(k0, k0 + m):
                mm(at(COUNT[b], 0, n), run(k, 1, "runh" if bank else "runs"), at("ge", 256 * c0 + n * k, 256 * c0 + n * k + n), done == 0, done == 15)
                done += 1

    def ranks(t, b):
        c0, c1 = BLOCKS[b]
        key, so, n = cols("key", c0, c1), 128 * c0, 16 * (c1 - c0)
        ac(key, at(COUNT[b], 0, n), bias=cc(C_K2 + signed.index(signed[b]) if signed[b] < 16 else C_KB), scale=16.0)
        for lo, hi, bank, e in DIFFS[b]:
            for d in range(lo, hi):
                mm(at(bank, n * (d - lo), n * (d - lo + 1)), mat("dm", d), key, True, True)
            either(at("sg", so + n * lo, so + n * hi), at(bank, 0, n * (hi - lo)), AF.Sign)
        bank, base = PLACES[b], 256
        out = cols(bank, c0, c1, base)
        group([(out, negq if TURN[b] == "t" else mat("negf"), cands(b)), (out, ident, at("sh", 0, n))]
              + [(out, mat("dm", 14 - d) if d < 7 else negi, at("sg", so + n * d, so + n * d + n)) for d in range(8)])
        for name, nodes, scale in (("utb", PAR, -1.0), ("uta", [PAR[p] for p in PAR], -float(R))):
            inner = [4 * p for p in nodes if c0 <= p // 4 < c1]
            if inner:
                lo, hi = min(inner), max(inner) + 4
                ts(at(name, lo, hi), at(bank, base + lo, base + hi), -2.0 * H / R, scale, OP.max, OP.mult)
        ac(cols("es", c0, c1, 256 * t), out, bias=cc(C_UC), scale=-R / 2.0)

    def commit(t):
        o = 48 * t

        def dd(lo, hi, step=1):
            return at(COMMIT, 160 + lo, 160 + hi, step)

        def top(name, n):
            return at(name, 4 * n, 4 * n + 4)

        terms = [(dd(0, 20), mat("negw"), at("cb", B_3, B_3 + 20)), (dd(12, 20), mat("negw"), at("l_ct", o + 36, o + 44))]
        terms += [(dd(12 + h, 20, 2), mat("onew"), top("uta", 0)) for h in range(2)]
        terms += [(dd(4, 20), mat("neg2"), at("cb", B_15, B_15 + 16)), (dd(4, 20), mat("neg2"), at("l_ct", o + 20, o + 36))]
        terms += [(dd(4 + h, 12, 2), ones, top("uta", 0)) for h in range(2)]
        terms += [(dd(12 + h, 20, 2), run(lo, ln), top("uta", p)) for p, h, lo, ln in runs_of(3, 2)]
        terms += [(dd(0, 20), negq, at("cb", B_15, B_15 + 20)), (dd(0, 20), negq, at("l_ct", o, o + 20)), (dd(0, 4), ones, top("utb", 0))]
        for d in (2, 3):
            terms += [(dd(8 * d - 12 + h, 8 * d - 4, 2), run(lo, ln), top("utb", p)) for p, h, lo, ln in runs_of(d, 1)]
        group(terms)
        ts(at("m", 0, 20), dd(0, 20), 0.0, None, OP.is_equal)
        later = [((4, 20, 2), (5, 20, 2)), ((0, 4), (4, 12, 2)), ((0, 4), (5, 12, 2)), ((4, 12), (12, 20)), ((4, 12, 2), (13, 20, 2)),
                 ((5, 12, 2), (12, 20, 2))]
        group([(dd(20, 40), ident, at("cb", B_NC, B_NC + 20)), (dd(20, 40), mat("upper"), at("m", 0, 20))]
              + [(dd(20 + a[0], 20 + a[1], *a[2:]), ones, at("m", *b)) for a, b in later])
        either(at("one"), dd(20, 40), AF.Relu, scale=-256.0)
        parts = [(0, 4, 1), (4, 12, 2), (5, 12, 2), (12, 20, 2), (13, 20, 2)]
        group([(dd(40, 44), ident, at("cb", B_S, B_S + 4))] + [(dd(40, 44), ones, at("one", *a)) for a in parts])
        ix = at("ix", 4 * t, 4 * t + 2)
        for j in range(2):
            ts(at("ix", 4 * t + j, 4 * t + j + 1), dd(40 + 2 * j, 41 + 2 * j), dd(41 + 2 * j, 42 + 2 * j), 4.0, OP.max, OP.mult)
        send(drafter(t), at("l_j", 4 * t, 4 * t + 2), ix, "a_e%d_4" % t)
        o, to = 40 * t + 16, verifier(t + 1, drafter(t))
        ac(at("xg", o - MID, o - MID + 32), ind(at("x", XW * t + 8, XW * t + XW), ix))
        send(to, at("x", XW * t + XW, XW * t + XW + 8), at("xg", o, o + 8), "a_x%d" % (t + 1))
        if t + 1 == LAST:
            cp(at("rq"), ind(tops("es", t, 256), ix))
            send(to, at("l_j", 12, 16), at("rq", MID, MID + 4), "a_r")

    def verify(t):
        states(t)
        for b in range(len(BLOCKS)):
            prepare(t, b)
            bounds(t, b)
        for b in range(len(BLOCKS)):
            votes(b)
            ranks(t, b)
        commit(t)
        for lo, hi, sem in back_parts(t):
            send(drafter(t), at("l_e", lo, hi), at("es", lo, hi), sem)

    def chain():
        xt, rep = at("x", XW * LAST, XW * LAST + 4), at("lst", L_REP, L_REP + 4)
        ac(block("thr", 0), ind(xt, rep), bias=cc(C_NK))
        ac(block("xrh", 0), ind(xt, rep), scale=0.5)
        ac(at("cs", 0, 4), xt)
        for d in range(4):
            lo, hi, tl = 64 * d, 64 * d + 64, at("ctl", 4 * d, 4 * d + 4) if d else at("l_j", 12, 16)
            ts(block("g1", d), ind(at("q"), tl), -float(H), None, OP.add)
            if d:
                tt(block("xr", d), ind(at("k"), tl), block("xrh", d - 1), OP.add)
                ac(block("thr", d), block("xr", d), bias=cc(C_NK))
                if d < 3:
                    ac(block("xrh", d), block("xr", d), scale=0.5)
            ts(at("c16", 4 * d, 4 * d + 4), at("g1", lo, hi, 16), float(H), None, OP.add)
            for s in range(lo, hi, 16):
                ac(at("dg", s, s + 16), at("diag", 0, 16), scale=at("g1", s, s + 1))
            tt(block("gec", d), ind(at("k"), at("c16", 4 * d, 4 * d + 4)), block("thr", d), OP.is_ge)
            group([(at("p3", 0, 128), ident, at("tie")), (at("p3", 0, 64), ident, at("cb", B_H, B_H + 64)), (at("p3", 0, 64), ones, block("dg", d)),
                   (at("p3", 0, 64), mat("onew"), block("gec", d)), (at("p3", 64, 128), mat("onew"), block("gec", d))])
            scan(at("zs", 2 * lo, 2 * hi), at("rst"), at("p3", 0, 128))
            for s in range(4 if d < 3 else 0):
                z = 2 * lo + 16 * s + 15
                ac(at("ctl", 4 * d + 4 + s, 4 * d + 5 + s), at("zs", z + 64, z + 65), bias=at("zs", z, z + 1), scale=-1.0)
            tt(at("cs", 16 + 4 * d, 20 + 4 * d), at("zs", 2 * lo + 15, 2 * lo + 64, 16), at("zs", 2 * lo + 79, 2 * hi, 16), OP.subtract)
            if d < 3:
                ac(at("cs", 32 + 4 * d, 36 + 4 * d), at("cs", 16 + 4 * d, 20 + 4 * d), bias=-float(H))
        ac(at("cs", 4, 16), at("xr", 64, 256, 16))
        o = 48 * LAST
        tt(at("m"), ind(at("cs", 32, 40), at("lst", L_CMP, L_CMP + 3)), at("l_ct", o, o + 48), OP.is_equal)
        tt(at("pp", 0, 8), at("m", 4, 12), at("m", 20, 28), OP.mult)
        tt(at("pp", 8, 16), at("m", 28, 36), at("m", 36, 44), OP.mult)
        ts(at("vm", 28, 36), at("pp", 8, 16), -float(R), float(R), OP.mult, OP.add)
        tt(at("vm", 36, 44), at("vm", 28, 36), at("l_ct", o + 12, o + 20), OP.add)
        for h in range(2):
            tt(at("pp", 16 + h, 24, 2), at("vm", 36 + h, 44, 2), at("cs", 40, 44), OP.is_equal)
        mm(at("p4", 0, 4), ones, at("m", 0, 4), True, True)
        for j, lo in enumerate((0, 16)):
            group([(at("p4", 4 * j + 4, 4 * j + 8), ones, at("pp", lo + h, lo + 8, 2)) for h in range(2)])
        tt(at("vm", 12, 24), at("p4", 0, 12), at("cst", K_DMK, K_DMK + 12), OP.mult)
        ac(at("vm", 0, 12), at("vm", 12, 24), AF.Sign, acc=at("vm", 24, 25))
        ts(at("ix", 12, 13), at("vm", 24, 25), 4.0, cc(C_IX), OP.mult, OP.add)
        cp(at("fin"), ind(at("cs", 0, 32), at("ix", 12, 13)))
        send(drafter(LAST), at("l_f"), at("fin", 0, 8), "a_f")

    def results():
        dma("s", T.yt[:, 0:12], T.ytb[0:128:16, :], "d_yu", ["yu"], [at("ytb")])
        for j, (lo, hi) in enumerate(((0, CUT), (CUT, 256))):
            send(drafter(LAST), at("l_y", lo, hi), at("x", XW * LAST + 8 + lo, XW * LAST + 8 + hi), "a_y%d" % j)
            dma("y", T.yn[:, lo:hi], T.l_y[:, lo:hi], "d_y%d" % j, ["y%d" % j], [at("l_y", lo, hi)], 128 * 4 * (hi - lo))
        dma("s", T.yx[:], T.l_f[:, 0:4], "d_yx", ["yx"], [at("l_f")])
        dma("s", T.yt[:, 12:16], T.l_f[0:128:16, 4:8], "d_yt", ["yt"], [at("l_f")])
        add("g", None, [], ["yx", "yt", "yu", "y0", "y1"], 50)

    def part(t, name, fn, *args):
        first = len(ops)
        fn(*args)
        for j in range(first, len(ops)):
            ops[j]["tag"] = (t, name, j - first)

    for op in ops:
        op["tag"] = (None, None, None)
    for t in range(NSTEP):
        part(t, "root" if t else "start", root, t)
        part(t, "draft", draft, t)
        if t < LAST:
            part(t, "twins", twins)
            part(t, "verify", verify, t)
            part(t, "overwrite", overwrite, t)
    part(LAST, "chain", chain)
    part(LAST, "states", states, LAST)
    part(LAST, "results", results)
    emit(g, T, arrange(ops, sends))
    g.wait_ge(T.sem.sent, sent[0])
